import numpy as np
import ml_dtypes


def mxq(x, axis, fmt="e4m3"):
    dtype, down = {"e4m3": (ml_dtypes.float8_e4m3fn, 7), "e5m2": (ml_dtypes.float8_e5m2, 14)}[fmt]
    v = np.moveaxis(np.asarray(x, np.float32).astype(ml_dtypes.bfloat16).astype(np.float64), axis, -1)
    blocks = v.reshape(v.shape[:-1] + (-1, 32))
    amax = np.abs(blocks).max(-1, keepdims=True)
    byte = np.maximum(np.where(amax > 0, np.frexp(amax)[1] - 1 + 127, 0) - down, 1)
    scale = np.exp2(byte - 127.0)
    codes = (blocks / scale).astype(np.float32).astype(dtype).astype(np.float64)
    return np.moveaxis((codes * scale).reshape(v.shape), -1, axis)


WIDE = False


def mx_kscale(k):
    if not WIDE:
        return np.ones(k)
    levels = np.array([10, -10, 5, -5, 0])
    if k % 512:
        return np.exp2(np.random.permutation(np.resize(levels, k // 32))).repeat(32)
    a = np.empty((k // 512, 16))
    for p in range(k // 512):
        a[p, :8] = np.random.permutation(np.resize(levels, 8))
        for g in range(8):
            far = levels[np.abs(levels - a[p, g]) >= 10]
            a[p, g + 8] = far[np.random.randint(len(far))]
    return np.exp2(a.ravel()).repeat(32)


def f64(x):
    return np.asarray(x).astype(np.float64)


def striped(idx):
    return np.tile(idx.reshape(-1, 16).T, (8, 1)).astype(np.uint16)


def unstriped(offs):
    return offs[:16].T.reshape(-1).astype(np.int64)


def pack_weight(w):
    k, n = w.shape
    w = f64(np.asarray(w, np.float32).astype(ml_dtypes.bfloat16)).reshape(k // 32, 32, n)
    amax = np.abs(w).max(1)
    byte = np.clip(np.where(amax > 0, np.frexp(amax)[1] - 1 + 127 - 7, 1), 1, 254)
    scaled = (w * np.exp2(127.0 - byte)[:, None, :]).reshape(k, n).astype(np.float32)
    words = np.ascontiguousarray(scaled.reshape(k // 512, 128, 4, n).transpose(0, 1, 3, 2)).astype(ml_dtypes.float8_e4m3fn).view(np.uint8)
    return words, np.ascontiguousarray(byte.astype(np.uint8).reshape(k // 512, 16, n))


def unpack_weight(words, scales):
    g, p, n, _ = words.shape
    vals = np.ascontiguousarray(words).view(ml_dtypes.float8_e4m3fn).astype(np.float64) * np.repeat(np.exp2(scales.astype(np.float64) - 127.0), 8, axis=1)[..., None]
    return vals.transpose(0, 1, 3, 2).reshape(g * 512, n)


def gelu(v):
    return 0.5 * v * (1.0 + np.tanh(np.sqrt(2.0 / np.pi) * (v + 0.044715 * v**3)))


K, T, E, C, N = 1024, 640, 5, 256, 128


def by_expert(wq, xq):
    return np.concatenate([wq[e].T @ xq[:, e * C:(e + 1) * C] for e in range(E)], axis=1)


def setup_inputs():
    n = np.random.standard_normal
    s = mx_kscale(K)[:, None]
    first = np.random.permutation(np.repeat(np.arange(E), T // E))
    second = (first + 1 + np.random.permutation(np.repeat(np.arange(E - 1), -(-T // (E - 1)))[:T])) % E
    while np.bincount(second, minlength=E).max() != T // E:
        load = np.bincount(second, minlength=E); hi, lo = int(load.argmax()), int(load.argmin())
        t = np.flatnonzero((second == hi) & (first != lo))[0]; second[t] = lo
    slot_token = np.empty(E * C, np.int64); pos = np.empty((2, T), np.int64); fill = np.zeros(E, np.int64)
    place = np.stack([np.random.permutation(C) for _ in range(E)])
    for r, deal in enumerate((first, second)):
        for t in np.random.permutation(T):
            e = deal[t]; j = e * C + place[e, fill[e]]; fill[e] += 1; slot_token[j] = t; pos[r, t] = j
    g = np.random.uniform(0.2, 0.8, T)
    packed = [pack_weight(m) for m in n((E, K, N)) / np.sqrt(K) / s[None]]
    w_slot = np.empty(E * C); w_slot[pos[0]] = g; w_slot[pos[1]] = 1.0 - g
    return {
        "xT": (n((K, T)) * s).astype(np.float32),
        "w_words": np.stack([m[0] for m in packed]),
        "w_scales": np.stack([m[1] for m in packed]),
        "b": (0.3 * n((N, E))).astype(np.float32),
        "gate": np.tile(w_slot, (K, 1)).astype(np.float32),
        "offs": striped(slot_token),
        "pos1": striped(pos[0]),
        "pos2": striped(pos[1]),
    }


def reference(xT, w_words, w_scales, b, gate, offs, pos1, pos2):
    idx = unstriped(offs)
    w = np.stack([unpack_weight(w_words[e], w_scales[e]) for e in range(E)])
    xq = mxq(f64(gate) * f64(xT)[:, idx], 0, "e4m3")
    y = by_expert(w, xq)
    y = gelu(y + np.repeat(f64(b), C, axis=1))
    return y[:, unstriped(pos1)] + y[:, unstriped(pos2)]

@@ -1,0 +1,131 @@
+from contextlib import ExitStack
+
+import concourse.mybir as mybir
+
+K, T, E, C, N = 1024, 640, 5, 256, 128
+S = E * C
+P = 128
+PACK = 4
+K_PASS = P * PACK
+PASSES = K // K_PASS
+
+F32 = mybir.dt.float32
+BF16 = mybir.dt.bfloat16
+I32 = mybir.dt.int32
+U32 = mybir.dt.uint32
+U16 = mybir.dt.uint16
+U8 = mybir.dt.uint8
+FP8X4 = mybir.dt.float8_e4m3fn_x4
+MULT = mybir.AluOpType.mult
+ADD = mybir.AluOpType.add
+GELU = mybir.ActivationFunctionType.Gelu_apprx_tanh
+
+FLOPS = 2 * K * N * S
+BYTES = 4 * K * T + E * K * N + E * K * N // 32 + 4 * N * E + 4 * S + 2 * P * (S + 2 * T) // 16 + 4 * N * T
+
+UNITS = [(0, 0, 512), (0, 512, 512), (0, 1024, 256),
+         (1, 0, 512), (1, 512, 256), (1, 768, 256), (1, 1024, 128), (1, 1152, 128)]
+GROUPS = [(0, 256), (256, 256), (512, 256), (768, 256), (1024, 128), (1152, 128)]
+GATE_PIECES = [(0, 256), (256, 256), (512, 768)]
+OUT_PIECES = [(0, 320), (320, 320)]
+
+
+def tile_moe_pre_lin_gelu_kernel(tc, xT, w_words, w_scales, b, gate, offs, pos1, pos2, out):
+    nc = tc.nc
+    with ExitStack() as ctx:
+        keep = ctx.enter_context(tc.tile_pool(name="keep", bufs=1))
+        psum = ctx.enter_context(tc.psum_pool(name="psum", bufs=1))
+
+        offs_sb = keep.tile([P, S // 16], U16, name="offs_sb")
+        pos1_sb = keep.tile([P, T // 16], U16, name="pos1_sb")
+        pos2_sb = keep.tile([P, T // 16], U16, name="pos2_sb")
+        gate_sb = keep.tile([P, S], F32, name="gate_sb")
+        bias_sb = keep.tile([P, E], F32, name="bias_sb")
+        w_codes = keep.tile([P, E * PASSES * N * PACK], U8, name="w_codes", align_bytes=64)
+        w_plane = keep.tile([P, E * PASSES * N], U8, name="w_plane", align_bytes=64)
+        x_rows = [keep.tile([P, T], F32, name="x_rows%d" % i) for i in range(PASSES * PACK)]
+        y = keep.tile([P, S], F32, name="y")
+
+        x_view = xT.rearrange("(a p r) t -> a r p t", p=P, r=PACK)
+
+        def load_x(i):
+            nc.sync.dma_start(x_rows[i][:], x_view[i // PACK, i % PACK])
+
+        def load_gate(i):
+            s0, n = GATE_PIECES[i]
+            nc.sync.dma_start(gate_sb[:, s0:s0 + n], gate[0:P, s0:s0 + n])
+
+        nc.vector.memset(w_plane[:].bitcast(I32), 0)
+        load_x(0)
+        nc.sync.dma_start(offs_sb[:], offs)
+        load_gate(0)
+        load_gate(1)
+        for i in range(1, 4):
+            load_x(i)
+        load_gate(2)
+        for i in range(4, 8):
+            load_x(i)
+        nc.sync.dma_start(
+            w_codes[:].bitcast(I32).rearrange("p (g n) -> p g n", n=N),
+            w_words.rearrange("e a p n r -> p (e a) (n r)").bitcast(I32))
+        scale_rows = w_scales.rearrange("e a q n -> q (e a) n").bitcast(I32)
+        for q in range(4):
+            nc.sync.dma_start(
+                w_plane[32 * q:32 * q + 4, :].bitcast(I32).rearrange("p (g n) -> p g n", g=E * PASSES),
+                scale_rows[4 * q:4 * q + 4])
+        nc.sync.dma_start(bias_sb[:], b)
+        nc.sync.dma_start(pos1_sb[:], pos1)
+        nc.sync.dma_start(pos2_sb[:], pos2)
+
+        acc = [psum.tile([P, n], F32, name="acc%d" % i) for i, (s0, n) in enumerate(GROUPS)]
+        grouped = {}
+
+        def gather(u):
+            a, s0, n = UNITS[u]
+            picked = keep.tile([P, PACK, n], F32, name="picked%d" % u)
+            for r in range(PACK):
+                cuts = [(0, 256), (256, 256)] if (u == 0 and r == 0) else [(0, n)]
+                for c0, m in cuts:
+                    lo = s0 + c0
+                    nc.vector.tensor_tensor(
+                        picked[:, r, c0:c0 + m],
+                        x_rows[a * PACK + r][:].indirect(offs_sb[:, lo // 16:(lo + m) // 16]),
+                        gate_sb[:, lo:lo + m], MULT)
+            grouped[u] = keep.tile([P, n, PACK], BF16, name="grouped%d" % u, align_bytes=64)
+            nc.scalar.copy(grouped[u][:], picked[:].rearrange("p r n -> p n r"))
+
+        def multiply(u):
+            a, s0, n = UNITS[u]
+            codes = keep.tile([P, n], U32, name="codes%d" % u, align_bytes=64)
+            plane = keep.tile([P, n], U8, name="plane%d" % u, align_bytes=64)
+            nc.vector.quantize_mx(out=codes[:].bitcast(FP8X4), scales=plane[:],
+                                  in_=grouped[u][:].rearrange("p n r -> p (n r)"))
+            for i, (g0, m) in enumerate(GROUPS):
+                if s0 <= g0 < s0 + n:
+                    e = g0 // C
+                    j = e * PASSES + a
+                    cols = slice(g0 - s0, g0 - s0 + m)
+                    nc.tensor.matmul_mx(
+                        out=acc[i][:],
+                        lhsT=w_codes[:, j * N * PACK:(j + 1) * N * PACK].bitcast(FP8X4),
+                        lhsT_scale=w_plane[:, j * N:(j + 1) * N],
+                        rhs=codes[:, cols].bitcast(FP8X4), rhs_scale=plane[:, cols],
+                        start=(a == 0), stop=(a == PASSES - 1))
+                    if a == PASSES - 1:
+                        nc.scalar.activation(y[:, g0:g0 + m], acc[i][:], GELU, bias=bias_sb[:, e:e + 1])
+
+        for u in range(len(UNITS)):
+            gather(u)
+            if u > 0:
+                multiply(u - 1)
+        multiply(len(UNITS) - 1)
+
+        for i, (t0, n) in enumerate(OUT_PIECES):
+            first = keep.tile([P, n], F32, name="first%d" % i)
+            second = keep.tile([P, n], F32, name="second%d" % i)
+            total = keep.tile([P, n], F32, name="total%d" % i)
+            cols = slice(t0 // 16, (t0 + n) // 16)
+            nc.vector.tensor_copy(first[:], y[:].indirect(pos1_sb[:, cols]))
+            nc.vector.tensor_copy(second[:], y[:].indirect(pos2_sb[:, cols]))
+            nc.vector.tensor_tensor(total[:], first[:], second[:], ADD)
+            nc.sync.dma_start(out[:, t0:t0 + n], total[:])

@@ -23,17 +23,25 @@ GELU = mybir.ActivationFunctionType.Gelu_apprx_tanh
 FLOPS = 2 * K * N * S
 BYTES = 4 * K * T + E * K * N + E * K * N // 32 + 4 * N * E + 4 * S + 2 * P * (S + 2 * T) // 16 + 4 * N * T
 
-UNITS = [(0, 0, 512), (0, 512, 512), (0, 1024, 256),
-         (1, 0, 512), (1, 512, 256), (1, 768, 256), (1, 1024, 128), (1, 1152, 128)]
+UNITS = [(0, 0, 384), (1, 0, 384), (0, 384, 896), (1, 384, 512), (1, 896, 256), (1, 1152, 128)]
 GROUPS = [(0, 256), (256, 256), (512, 256), (768, 256), (1024, 128), (1152, 128)]
-GATE_PIECES = [(0, 256), (256, 256), (512, 768)]
-OUT_PIECES = [(0, 320), (320, 320)]
+GATE_PIECES = [(0, 128), (128, 256), (384, 896)]
+FIRST_CUTS = [(0, 128), (128, 256)]
+OUT_PIECES = [(0, 480), (480, 160)]
+ORDER = [("G", 0), ("G", 1), ("Q", 0), ("M", 0), ("G", 2), ("G", 3), ("Q", 1), ("G", 4), ("Q", 2), ("M", 1), ("M", 2), ("G", 5), ("Q", 3), ("M", 3), ("Q", 4), ("M", 4), ("Q", 5), ("M", 5)]
+LOADS = [("x", 0), ("o", 0), ("g", 0), ("g", 1), ("x", 1), ("x", 2), ("x", 3), ("x", 4), ("x", 5), ("x", 6), ("x", 7), ("g", 2), ("w", 0), ("s", 0), ("r", 0)]
+WIDTHS = [912] * 4 + [640] * 4
+SLABS = [[(0, 0, 256), (1, 0, 256)], [(0, 256, 128), (0, 384, 896)], [(1, 256, 128), (1, 384, 384)], [(1, 768, 128), (1, 896, 128)], [(1, 1024, 128)], [(1, 1152, 128)]]
+RUN = 2
+PAIRED = []
+POOL_ADDS = []
 
 
 def tile_moe_pre_lin_gelu_kernel(tc, xT, w_words, w_scales, b, gate, offs, pos1, pos2, out):
     nc = tc.nc
     with ExitStack() as ctx:
         keep = ctx.enter_context(tc.tile_pool(name="keep", bufs=1))
+        ring = ctx.enter_context(tc.tile_pool(name="ring", bufs=2))
         psum = ctx.enter_context(tc.psum_pool(name="psum", bufs=1))
 
         offs_sb = keep.tile([P, S // 16], U16, name="offs_sb")
@@ -43,89 +51,113 @@ def tile_moe_pre_lin_gelu_kernel(tc, xT, w_words, w_scales, b, gate, offs, pos1,
         bias_sb = keep.tile([P, E], F32, name="bias_sb")
         w_codes = keep.tile([P, E * PASSES * N * PACK], U8, name="w_codes", align_bytes=64)
         w_plane = keep.tile([P, E * PASSES * N], U8, name="w_plane", align_bytes=64)
-        x_rows = [keep.tile([P, T], F32, name="x_rows%d" % i) for i in range(PASSES * PACK)]
+        x_rows = [keep.tile([P, WIDTHS[i]], F32, name="x_rows%d" % i) for i in range(PASSES * PACK)]
         y = keep.tile([P, S], F32, name="y")
+        words = [sum(n for a, s0, n in slab) for slab in SLABS]
+        grouped = [keep.tile([P, n, PACK], BF16, name="grouped%d" % i, align_bytes=64) for i, n in enumerate(words)]
+        codes = [keep.tile([P, n], U32, name="codes%d" % i, align_bytes=64) for i, n in enumerate(words)]
+        plane = [keep.tile([P, n], U8, name="plane%d" % i, align_bytes=64) for i, n in enumerate(words)]
 
         x_view = xT.rearrange("(a p r) t -> a r p t", p=P, r=PACK)
 
-        def load_x(i):
-            nc.sync.dma_start(x_rows[i][:], x_view[i // PACK, i % PACK])
-
-        def load_gate(i):
-            s0, n = GATE_PIECES[i]
-            nc.sync.dma_start(gate_sb[:, s0:s0 + n], gate[0:P, s0:s0 + n])
-
         nc.vector.memset(w_plane[:].bitcast(I32), 0)
-        load_x(0)
-        nc.sync.dma_start(offs_sb[:], offs)
-        load_gate(0)
-        load_gate(1)
-        for i in range(1, 4):
-            load_x(i)
-        load_gate(2)
-        for i in range(4, 8):
-            load_x(i)
-        nc.sync.dma_start(
-            w_codes[:].bitcast(I32).rearrange("p (g n) -> p g n", n=N),
-            w_words.rearrange("e a p n r -> p (e a) (n r)").bitcast(I32))
-        scale_rows = w_scales.rearrange("e a q n -> q (e a) n").bitcast(I32)
-        for q in range(4):
-            nc.sync.dma_start(
-                w_plane[32 * q:32 * q + 4, :].bitcast(I32).rearrange("p (g n) -> p g n", g=E * PASSES),
-                scale_rows[4 * q:4 * q + 4])
-        nc.sync.dma_start(bias_sb[:], b)
-        nc.sync.dma_start(pos1_sb[:], pos1)
-        nc.sync.dma_start(pos2_sb[:], pos2)
+
+        for kind, i in LOADS:
+            if kind == "x":
+                nc.sync.dma_start(x_rows[i][:, 0:T], x_view[i // PACK, i % PACK])
+            elif kind == "g":
+                s0, n = GATE_PIECES[i]
+                nc.sync.dma_start(gate_sb[:, s0:s0 + n], gate[0:P, s0:s0 + n])
+            elif kind == "o":
+                nc.sync.dma_start(offs_sb[:], offs)
+            elif kind == "w":
+                nc.sync.dma_start(
+                    w_codes[:].bitcast(I32).rearrange("p (g n) -> p g n", n=N),
+                    w_words.rearrange("e a p n r -> p (e a) (n r)").bitcast(I32))
+            elif kind == "s":
+                scale_rows = w_scales.rearrange("e a q n -> q (e a) n").bitcast(I32)
+                for q in range(4):
+                    nc.sync.dma_start(
+                        w_plane[32 * q:32 * q + 4, :].bitcast(I32).rearrange("p (g n) -> p g n", g=E * PASSES),
+                        scale_rows[4 * q:4 * q + 4])
+            else:
+                nc.sync.dma_start(bias_sb[:], b)
+                nc.sync.dma_start(pos1_sb[:], pos1)
+                nc.sync.dma_start(pos2_sb[:], pos2)
 
         acc = [psum.tile([P, n], F32, name="acc%d" % i) for i, (s0, n) in enumerate(GROUPS)]
-        grouped = {}
+
+        def place(a, s):
+            for i, slab in enumerate(SLABS):
+                w0 = 0
+                for pa, p0, pn in slab:
+                    if pa == a and p0 <= s < p0 + pn:
+                        return i, w0 + s - p0
+                    w0 += pn
+            raise ValueError
 
         def gather(u):
             a, s0, n = UNITS[u]
-            picked = keep.tile([P, PACK, n], F32, name="picked%d" % u)
+            picked = ring.tile([P, PACK, n], F32, name="picked")
             for r in range(PACK):
-                cuts = [(0, 256), (256, 256)] if (u == 0 and r == 0) else [(0, n)]
+                cuts = FIRST_CUTS if (u == 0 and r == 0) else [(0, n)]
                 for c0, m in cuts:
                     lo = s0 + c0
                     nc.vector.tensor_tensor(
                         picked[:, r, c0:c0 + m],
                         x_rows[a * PACK + r][:].indirect(offs_sb[:, lo // 16:(lo + m) // 16]),
                         gate_sb[:, lo:lo + m], MULT)
-            grouped[u] = keep.tile([P, n, PACK], BF16, name="grouped%d" % u, align_bytes=64)
-            nc.scalar.copy(grouped[u][:], picked[:].rearrange("p r n -> p n r"))
+            for slab in SLABS:
+                for pa, p0, pn in slab:
+                    if pa == a and s0 <= p0 < s0 + n:
+                        i, w0 = place(a, p0)
+                        nc.scalar.copy(
+                            grouped[i][:, w0:w0 + pn, :].rearrange("p (c i) r -> p c r i", i=RUN),
+                            picked[:, :, p0 - s0:p0 - s0 + pn].rearrange("p r (c i) -> p c r i", i=RUN))
 
-        def multiply(u):
-            a, s0, n = UNITS[u]
-            codes = keep.tile([P, n], U32, name="codes%d" % u, align_bytes=64)
-            plane = keep.tile([P, n], U8, name="plane%d" % u, align_bytes=64)
-            nc.vector.quantize_mx(out=codes[:].bitcast(FP8X4), scales=plane[:],
-                                  in_=grouped[u][:].rearrange("p n r -> p (n r)"))
-            for i, (g0, m) in enumerate(GROUPS):
-                if s0 <= g0 < s0 + n:
-                    e = g0 // C
-                    j = e * PASSES + a
-                    cols = slice(g0 - s0, g0 - s0 + m)
-                    nc.tensor.matmul_mx(
-                        out=acc[i][:],
-                        lhsT=w_codes[:, j * N * PACK:(j + 1) * N * PACK].bitcast(FP8X4),
-                        lhsT_scale=w_plane[:, j * N:(j + 1) * N],
-                        rhs=codes[:, cols].bitcast(FP8X4), rhs_scale=plane[:, cols],
-                        start=(a == 0), stop=(a == PASSES - 1))
-                    if a == PASSES - 1:
-                        nc.scalar.activation(y[:, g0:g0 + m], acc[i][:], GELU, bias=bias_sb[:, e:e + 1])
+        def quantize(i):
+            nc.vector.quantize_mx(out=codes[i][:].bitcast(FP8X4), scales=plane[i][:],
+                                  in_=grouped[i][:].rearrange("p n r -> p (n r)"))
 
-        for u in range(len(UNITS)):
-            gather(u)
-            if u > 0:
-                multiply(u - 1)
-        multiply(len(UNITS) - 1)
+        def multiply(i):
+            g0, m = GROUPS[i]
+            e = g0 // C
+            for a in range(PASSES):
+                h, w0 = place(a, g0)
+                j = e * PASSES + a
+                nc.tensor.matmul_mx(
+                    out=acc[i][:],
+                    lhsT=w_codes[:, j * N * PACK:(j + 1) * N * PACK].bitcast(FP8X4),
+                    lhsT_scale=w_plane[:, j * N:(j + 1) * N],
+                    rhs=codes[h][:, w0:w0 + m].bitcast(FP8X4), rhs_scale=plane[h][:, w0:w0 + m],
+                    start=(a == 0), stop=(a == PASSES - 1))
+            nc.scalar.activation(y[:, g0:g0 + m], acc[i][:], GELU, bias=bias_sb[:, e:e + 1])
 
+        for step in ORDER:
+            if step[0] == "G":
+                gather(step[1])
+            elif step[0] == "Q":
+                quantize(step[1])
+            else:
+                multiply(step[1])
+
+        pending = []
         for i, (t0, n) in enumerate(OUT_PIECES):
             first = keep.tile([P, n], F32, name="first%d" % i)
             second = keep.tile([P, n], F32, name="second%d" % i)
             total = keep.tile([P, n], F32, name="total%d" % i)
             cols = slice(t0 // 16, (t0 + n) // 16)
             nc.vector.tensor_copy(first[:], y[:].indirect(pos1_sb[:, cols]))
+            for a1, a2, a3, a4 in pending:
+                nc.vector.tensor_tensor(a3[:], a1[:], a2[:], ADD)
+                nc.sync.dma_start(a4, a3[:])
+            pending = []
             nc.vector.tensor_copy(second[:], y[:].indirect(pos2_sb[:, cols]))
-            nc.vector.tensor_tensor(total[:], first[:], second[:], ADD)
-            nc.sync.dma_start(out[:, t0:t0 + n], total[:])
+            if i in POOL_ADDS:
+                nc.gpsimd.tensor_tensor(total[:], first[:], second[:], ADD)
+                nc.sync.dma_start(out[:, t0:t0 + n], total[:])
+            else:
+                pending = [(first, second, total, out[:, t0:t0 + n])]
+        for a1, a2, a3, a4 in pending:
+            nc.vector.tensor_tensor(a3[:], a1[:], a2[:], ADD)
+            nc.sync.dma_start(a4, a3[:])

@@ -23,18 +23,20 @@ GELU = mybir.ActivationFunctionType.Gelu_apprx_tanh
 FLOPS = 2 * K * N * S
 BYTES = 4 * K * T + E * K * N + E * K * N // 32 + 4 * N * E + 4 * S + 2 * P * (S + 2 * T) // 16 + 4 * N * T
 
-UNITS = [(0, 0, 384), (1, 0, 384), (0, 384, 896), (1, 384, 512), (1, 896, 256), (1, 1152, 128)]
+UNITS = [(0, 0, 512), (1, 0, 512), (0, 512, 768), (1, 512, 384), (1, 896, 256), (1, 1152, 128)]
 GROUPS = [(0, 256), (256, 256), (512, 256), (768, 256), (1024, 128), (1152, 128)]
-GATE_PIECES = [(0, 128), (128, 256), (384, 896)]
-FIRST_CUTS = [(0, 128), (128, 256)]
-OUT_PIECES = [(0, 480), (480, 160)]
-ORDER = [("G", 0), ("G", 1), ("Q", 0), ("M", 0), ("G", 2), ("G", 3), ("Q", 1), ("G", 4), ("Q", 2), ("M", 1), ("M", 2), ("G", 5), ("Q", 3), ("M", 3), ("Q", 4), ("M", 4), ("Q", 5), ("M", 5)]
-LOADS = [("x", 0), ("o", 0), ("g", 0), ("g", 1), ("x", 1), ("x", 2), ("x", 3), ("x", 4), ("x", 5), ("x", 6), ("x", 7), ("g", 2), ("w", 0), ("s", 0), ("r", 0)]
-WIDTHS = [912] * 4 + [640] * 4
-SLABS = [[(0, 0, 256), (1, 0, 256)], [(0, 256, 128), (0, 384, 896)], [(1, 256, 128), (1, 384, 384)], [(1, 768, 128), (1, 896, 128)], [(1, 1024, 128)], [(1, 1152, 128)]]
+GATE_PIECES = [(0, 128), (128, 384), (512, 768)]
+FIRST_CUTS = [(0, 128), (128, 384)]
+OUT_PIECES = [(0, 256), (256, 224), (480, 160)]
+ORDER = [("G", 0), ("G", 1), ("Q", 0), ("M", 0), ("M", 1), ("G", 2), ("G", 3), ("Q", 1), ("G", 4), ("Q", 2), ("M", 2), ("G", 5), ("Q", 3), ("V", 0), ("M", 3), ("Q", 4), ("M", 4), ("Q", 5), ("M", 5)]
+LOADS = [("x", 0), ("o", 0), ("g", 0), ("g", 1), ("x", 1), ("x", 2), ("x", 3), ("x", 4), ("w", 0), ("s", 0), ("b", 0), ("x", 5), ("x", 6), ("x", 7), ("g", 2), ("w", 1), ("r", 0)]
+WIDTHS = [784] * 4 + [640] * 4
+SLABS = [[(0, 0, 512), (1, 0, 512)], [(0, 512, 512)], [(0, 1024, 256), (1, 512, 256)], [(1, 768, 128), (1, 896, 128)], [(1, 1024, 128)], [(1, 1152, 128)]]
 RUN = 2
+VECTOR_SHARE = 64
+W_PIECES = [(0, 4), (4, 10)]
 PAIRED = []
-POOL_ADDS = []
+POOL_ADDS = [0, 1]
 
 
 def tile_moe_pre_lin_gelu_kernel(tc, xT, w_words, w_scales, b, gate, offs, pos1, pos2, out):
@@ -71,9 +73,12 @@ def tile_moe_pre_lin_gelu_kernel(tc, xT, w_words, w_scales, b, gate, offs, pos1,
             elif kind == "o":
                 nc.sync.dma_start(offs_sb[:], offs)
             elif kind == "w":
+                lo, hi = W_PIECES[i]
                 nc.sync.dma_start(
-                    w_codes[:].bitcast(I32).rearrange("p (g n) -> p g n", n=N),
-                    w_words.rearrange("e a p n r -> p (e a) (n r)").bitcast(I32))
+                    w_codes[:].bitcast(I32).rearrange("p (g n) -> p g n", n=N)[:, lo:hi, :],
+                    w_words.rearrange("e a p n r -> p (e a) (n r)").bitcast(I32)[:, lo:hi, :])
+            elif kind == "b":
+                nc.sync.dma_start(bias_sb[:], b)
             elif kind == "s":
                 scale_rows = w_scales.rearrange("e a q n -> q (e a) n").bitcast(I32)
                 for q in range(4):
@@ -81,7 +86,6 @@ def tile_moe_pre_lin_gelu_kernel(tc, xT, w_words, w_scales, b, gate, offs, pos1,
                         w_plane[32 * q:32 * q + 4, :].bitcast(I32).rearrange("p (g n) -> p g n", g=E * PASSES),
                         scale_rows[4 * q:4 * q + 4])
             else:
-                nc.sync.dma_start(bias_sb[:], b)
                 nc.sync.dma_start(pos1_sb[:], pos1)
                 nc.sync.dma_start(pos2_sb[:], pos2)
 
@@ -95,6 +99,12 @@ def tile_moe_pre_lin_gelu_kernel(tc, xT, w_words, w_scales, b, gate, offs, pos1,
                         return i, w0 + s - p0
                     w0 += pn
             raise ValueError
+
+        late = []
+
+        def interleave(picked, c0, i, w0, n):
+            return (grouped[i][:, w0:w0 + n, :].rearrange("p (c i) r -> p c r i", i=RUN),
+                    picked[:, :, c0:c0 + n].rearrange("p r (c i) -> p c r i", i=RUN))
 
         def gather(u):
             a, s0, n = UNITS[u]
@@ -111,9 +121,10 @@ def tile_moe_pre_lin_gelu_kernel(tc, xT, w_words, w_scales, b, gate, offs, pos1,
                 for pa, p0, pn in slab:
                     if pa == a and s0 <= p0 < s0 + n:
                         i, w0 = place(a, p0)
-                        nc.scalar.copy(
-                            grouped[i][:, w0:w0 + pn, :].rearrange("p (c i) r -> p c r i", i=RUN),
-                            picked[:, :, p0 - s0:p0 - s0 + pn].rearrange("p r (c i) -> p c r i", i=RUN))
+                        own = pn - VECTOR_SHARE if u == len(UNITS) - 1 else pn
+                        nc.scalar.copy(*interleave(picked, p0 - s0, i, w0, own))
+                        if own < pn:
+                            late.append(interleave(picked, p0 - s0 + own, i, w0 + own, pn - own))
 
         def quantize(i):
             nc.vector.quantize_mx(out=codes[i][:].bitcast(FP8X4), scales=plane[i][:],
@@ -138,6 +149,8 @@ def tile_moe_pre_lin_gelu_kernel(tc, xT, w_words, w_scales, b, gate, offs, pos1,
                 gather(step[1])
             elif step[0] == "Q":
                 quantize(step[1])
+            elif step[0] == "V":
+                nc.vector.tensor_copy(*late[0])
             else:
                 multiply(step[1])
 

@@ -1,3 +1,4 @@
+import math
 from contextlib import ExitStack
 
 import concourse.mybir as mybir
@@ -8,6 +9,7 @@ P = 128
 PACK = 4
 K_PASS = P * PACK
 PASSES = K // K_PASS
+PER_COLUMN = 16
 
 F32 = mybir.dt.float32
 BF16 = mybir.dt.bfloat16
@@ -23,154 +25,143 @@ GELU = mybir.ActivationFunctionType.Gelu_apprx_tanh
 FLOPS = 2 * K * N * S
 BYTES = 4 * K * T + E * K * N + E * K * N // 32 + 4 * N * E + 4 * S + 2 * P * (S + 2 * T) // 16 + 4 * N * T
 
-UNITS = [(0, 0, 512), (1, 0, 512), (0, 512, 768), (1, 512, 384), (1, 896, 256), (1, 1152, 128)]
+STRETCHES = [(0, 0, 1280), (1, 0, 768), (1, 768, 384), (1, 1152, 128)]
+BORDER = PACK * STRETCHES[1][2]
+STAGE_AT = [BORDER, 0, BORDER, BORDER - (PACK - 1) * STRETCHES[3][2]]
 GROUPS = [(0, 256), (256, 256), (512, 256), (768, 256), (1024, 128), (1152, 128)]
-GATE_PIECES = [(0, 128), (128, 384), (512, 768)]
-FIRST_CUTS = [(0, 128), (128, 384)]
-OUT_PIECES = [(0, 256), (256, 224), (480, 160)]
-ORDER = [("G", 0), ("G", 1), ("Q", 0), ("M", 0), ("M", 1), ("G", 2), ("G", 3), ("Q", 1), ("G", 4), ("Q", 2), ("M", 2), ("G", 5), ("Q", 3), ("V", 0), ("M", 3), ("Q", 4), ("M", 4), ("Q", 5), ("M", 5)]
-LOADS = [("x", 0), ("o", 0), ("g", 0), ("g", 1), ("x", 1), ("x", 2), ("x", 3), ("x", 4), ("w", 0), ("s", 0), ("b", 0), ("x", 5), ("x", 6), ("x", 7), ("g", 2), ("w", 1), ("r", 0)]
-WIDTHS = [784] * 4 + [640] * 4
-SLABS = [[(0, 0, 512), (1, 0, 512)], [(0, 512, 512)], [(0, 1024, 256), (1, 512, 256)], [(1, 768, 128), (1, 896, 128)], [(1, 1024, 128)], [(1, 1152, 128)]]
+GATE_PIECES = [(0, 128), (128, 448), (576, 704)]
+FIRST_CUT = [(0, 128), (128, 448), (576, 704)]
 RUN = 2
-VECTOR_SHARE = 64
-W_PIECES = [(0, 4), (4, 10)]
-PAIRED = []
-POOL_ADDS = [0, 1]
+FIRST_PIECES = [(0, 448), (448, 192)]
+OUT_PIECES = [(0, 448), (448, 192)]
+WINDOW = [1296, 784]
 
 
 def tile_moe_pre_lin_gelu_kernel(tc, xT, w_words, w_scales, b, gate, offs, pos1, pos2, out):
     nc = tc.nc
     with ExitStack() as ctx:
         keep = ctx.enter_context(tc.tile_pool(name="keep", bufs=1))
-        ring = ctx.enter_context(tc.tile_pool(name="ring", bufs=2))
         psum = ctx.enter_context(tc.psum_pool(name="psum", bufs=1))
 
-        offs_sb = keep.tile([P, S // 16], U16, name="offs_sb")
-        pos1_sb = keep.tile([P, T // 16], U16, name="pos1_sb")
-        pos2_sb = keep.tile([P, T // 16], U16, name="pos2_sb")
+        offs_sb = keep.tile([P, S // PER_COLUMN], U16, name="offs_sb")
+        pos1_sb = keep.tile([P, T // PER_COLUMN], U16, name="pos1_sb")
+        pos2_sb = keep.tile([P, T // PER_COLUMN], U16, name="pos2_sb")
         gate_sb = keep.tile([P, S], F32, name="gate_sb")
         bias_sb = keep.tile([P, E], F32, name="bias_sb")
         w_codes = keep.tile([P, E * PASSES * N * PACK], U8, name="w_codes", align_bytes=64)
         w_plane = keep.tile([P, E * PASSES * N], U8, name="w_plane", align_bytes=64)
-        x_rows = [keep.tile([P, WIDTHS[i]], F32, name="x_rows%d" % i) for i in range(PASSES * PACK)]
+        x_rows = [keep.tile([P, WINDOW[i // PACK]], F32, name="x_rows%d" % i) for i in range(PASSES * PACK)]
+        staged = keep.tile([P, PACK * (STRETCHES[0][2] + STRETCHES[1][2])], F32, name="staged")
         y = keep.tile([P, S], F32, name="y")
-        words = [sum(n for a, s0, n in slab) for slab in SLABS]
-        grouped = [keep.tile([P, n, PACK], BF16, name="grouped%d" % i, align_bytes=64) for i, n in enumerate(words)]
-        codes = [keep.tile([P, n], U32, name="codes%d" % i, align_bytes=64) for i, n in enumerate(words)]
-        plane = [keep.tile([P, n], U8, name="plane%d" % i, align_bytes=64) for i, n in enumerate(words)]
+        grouped = [keep.tile([P, n, PACK], BF16, name="grouped%d" % i, align_bytes=64) for i, (a, s0, n) in enumerate(STRETCHES)]
+        codes = [keep.tile([P, n], U32, name="codes%d" % i, align_bytes=64) for i, (a, s0, n) in enumerate(STRETCHES)]
+        plane = [keep.tile([P, n], U8, name="plane%d" % i, align_bytes=64) for i, (a, s0, n) in enumerate(STRETCHES)]
+        acc = [psum.tile([P, n], F32, name="acc%d" % i) for i, (s0, n) in enumerate(GROUPS)]
+
+        warm_in = keep.tile([P, 1], F32, name="warm_in")
+        warm_out = keep.tile([P, 1], F32, name="warm_out")
+        nc.vector.memset(warm_in[:], 0.0)
+        nc.scalar.activation(warm_out[:], warm_in[:], GELU)
+        nc.vector.memset(w_plane[:].bitcast(I32), 0)
 
         x_view = xT.rearrange("(a p r) t -> a r p t", p=P, r=PACK)
 
-        nc.vector.memset(w_plane[:].bitcast(I32), 0)
+        def load_x(i):
+            nc.sync.dma_start(x_rows[i][:, 0:T], x_view[i // PACK, i % PACK])
 
-        for kind, i in LOADS:
-            if kind == "x":
-                nc.sync.dma_start(x_rows[i][:, 0:T], x_view[i // PACK, i % PACK])
-            elif kind == "g":
-                s0, n = GATE_PIECES[i]
-                nc.sync.dma_start(gate_sb[:, s0:s0 + n], gate[0:P, s0:s0 + n])
-            elif kind == "o":
-                nc.sync.dma_start(offs_sb[:], offs)
-            elif kind == "w":
-                lo, hi = W_PIECES[i]
-                nc.sync.dma_start(
-                    w_codes[:].bitcast(I32).rearrange("p (g n) -> p g n", n=N)[:, lo:hi, :],
-                    w_words.rearrange("e a p n r -> p (e a) (n r)").bitcast(I32)[:, lo:hi, :])
-            elif kind == "b":
-                nc.sync.dma_start(bias_sb[:], b)
-            elif kind == "s":
-                scale_rows = w_scales.rearrange("e a q n -> q (e a) n").bitcast(I32)
-                for q in range(4):
-                    nc.sync.dma_start(
-                        w_plane[32 * q:32 * q + 4, :].bitcast(I32).rearrange("p (g n) -> p g n", g=E * PASSES),
-                        scale_rows[4 * q:4 * q + 4])
-            else:
-                nc.sync.dma_start(pos1_sb[:], pos1)
-                nc.sync.dma_start(pos2_sb[:], pos2)
+        def load_gate(i):
+            s0, n = GATE_PIECES[i]
+            nc.sync.dma_start(gate_sb[:, s0:s0 + n], gate[0:P, s0:s0 + n])
 
-        acc = [psum.tile([P, n], F32, name="acc%d" % i) for i, (s0, n) in enumerate(GROUPS)]
+        load_x(0)
+        nc.sync.dma_start(offs_sb[:], offs)
+        for i in range(len(GATE_PIECES)):
+            load_gate(i)
+        for i in range(1, PASSES * PACK):
+            load_x(i)
+        nc.sync.dma_start(
+            w_codes[:].bitcast(I32).rearrange("p (g n) -> p g n", n=N),
+            w_words.rearrange("e a p n r -> p (e a) (n r)").bitcast(I32))
+        scale_rows = w_scales.rearrange("e a q n -> q (e a) n").bitcast(I32)
+        for q in range(4):
+            nc.sync.dma_start(
+                w_plane[32 * q:32 * q + 4, :].bitcast(I32).rearrange("p (g n) -> p g n", g=E * PASSES),
+                scale_rows[4 * q:4 * q + 4])
+        nc.sync.dma_start(bias_sb[:], b)
+        nc.sync.dma_start(pos1_sb[:], pos1)
+        nc.sync.dma_start(pos2_sb[:], pos2)
 
-        def place(a, s):
-            for i, slab in enumerate(SLABS):
-                w0 = 0
-                for pa, p0, pn in slab:
-                    if pa == a and p0 <= s < p0 + pn:
-                        return i, w0 + s - p0
-                    w0 += pn
-            raise ValueError
+        def columns(s0, n):
+            return slice(s0 // PER_COLUMN, (s0 + n) // PER_COLUMN)
 
-        late = []
-
-        def interleave(picked, c0, i, w0, n):
-            return (grouped[i][:, w0:w0 + n, :].rearrange("p (c i) r -> p c r i", i=RUN),
+        def interleave(picked, u, c0, n):
+            return (grouped[u][:, c0:c0 + n, :].rearrange("p (c i) r -> p c r i", i=RUN),
                     picked[:, :, c0:c0 + n].rearrange("p r (c i) -> p c r i", i=RUN))
 
         def gather(u):
-            a, s0, n = UNITS[u]
-            picked = ring.tile([P, PACK, n], F32, name="picked")
+            a, s0, n = STRETCHES[u]
+            picked = staged[:, STAGE_AT[u]:STAGE_AT[u] + PACK * n].rearrange("p (r n) -> p r n", r=PACK)
             for r in range(PACK):
-                cuts = FIRST_CUTS if (u == 0 and r == 0) else [(0, n)]
+                cuts = FIRST_CUT if (u == 0 and r == 0) else [(0, n)]
                 for c0, m in cuts:
-                    lo = s0 + c0
                     nc.vector.tensor_tensor(
                         picked[:, r, c0:c0 + m],
-                        x_rows[a * PACK + r][:].indirect(offs_sb[:, lo // 16:(lo + m) // 16]),
-                        gate_sb[:, lo:lo + m], MULT)
-            for slab in SLABS:
-                for pa, p0, pn in slab:
-                    if pa == a and s0 <= p0 < s0 + n:
-                        i, w0 = place(a, p0)
-                        own = pn - VECTOR_SHARE if u == len(UNITS) - 1 else pn
-                        nc.scalar.copy(*interleave(picked, p0 - s0, i, w0, own))
-                        if own < pn:
-                            late.append(interleave(picked, p0 - s0 + own, i, w0 + own, pn - own))
+                        x_rows[a * PACK + r][:].indirect(offs_sb[:, columns(s0 + c0, m)]),
+                        gate_sb[:, s0 + c0:s0 + c0 + m], MULT)
+            return picked
 
-        def quantize(i):
-            nc.vector.quantize_mx(out=codes[i][:].bitcast(FP8X4), scales=plane[i][:],
-                                  in_=grouped[i][:].rearrange("p n r -> p (n r)"))
+        def pieces(u):
+            n = STRETCHES[u][2]
+            wide = 1 << int(math.log2(n))
+            return [(0, wide), (wide, n - wide)] if wide < n else [(0, n)]
+
+        def quantize(u, c0, m):
+            nc.vector.quantize_mx(out=codes[u][:, c0:c0 + m].bitcast(FP8X4), scales=plane[u][:, c0:c0 + m],
+                                  in_=grouped[u][:, c0:c0 + m, :].rearrange("p n r -> p (n r)"))
+
+        def holder(a, s):
+            return [u for u, (pa, s0, n) in enumerate(STRETCHES) if pa == a and s0 <= s < s0 + n][0]
 
         def multiply(i):
             g0, m = GROUPS[i]
             e = g0 // C
             for a in range(PASSES):
-                h, w0 = place(a, g0)
+                u = holder(a, g0)
+                w0 = g0 - STRETCHES[u][1]
                 j = e * PASSES + a
                 nc.tensor.matmul_mx(
                     out=acc[i][:],
                     lhsT=w_codes[:, j * N * PACK:(j + 1) * N * PACK].bitcast(FP8X4),
                     lhsT_scale=w_plane[:, j * N:(j + 1) * N],
-                    rhs=codes[h][:, w0:w0 + m].bitcast(FP8X4), rhs_scale=plane[h][:, w0:w0 + m],
+                    rhs=codes[u][:, w0:w0 + m].bitcast(FP8X4), rhs_scale=plane[u][:, w0:w0 + m],
                     start=(a == 0), stop=(a == PASSES - 1))
             nc.scalar.activation(y[:, g0:g0 + m], acc[i][:], GELU, bias=bias_sb[:, e:e + 1])
 
-        for step in ORDER:
-            if step[0] == "G":
-                gather(step[1])
-            elif step[0] == "Q":
-                quantize(step[1])
-            elif step[0] == "V":
-                nc.vector.tensor_copy(*late[0])
-            else:
-                multiply(step[1])
+        def finish(u, c0, m):
+            quantize(u, c0, m)
+            s0 = STRETCHES[u][1] + c0
+            for i, (g0, width) in enumerate(GROUPS):
+                if holder(PASSES - 1, g0) == u and s0 <= g0 < s0 + m:
+                    multiply(i)
 
-        pending = []
+        last = len(STRETCHES) - 1
+        for u in range(last):
+            picked = gather(u)
+            nc.scalar.copy(*interleave(picked, u, 0, STRETCHES[u][2]))
+            if u >= 1:
+                for piece in pieces(u - 1):
+                    finish(u - 1, *piece)
+        picked = gather(last)
+        wide, narrow = pieces(last - 1)
+        finish(last - 1, *wide)
+        nc.vector.tensor_copy(*interleave(picked, last, 0, STRETCHES[last][2]))
+        finish(last - 1, *narrow)
+        finish(last, 0, STRETCHES[last][2])
+
+        first = keep.tile([P, T], F32, name="first")
+        for t0, n in FIRST_PIECES:
+            nc.vector.tensor_copy(first[:, t0:t0 + n], y[:].indirect(pos1_sb[:, columns(t0, n)]))
         for i, (t0, n) in enumerate(OUT_PIECES):
-            first = keep.tile([P, n], F32, name="first%d" % i)
-            second = keep.tile([P, n], F32, name="second%d" % i)
             total = keep.tile([P, n], F32, name="total%d" % i)
-            cols = slice(t0 // 16, (t0 + n) // 16)
-            nc.vector.tensor_copy(first[:], y[:].indirect(pos1_sb[:, cols]))
-            for a1, a2, a3, a4 in pending:
-                nc.vector.tensor_tensor(a3[:], a1[:], a2[:], ADD)
-                nc.sync.dma_start(a4, a3[:])
-            pending = []
-            nc.vector.tensor_copy(second[:], y[:].indirect(pos2_sb[:, cols]))
-            if i in POOL_ADDS:
-                nc.gpsimd.tensor_tensor(total[:], first[:], second[:], ADD)
-                nc.sync.dma_start(out[:, t0:t0 + n], total[:])
-            else:
-                pending = [(first, second, total, out[:, t0:t0 + n])]
-        for a1, a2, a3, a4 in pending:
-            nc.vector.tensor_tensor(a3[:], a1[:], a2[:], ADD)
-            nc.sync.dma_start(a4, a3[:])
+            nc.vector.tensor_tensor(total[:], y[:].indirect(pos2_sb[:, columns(t0, n)]), first[:, t0:t0 + n], ADD)
+            nc.sync.dma_start(out[:, t0:t0 + n], total[:])

@@ -29,8 +29,8 @@ STRETCHES = [(0, 0, 1280), (1, 0, 768), (1, 768, 384), (1, 1152, 128)]
 BORDER = PACK * STRETCHES[1][2]
 STAGE_AT = [BORDER, 0, BORDER, BORDER - (PACK - 1) * STRETCHES[3][2]]
 GROUPS = [(0, 256), (256, 256), (512, 256), (768, 256), (1024, 128), (1152, 128)]
-GATE_PIECES = [(0, 128), (128, 448), (576, 704)]
-FIRST_CUT = [(0, 128), (128, 448), (576, 704)]
+GATE_PIECES = [(0, 160), (160, 384), (544, 736)]
+FIRST_CUT = [(0, 160), (160, 384), (544, 736)]
 RUN = 2
 FIRST_PIECES = [(0, 448), (448, 192)]
 OUT_PIECES = [(0, 448), (448, 192)]
@@ -147,7 +147,8 @@ def tile_moe_pre_lin_gelu_kernel(tc, xT, w_words, w_scales, b, gate, offs, pos1,
         last = len(STRETCHES) - 1
         for u in range(last):
             picked = gather(u)
-            nc.scalar.copy(*interleave(picked, u, 0, STRETCHES[u][2]))
+            for piece in pieces(u):
+                nc.scalar.copy(*interleave(picked, u, *piece))
             if u >= 1:
                 for piece in pieces(u - 1):
                     finish(u - 1, *piece)

@@ -1,4 +1,3 @@
-import math
 from contextlib import ExitStack
 
 import concourse.mybir as mybir
@@ -7,8 +6,7 @@ K, T, E, C, N = 1024, 640, 5, 256, 128
 S = E * C
 P = 128
 PACK = 4
-K_PASS = P * PACK
-PASSES = K // K_PASS
+PASSES = K // (P * PACK)
 PER_COLUMN = 16
 
 F32 = mybir.dt.float32
@@ -25,16 +23,12 @@ GELU = mybir.ActivationFunctionType.Gelu_apprx_tanh
 FLOPS = 2 * K * N * S
 BYTES = 4 * K * T + E * K * N + E * K * N // 32 + 4 * N * E + 4 * S + 2 * P * (S + 2 * T) // 16 + 4 * N * T
 
-STRETCHES = [(0, 0, 1280), (1, 0, 768), (1, 768, 384), (1, 1152, 128)]
-BORDER = PACK * STRETCHES[1][2]
-STAGE_AT = [BORDER, 0, BORDER, BORDER - (PACK - 1) * STRETCHES[3][2]]
-GROUPS = [(0, 256), (256, 256), (512, 256), (768, 256), (1024, 128), (1152, 128)]
+LONG, MIDDLE, SHORT = 768, 384, 128
 GATE_PIECES = [(0, 160), (160, 384), (544, 736)]
-FIRST_CUT = [(0, 160), (160, 384), (544, 736)]
 RUN = 2
 FIRST_PIECES = [(0, 448), (448, 192)]
 OUT_PIECES = [(0, 448), (448, 192)]
-WINDOW = [1296, 784]
+SPARE = 16
 
 
 def tile_moe_pre_lin_gelu_kernel(tc, xT, w_words, w_scales, b, gate, offs, pos1, pos2, out):
@@ -50,19 +44,16 @@ def tile_moe_pre_lin_gelu_kernel(tc, xT, w_words, w_scales, b, gate, offs, pos1,
         bias_sb = keep.tile([P, E], F32, name="bias_sb")
         w_codes = keep.tile([P, E * PASSES * N * PACK], U8, name="w_codes", align_bytes=64)
         w_plane = keep.tile([P, E * PASSES * N], U8, name="w_plane", align_bytes=64)
-        x_rows = [keep.tile([P, WINDOW[i // PACK]], F32, name="x_rows%d" % i) for i in range(PASSES * PACK)]
-        staged = keep.tile([P, PACK * (STRETCHES[0][2] + STRETCHES[1][2])], F32, name="staged")
+        x_rows = [keep.tile([P, (S, LONG)[i // PACK] + SPARE], F32, name="x_rows%d" % i) for i in range(PASSES * PACK)]
+        staged = keep.tile([P, PACK * (LONG + S)], F32, name="staged")
+        grouped = keep.tile([P, PASSES * S, PACK], BF16, name="grouped", align_bytes=64)
+        codes = keep.tile([P, PASSES * S], U32, name="codes", align_bytes=64)
+        plane = keep.tile([P, PASSES * S], U8, name="plane", align_bytes=64)
         y = keep.tile([P, S], F32, name="y")
-        grouped = [keep.tile([P, n, PACK], BF16, name="grouped%d" % i, align_bytes=64) for i, (a, s0, n) in enumerate(STRETCHES)]
-        codes = [keep.tile([P, n], U32, name="codes%d" % i, align_bytes=64) for i, (a, s0, n) in enumerate(STRETCHES)]
-        plane = [keep.tile([P, n], U8, name="plane%d" % i, align_bytes=64) for i, (a, s0, n) in enumerate(STRETCHES)]
-        acc = [psum.tile([P, n], F32, name="acc%d" % i) for i, (s0, n) in enumerate(GROUPS)]
 
-        warm_in = keep.tile([P, 1], F32, name="warm_in")
-        warm_out = keep.tile([P, 1], F32, name="warm_out")
-        nc.vector.memset(warm_in[:], 0.0)
-        nc.scalar.activation(warm_out[:], warm_in[:], GELU)
         nc.vector.memset(w_plane[:].bitcast(I32), 0)
+        warm = keep.tile([P, 1], F32, name="warm")
+        nc.scalar.activation(warm[:], w_plane[:, 0:4].bitcast(U32), GELU)
 
         x_view = xT.rearrange("(a p r) t -> a r p t", p=P, r=PACK)
 
@@ -94,75 +85,69 @@ def tile_moe_pre_lin_gelu_kernel(tc, xT, w_words, w_scales, b, gate, offs, pos1,
         def columns(s0, n):
             return slice(s0 // PER_COLUMN, (s0 + n) // PER_COLUMN)
 
-        def interleave(picked, u, c0, n):
-            return (grouped[u][:, c0:c0 + n, :].rearrange("p (c i) r -> p c r i", i=RUN),
-                    picked[:, :, c0:c0 + n].rearrange("p r (c i) -> p c r i", i=RUN))
-
-        def gather(u):
-            a, s0, n = STRETCHES[u]
-            picked = staged[:, STAGE_AT[u]:STAGE_AT[u] + PACK * n].rearrange("p (r n) -> p r n", r=PACK)
+        def gather(a, s0, n, at, first_cuts):
+            picked = staged[:, at:at + PACK * n].rearrange("p (r n) -> p r n", r=PACK)
             for r in range(PACK):
-                cuts = FIRST_CUT if (u == 0 and r == 0) else [(0, n)]
-                for c0, m in cuts:
+                for c0, m in (first_cuts if r == 0 else [(0, n)]):
                     nc.vector.tensor_tensor(
                         picked[:, r, c0:c0 + m],
                         x_rows[a * PACK + r][:].indirect(offs_sb[:, columns(s0 + c0, m)]),
                         gate_sb[:, s0 + c0:s0 + c0 + m], MULT)
             return picked
 
-        def pieces(u):
-            n = STRETCHES[u][2]
-            wide = 1 << int(math.log2(n))
-            return [(0, wide), (wide, n - wide)] if wide < n else [(0, n)]
+        def interleave(picked, w0, c0, n):
+            return (grouped[:, w0 + c0:w0 + c0 + n, :].rearrange("p (c i) r -> p c r i", i=RUN),
+                    picked[:, :, c0:c0 + n].rearrange("p r (c i) -> p c r i", i=RUN))
 
-        def quantize(u, c0, m):
-            nc.vector.quantize_mx(out=codes[u][:, c0:c0 + m].bitcast(FP8X4), scales=plane[u][:, c0:c0 + m],
-                                  in_=grouped[u][:, c0:c0 + m, :].rearrange("p n r -> p (n r)"))
+        def quantize(w0, n):
+            nc.vector.quantize_mx(out=codes[:, w0:w0 + n].bitcast(FP8X4), scales=plane[:, w0:w0 + n],
+                                  in_=grouped[:, w0:w0 + n, :].rearrange("p n r -> p (n r)"))
 
-        def holder(a, s):
-            return [u for u, (pa, s0, n) in enumerate(STRETCHES) if pa == a and s0 <= s < s0 + n][0]
-
-        def multiply(i):
-            g0, m = GROUPS[i]
-            e = g0 // C
+        def multiply(s0, n):
+            e = s0 // C
+            acc = psum.tile([P, n], F32, name="acc%d" % s0)
             for a in range(PASSES):
-                u = holder(a, g0)
-                w0 = g0 - STRETCHES[u][1]
                 j = e * PASSES + a
+                w0 = a * S + s0
                 nc.tensor.matmul_mx(
-                    out=acc[i][:],
+                    out=acc[:],
                     lhsT=w_codes[:, j * N * PACK:(j + 1) * N * PACK].bitcast(FP8X4),
                     lhsT_scale=w_plane[:, j * N:(j + 1) * N],
-                    rhs=codes[u][:, w0:w0 + m].bitcast(FP8X4), rhs_scale=plane[u][:, w0:w0 + m],
+                    rhs=codes[:, w0:w0 + n].bitcast(FP8X4), rhs_scale=plane[:, w0:w0 + n],
                     start=(a == 0), stop=(a == PASSES - 1))
-            nc.scalar.activation(y[:, g0:g0 + m], acc[i][:], GELU, bias=bias_sb[:, e:e + 1])
+            nc.scalar.activation(y[:, s0:s0 + n], acc[:], GELU, bias=bias_sb[:, e:e + 1])
 
-        def finish(u, c0, m):
-            quantize(u, c0, m)
-            s0 = STRETCHES[u][1] + c0
-            for i, (g0, width) in enumerate(GROUPS):
-                if holder(PASSES - 1, g0) == u and s0 <= g0 < s0 + m:
-                    multiply(i)
+        border = PACK * LONG
+        wide = S - C
 
-        last = len(STRETCHES) - 1
-        for u in range(last):
-            picked = gather(u)
-            for piece in pieces(u):
-                nc.scalar.copy(*interleave(picked, u, *piece))
-            if u >= 1:
-                for piece in pieces(u - 1):
-                    finish(u - 1, *piece)
-        picked = gather(last)
-        wide, narrow = pieces(last - 1)
-        finish(last - 1, *wide)
-        nc.vector.tensor_copy(*interleave(picked, last, 0, STRETCHES[last][2]))
-        finish(last - 1, *narrow)
-        finish(last, 0, STRETCHES[last][2])
+        picked = gather(0, 0, S, border, GATE_PIECES)
+        nc.scalar.copy(*interleave(picked, 0, 0, wide))
+        nc.scalar.copy(*interleave(picked, 0, wide, C))
+
+        picked = gather(1, 0, LONG, 0, [(0, LONG)])
+        nc.scalar.copy(*interleave(picked, S, 0, LONG))
+        quantize(0, wide)
+
+        picked = gather(1, LONG, MIDDLE, border, [(0, MIDDLE)])
+        nc.scalar.copy(*interleave(picked, S + LONG, 0, C))
+        nc.scalar.copy(*interleave(picked, S + LONG, C, MIDDLE - C))
+        quantize(wide, C + LONG)
+        for s0 in range(0, LONG, C):
+            multiply(s0, C)
+
+        picked = gather(1, LONG + MIDDLE, SHORT, border - (PACK - 1) * SHORT, [(0, SHORT)])
+        quantize(S + LONG, C)
+        multiply(LONG, C)
+        nc.vector.tensor_copy(*interleave(picked, S + LONG + MIDDLE, 0, SHORT))
+        quantize(S + LONG + C, MIDDLE - C)
+        multiply(LONG + C, MIDDLE - C)
+        quantize(S + LONG + MIDDLE, SHORT)
+        multiply(LONG + MIDDLE, SHORT)
 
         first = keep.tile([P, T], F32, name="first")
         for t0, n in FIRST_PIECES:
             nc.vector.tensor_copy(first[:, t0:t0 + n], y[:].indirect(pos1_sb[:, columns(t0, n)]))
-        for i, (t0, n) in enumerate(OUT_PIECES):
-            total = keep.tile([P, n], F32, name="total%d" % i)
+        for t0, n in OUT_PIECES:
+            total = keep.tile([P, n], F32, name="total%d" % t0)
             nc.vector.tensor_tensor(total[:], y[:].indirect(pos2_sb[:, columns(t0, n)]), first[:, t0:t0 + n], ADD)
             nc.sync.dma_start(out[:, t0:t0 + n], total[:])

@@ -23,9 +23,10 @@ GELU = mybir.ActivationFunctionType.Gelu_apprx_tanh
 FLOPS = 2 * K * N * S
 BYTES = 4 * K * T + E * K * N + E * K * N // 32 + 4 * N * E + 4 * S + 2 * P * (S + 2 * T) // 16 + 4 * N * T
 
-LONG, MIDDLE, SHORT = 768, 384, 128
+SECOND_PIECES = [(0, 512), (512, 768)]
+LAST_PIECES = [(0, 320), (320, 384), (704, 576)]
+PAIR = 2
 GATE_PIECES = [(0, 160), (160, 384), (544, 736)]
-RUN = 2
 FIRST_PIECES = [(0, 448), (448, 192)]
 OUT_PIECES = [(0, 448), (448, 192)]
 SPARE = 16
@@ -44,8 +45,8 @@ def tile_moe_pre_lin_gelu_kernel(tc, xT, w_words, w_scales, b, gate, offs, pos1,
         bias_sb = keep.tile([P, E], F32, name="bias_sb")
         w_codes = keep.tile([P, E * PASSES * N * PACK], U8, name="w_codes", align_bytes=64)
         w_plane = keep.tile([P, E * PASSES * N], U8, name="w_plane", align_bytes=64)
-        x_rows = [keep.tile([P, (S, LONG)[i // PACK] + SPARE], F32, name="x_rows%d" % i) for i in range(PASSES * PACK)]
-        staged = keep.tile([P, PACK * (LONG + S)], F32, name="staged")
+        x_rows = [keep.tile([P, S + SPARE], F32, name="x_rows%d" % i) for i in range(PASSES * PACK)]
+        staged = [keep.tile([P, PAIR, S], F32, name="staged%d" % i) for i in range(PASSES * PACK // PAIR)]
         grouped = keep.tile([P, PASSES * S, PACK], BF16, name="grouped", align_bytes=64)
         codes = keep.tile([P, PASSES * S], U32, name="codes", align_bytes=64)
         plane = keep.tile([P, PASSES * S], U8, name="plane", align_bytes=64)
@@ -85,64 +86,60 @@ def tile_moe_pre_lin_gelu_kernel(tc, xT, w_words, w_scales, b, gate, offs, pos1,
         def columns(s0, n):
             return slice(s0 // PER_COLUMN, (s0 + n) // PER_COLUMN)
 
-        def gather(a, s0, n, at, first_cuts):
-            picked = staged[:, at:at + PACK * n].rearrange("p (r n) -> p r n", r=PACK)
-            for r in range(PACK):
-                for c0, m in (first_cuts if r == 0 else [(0, n)]):
-                    nc.vector.tensor_tensor(
-                        picked[:, r, c0:c0 + m],
-                        x_rows[a * PACK + r][:].indirect(offs_sb[:, columns(s0 + c0, m)]),
-                        gate_sb[:, s0 + c0:s0 + c0 + m], MULT)
-            return picked
+        def gather(i, s0, n):
+            nc.vector.tensor_tensor(
+                staged[i // PAIR][:, i % PAIR, s0:s0 + n],
+                x_rows[i][:].indirect(offs_sb[:, columns(s0, n)]),
+                gate_sb[:, s0:s0 + n], MULT)
 
-        def interleave(picked, w0, c0, n):
-            return (grouped[:, w0 + c0:w0 + c0 + n, :].rearrange("p (c i) r -> p c r i", i=RUN),
-                    picked[:, :, c0:c0 + n].rearrange("p r (c i) -> p c r i", i=RUN))
+        def word(a, s0):
+            return a * S + s0
+
+        def interleave(j, s0, n):
+            a, r0 = j // PAIR, PAIR * (j % PAIR)
+            w0 = word(a, s0)
+            nc.scalar.copy(grouped[:, w0:w0 + n, r0:r0 + PAIR],
+                           staged[j][:, :, s0:s0 + n].rearrange("p r n -> p n r"))
 
         def quantize(w0, n):
             nc.vector.quantize_mx(out=codes[:, w0:w0 + n].bitcast(FP8X4), scales=plane[:, w0:w0 + n],
                                   in_=grouped[:, w0:w0 + n, :].rearrange("p n r -> p (n r)"))
 
-        def multiply(s0, n):
+        def multiply(acc, a, s0, n):
+            j = (s0 // C) * PASSES + a
+            w0 = word(a, s0)
+            nc.tensor.matmul_mx(
+                out=acc[:],
+                lhsT=w_codes[:, j * N * PACK:(j + 1) * N * PACK].bitcast(FP8X4),
+                lhsT_scale=w_plane[:, j * N:(j + 1) * N],
+                rhs=codes[:, w0:w0 + n].bitcast(FP8X4), rhs_scale=plane[:, w0:w0 + n],
+                start=(a == 0), stop=(a == PASSES - 1))
+
+        def activate(acc, s0, n):
             e = s0 // C
-            acc = psum.tile([P, n], F32, name="acc%d" % s0)
-            for a in range(PASSES):
-                j = e * PASSES + a
-                w0 = a * S + s0
-                nc.tensor.matmul_mx(
-                    out=acc[:],
-                    lhsT=w_codes[:, j * N * PACK:(j + 1) * N * PACK].bitcast(FP8X4),
-                    lhsT_scale=w_plane[:, j * N:(j + 1) * N],
-                    rhs=codes[:, w0:w0 + n].bitcast(FP8X4), rhs_scale=plane[:, w0:w0 + n],
-                    start=(a == 0), stop=(a == PASSES - 1))
             nc.scalar.activation(y[:, s0:s0 + n], acc[:], GELU, bias=bias_sb[:, e:e + 1])
 
-        border = PACK * LONG
-        wide = S - C
+        whole = [(0, S)]
+        last = (E - 1) * C
+        cuts = [GATE_PIECES, whole, whole, whole, whole, SECOND_PIECES, whole, LAST_PIECES]
+        for i in range(PASSES * PACK):
+            for s0, n in cuts[i]:
+                gather(i, s0, n)
+                if i % PAIR == 1 and i == PASSES * PACK - 1 and s0 + n == S:
+                    interleave(i // PAIR, s0, last - s0)
+                    interleave(i // PAIR, last, C)
+                elif i % PAIR == 1:
+                    interleave(i // PAIR, s0, n)
 
-        picked = gather(0, 0, S, border, GATE_PIECES)
-        nc.scalar.copy(*interleave(picked, 0, 0, wide))
-        nc.scalar.copy(*interleave(picked, 0, wide, C))
-
-        picked = gather(1, 0, LONG, 0, [(0, LONG)])
-        nc.scalar.copy(*interleave(picked, S, 0, LONG))
-        quantize(0, wide)
-
-        picked = gather(1, LONG, MIDDLE, border, [(0, MIDDLE)])
-        nc.scalar.copy(*interleave(picked, S + LONG, 0, C))
-        nc.scalar.copy(*interleave(picked, S + LONG, C, MIDDLE - C))
-        quantize(wide, C + LONG)
-        for s0 in range(0, LONG, C):
-            multiply(s0, C)
-
-        picked = gather(1, LONG + MIDDLE, SHORT, border - (PACK - 1) * SHORT, [(0, SHORT)])
-        quantize(S + LONG, C)
-        multiply(LONG, C)
-        nc.vector.tensor_copy(*interleave(picked, S + LONG + MIDDLE, 0, SHORT))
-        quantize(S + LONG + C, MIDDLE - C)
-        multiply(LONG + C, MIDDLE - C)
-        quantize(S + LONG + MIDDLE, SHORT)
-        multiply(LONG + MIDDLE, SHORT)
+        for e0 in range(0, E, 2):
+            experts = range(e0, min(e0 + 2, E))
+            accs = [psum.tile([P, C], F32, name="acc%d" % e) for e in experts]
+            for a in range(PASSES):
+                quantize(word(a, e0 * C), len(experts) * C)
+                for e, acc in zip(experts, accs):
+                    multiply(acc, a, e * C, C)
+            for e, acc in zip(experts, accs):
+                activate(acc, e * C, C)
 
         first = keep.tile([P, T], F32, name="first")
         for t0, n in FIRST_PIECES:

@@ -24,7 +24,8 @@ FLOPS = 2 * K * N * S
 BYTES = 4 * K * T + E * K * N + E * K * N // 32 + 4 * N * E + 4 * S + 2 * P * (S + 2 * T) // 16 + 4 * N * T
 
 SECOND_PIECES = [(0, 512), (512, 768)]
-LAST_PIECES = [(0, 320), (320, 384), (704, 576)]
+LAST_PIECES = [(0, 320), (320, 448), (768, 384), (1152, 128)]
+HALF = C // 2
 PAIR = 2
 GATE_PIECES = [(0, 160), (160, 384), (544, 736)]
 FIRST_PIECES = [(0, 448), (448, 192)]
@@ -46,7 +47,10 @@ def tile_moe_pre_lin_gelu_kernel(tc, xT, w_words, w_scales, b, gate, offs, pos1,
         w_codes = keep.tile([P, E * PASSES * N * PACK], U8, name="w_codes", align_bytes=64)
         w_plane = keep.tile([P, E * PASSES * N], U8, name="w_plane", align_bytes=64)
         x_rows = [keep.tile([P, S + SPARE], F32, name="x_rows%d" % i) for i in range(PASSES * PACK)]
-        staged = [keep.tile([P, PAIR, S], F32, name="staged%d" % i) for i in range(PASSES * PACK // PAIR)]
+        staged = [keep.tile([P, PAIR, S], F32, name="staged%d" % i) for i in range(2)]
+        shared = keep.tile([P, (PAIR + 1) * S], F32, name="shared")
+        thirds = shared[:].rearrange("p (r n) -> p r n", n=S)
+        staged = [staged[0][:], thirds[:, 1:3, :], staged[1][:], thirds[:, 0:2, :]]
         grouped = keep.tile([P, PASSES * S, PACK], BF16, name="grouped", align_bytes=64)
         codes = keep.tile([P, PASSES * S], U32, name="codes", align_bytes=64)
         plane = keep.tile([P, PASSES * S], U8, name="plane", align_bytes=64)
@@ -86,9 +90,9 @@ def tile_moe_pre_lin_gelu_kernel(tc, xT, w_words, w_scales, b, gate, offs, pos1,
         def columns(s0, n):
             return slice(s0 // PER_COLUMN, (s0 + n) // PER_COLUMN)
 
-        def gather(i, s0, n):
+        def gather(i, s0, n, to=None):
             nc.vector.tensor_tensor(
-                staged[i // PAIR][:, i % PAIR, s0:s0 + n],
+                staged[i // PAIR][:, i % PAIR, s0:s0 + n] if to is None else to,
                 x_rows[i][:].indirect(offs_sb[:, columns(s0, n)]),
                 gate_sb[:, s0:s0 + n], MULT)
 
@@ -121,25 +125,46 @@ def tile_moe_pre_lin_gelu_kernel(tc, xT, w_words, w_scales, b, gate, offs, pos1,
 
         whole = [(0, S)]
         last = (E - 1) * C
-        cuts = [GATE_PIECES, whole, whole, whole, whole, SECOND_PIECES, whole, LAST_PIECES]
-        for i in range(PASSES * PACK):
+        cuts = [GATE_PIECES, whole, whole, whole, whole, SECOND_PIECES, whole]
+        for i in range(PASSES * PACK - 1):
             for s0, n in cuts[i]:
                 gather(i, s0, n)
-                if i % PAIR == 1 and i == PASSES * PACK - 1 and s0 + n == S:
-                    interleave(i // PAIR, s0, last - s0)
-                    interleave(i // PAIR, last, C)
-                elif i % PAIR == 1:
+                if i % PAIR == 1:
                     interleave(i // PAIR, s0, n)
 
-        for e0 in range(0, E, 2):
-            experts = range(e0, min(e0 + 2, E))
-            accs = [psum.tile([P, C], F32, name="acc%d" % e) for e in experts]
+        groups = [(e * C, C) for e in range(E - 1)] + [(last, HALF), (last + HALF, HALF)]
+        accs = [psum.tile([P, n], F32, name="acc%d" % s0) for s0, n in groups]
+
+        def step(w0, n):
+            quantize(w0, n)
             for a in range(PASSES):
-                quantize(word(a, e0 * C), len(experts) * C)
-                for e, acc in zip(experts, accs):
-                    multiply(acc, a, e * C, C)
-            for e, acc in zip(experts, accs):
-                activate(acc, e * C, C)
+                for acc, (s0, m) in zip(accs, groups):
+                    if w0 <= word(a, s0) < w0 + n:
+                        multiply(acc, a, s0, m)
+
+        i = PASSES * PACK - 1
+        gather(i, *LAST_PIECES[0])
+        interleave(3, *LAST_PIECES[0])
+        gather(i, *LAST_PIECES[1])
+        interleave(3, 320, 2 * C - 320)
+        interleave(3, 2 * C, C)
+        step(0, 2 * C)
+        gather(i, *LAST_PIECES[2])
+        interleave(3, 3 * C, C)
+        interleave(3, last, HALF)
+        step(2 * C, 2 * C)
+        step(last, 2 * C)
+        step(S + C, 2 * C)
+        tail = S - HALF
+        reach = S + 3 * C - HALF - tail
+        pair = shared[:, tail:tail + PAIR * reach].rearrange("p (r n) -> p r n", r=PAIR)[:, :, 0:HALF]
+        gather(i, tail, HALF, pair[:, 1, :])
+        step(S + 3 * C, C)
+        nc.vector.tensor_copy(grouped[:, S + tail:S + S, PAIR:PACK], pair.rearrange("p r n -> p n r"))
+        step(S + last, HALF)
+        step(S + tail, HALF)
+        for acc, (s0, m) in zip(accs, groups):
+            activate(acc, s0, m)
 
         first = keep.tile([P, T], F32, name="first")
         for t0, n in FIRST_PIECES:

@@ -97,13 +97,30 @@ def tile_moe_pre_lin_gelu_kernel(tc, xT, w_words, w_scales, b, gate, offs, pos1,
                 gate_sb[:, s0:s0 + n], MULT)
 
         def word(a, s0):
-            return a * S + s0
+            e = s0 // C
+            if e == 0:
+                return a * C + s0
+            if e < E - 1:
+                return C + a * 3 * C + s0
+            return PASSES * (s0 - s0 % HALF) + a * HALF + s0 % HALF
 
         def interleave(j, s0, n):
             a, r0 = j // PAIR, PAIR * (j % PAIR)
-            w0 = word(a, s0)
-            nc.scalar.copy(grouped[:, w0:w0 + n, r0:r0 + PAIR],
-                           staged[j][:, :, s0:s0 + n].rearrange("p r n -> p n r"))
+            for c0, c1, m in [(0, C, C), (C, 4 * C, 3 * C), (4 * C, S, HALF)]:
+                lo, hi = max(c0, s0), min(c1, s0 + n)
+                if lo >= hi:
+                    continue
+                if (lo, hi) == (c0, c1) and m < hi - lo:
+                    words = grouped[:, PASSES * lo:PASSES * hi, r0:r0 + PAIR]
+                    words = words.rearrange("p (e a c) r -> p e a c r", a=PASSES, c=m)[:, :, a, :, :]
+                    nc.scalar.copy(words, staged[j][:, :, lo:hi].rearrange("p r (e c) -> p e c r", c=m))
+                    continue
+                while lo < hi:
+                    end = min(hi, lo - (lo - c0) % m + m)
+                    w0 = word(a, lo)
+                    nc.scalar.copy(grouped[:, w0:w0 + end - lo, r0:r0 + PAIR],
+                                   staged[j][:, :, lo:end].rearrange("p r n -> p n r"))
+                    lo = end
 
         def quantize(w0, n):
             nc.vector.quantize_mx(out=codes[:, w0:w0 + n].bitcast(FP8X4), scales=plane[:, w0:w0 + n],
@@ -146,23 +163,23 @@ def tile_moe_pre_lin_gelu_kernel(tc, xT, w_words, w_scales, b, gate, offs, pos1,
         gather(i, *LAST_PIECES[0])
         interleave(3, *LAST_PIECES[0])
         gather(i, *LAST_PIECES[1])
-        interleave(3, 320, 2 * C - 320)
-        interleave(3, 2 * C, C)
-        step(0, 2 * C)
+        interleave(3, *LAST_PIECES[1])
+        step(word(0, C), 2 * C)
         gather(i, *LAST_PIECES[2])
         interleave(3, 3 * C, C)
         interleave(3, last, HALF)
-        step(2 * C, 2 * C)
-        step(last, 2 * C)
-        step(S + C, 2 * C)
+        step(word(0, 3 * C), C)
+        step(word(0, 0), 2 * C)
         tail = S - HALF
-        reach = S + 3 * C - HALF - tail
+        reach = S + C - HALF - tail
         pair = shared[:, tail:tail + PAIR * reach].rearrange("p (r n) -> p r n", r=PAIR)[:, :, 0:HALF]
         gather(i, tail, HALF, pair[:, 1, :])
-        step(S + 3 * C, C)
-        nc.vector.tensor_copy(grouped[:, S + tail:S + S, PAIR:PACK], pair.rearrange("p r n -> p n r"))
-        step(S + last, HALF)
-        step(S + tail, HALF)
+        nc.scalar.copy(grouped[:, word(1, tail):word(1, tail) + HALF, PAIR:PACK], pair.rearrange("p r n -> p n r"))
+        step(word(1, C), C)
+        step(word(1, 2 * C), C)
+        step(word(1, 3 * C), C)
+        step(word(0, last), C)
+        step(word(0, tail), C)
         for acc, (s0, m) in zip(accs, groups):
             activate(acc, s0, m)
 

@@ -27,7 +27,7 @@ SECOND_PIECES = [(0, 512), (512, 768)]
 LAST_PIECES = [(0, 320), (320, 448), (768, 384), (1152, 128)]
 HALF = C // 2
 PAIR = 2
-GATE_PIECES = [(0, 160), (160, 384), (544, 736)]
+GATE_PIECES = [(0, 64), (64, 160), (224, 352), (576, 704)]
 FIRST_PIECES = [(0, 448), (448, 192)]
 OUT_PIECES = [(0, 448), (448, 192)]
 SPARE = 16
@@ -98,15 +98,13 @@ def tile_moe_pre_lin_gelu_kernel(tc, xT, w_words, w_scales, b, gate, offs, pos1,
 
         def word(a, s0):
             e = s0 // C
-            if e == 0:
-                return a * C + s0
             if e < E - 1:
-                return C + a * 3 * C + s0
+                return C + s0 if a == 1 else s0 if e == 0 else 4 * C + s0
             return PASSES * (s0 - s0 % HALF) + a * HALF + s0 % HALF
 
         def interleave(j, s0, n):
             a, r0 = j // PAIR, PAIR * (j % PAIR)
-            for c0, c1, m in [(0, C, C), (C, 4 * C, 3 * C), (4 * C, S, HALF)]:
+            for c0, c1, m in ([(0, C, C), (C, 4 * C, 3 * C)], [(0, 4 * C, 4 * C)])[a] + [(4 * C, S, HALF)]:
                 lo, hi = max(c0, s0), min(c1, s0 + n)
                 if lo >= hi:
                     continue
@@ -165,6 +163,11 @@ def tile_moe_pre_lin_gelu_kernel(tc, xT, w_words, w_scales, b, gate, offs, pos1,
         gather(i, *LAST_PIECES[1])
         interleave(3, *LAST_PIECES[1])
         step(word(0, C), 2 * C)
+        idle = psum.tile([P, 2 * C], F32, name="idle")
+        nc.tensor.matmul_mx(
+            out=idle[:], lhsT=w_codes[:, 0:N * PACK].bitcast(FP8X4), lhsT_scale=w_plane[:, 0:N],
+            rhs=codes[:, word(0, C):word(0, 3 * C)].bitcast(FP8X4), rhs_scale=plane[:, word(0, C):word(0, 3 * C)],
+            start=True, stop=True)
         gather(i, *LAST_PIECES[2])
         interleave(3, 3 * C, C)
         interleave(3, last, HALF)

@@ -163,11 +163,6 @@ def tile_moe_pre_lin_gelu_kernel(tc, xT, w_words, w_scales, b, gate, offs, pos1,
         gather(i, *LAST_PIECES[1])
         interleave(3, *LAST_PIECES[1])
         step(word(0, C), 2 * C)
-        idle = psum.tile([P, 2 * C], F32, name="idle")
-        nc.tensor.matmul_mx(
-            out=idle[:], lhsT=w_codes[:, 0:N * PACK].bitcast(FP8X4), lhsT_scale=w_plane[:, 0:N],
-            rhs=codes[:, word(0, C):word(0, 3 * C)].bitcast(FP8X4), rhs_scale=plane[:, word(0, C):word(0, 3 * C)],
-            start=True, stop=True)
         gather(i, *LAST_PIECES[2])
         interleave(3, 3 * C, C)
         interleave(3, last, HALF)

@@ -1,6 +1,7 @@
 from contextlib import ExitStack
 
 import concourse.mybir as mybir
+from concourse.masks import make_identity
 
 K, T, E, C, N = 1024, 640, 5, 256, 128
 S = E * C
@@ -18,6 +19,7 @@ U8 = mybir.dt.uint8
 FP8X4 = mybir.dt.float8_e4m3fn_x4
 MULT = mybir.AluOpType.mult
 ADD = mybir.AluOpType.add
+COPY = mybir.ActivationFunctionType.Copy
 GELU = mybir.ActivationFunctionType.Gelu_apprx_tanh
 
 FLOPS = 2 * K * N * S
@@ -27,10 +29,14 @@ SECOND_PIECES = [(0, 512), (512, 768)]
 LAST_PIECES = [(0, 320), (320, 448), (768, 384), (1152, 128)]
 HALF = C // 2
 PAIR = 2
-GATE_PIECES = [(0, 64), (64, 160), (224, 352), (576, 704)]
+GATE_PIECES = [(0, 512), (512, 512), (1024, 256)]
 FIRST_PIECES = [(0, 448), (448, 192)]
 OUT_PIECES = [(0, 448), (448, 192)]
 SPARE = 16
+BANK = 512
+BLOCKS = S // P
+COPIED = (0,)
+WIDE = 1728
 
 
 def tile_moe_pre_lin_gelu_kernel(tc, xT, w_words, w_scales, b, gate, offs, pos1, pos2, out):
@@ -46,7 +52,8 @@ def tile_moe_pre_lin_gelu_kernel(tc, xT, w_words, w_scales, b, gate, offs, pos1,
         bias_sb = keep.tile([P, E], F32, name="bias_sb")
         w_codes = keep.tile([P, E * PASSES * N * PACK], U8, name="w_codes", align_bytes=64)
         w_plane = keep.tile([P, E * PASSES * N], U8, name="w_plane", align_bytes=64)
-        x_rows = [keep.tile([P, S + SPARE], F32, name="x_rows%d" % i) for i in range(PASSES * PACK)]
+        x_rows = [keep.tile([P, WIDE if i in COPIED else S + SPARE], F32, name="x_rows%d" % i)
+                  for i in range(PASSES * PACK)]
         staged = [keep.tile([P, PAIR, S], F32, name="staged%d" % i) for i in range(2)]
         shared = keep.tile([P, (PAIR + 1) * S], F32, name="shared")
         thirds = shared[:].rearrange("p (r n) -> p r n", n=S)
@@ -55,6 +62,11 @@ def tile_moe_pre_lin_gelu_kernel(tc, xT, w_words, w_scales, b, gate, offs, pos1,
         codes = keep.tile([P, PASSES * S], U32, name="codes", align_bytes=64)
         plane = keep.tile([P, PASSES * S], U8, name="plane", align_bytes=64)
         y = keep.tile([P, S], F32, name="y")
+        ident = keep.tile([P, P], F32, name="ident")
+        plain = keep.tile([P, S], F32, name="plain")
+        gate_col = keep.tile([P, BLOCKS], F32, name="gate_col")
+        banks = [psum.tile([P, BANK], F32, name="bank%d" % i) for i in range(8)]
+        make_identity(nc, ident[:])
 
         nc.vector.memset(w_plane[:].bitcast(I32), 0)
         warm = keep.tile([P, 1], F32, name="warm")
@@ -71,13 +83,15 @@ def tile_moe_pre_lin_gelu_kernel(tc, xT, w_words, w_scales, b, gate, offs, pos1,
 
         load_x(0)
         nc.sync.dma_start(offs_sb[:], offs)
+        load_x(1)
         for i in range(len(GATE_PIECES)):
             load_gate(i)
-        for i in range(1, PASSES * PACK):
+        for i in range(2, PASSES * PACK):
             load_x(i)
-        nc.sync.dma_start(
-            w_codes[:].bitcast(I32).rearrange("p (g n) -> p g n", n=N),
-            w_words.rearrange("e a p n r -> p (e a) (n r)").bitcast(I32))
+        w_to = w_codes[:].bitcast(I32).rearrange("p (g n) -> p g n", n=N)
+        w_from = w_words.rearrange("e a p n r -> p (e a) (n r)").bitcast(I32)
+        for g0 in (0, E):
+            nc.sync.dma_start(w_to[:, g0:g0 + E, :], w_from[:, g0:g0 + E, :])
         scale_rows = w_scales.rearrange("e a q n -> q (e a) n").bitcast(I32)
         for q in range(4):
             nc.sync.dma_start(
@@ -90,7 +104,39 @@ def tile_moe_pre_lin_gelu_kernel(tc, xT, w_words, w_scales, b, gate, offs, pos1,
         def columns(s0, n):
             return slice(s0 // PER_COLUMN, (s0 + n) // PER_COLUMN)
 
+        later = [(2, 0, 0), (2, 1, 0), (2, 1, SECOND_PIECES[1][0]), (3, 0, 0)]
+        spots = [(1, 1, m * P) for m in range(BLOCKS - len(later))] + later
+        turned = [staged[j][:, r, c:c + P] for j, r, c in spots]
+
+        def blocks(tile):
+            return [tile[:, c:c + P] for c in range(0, S, P)]
+
+        def turn(src, first_bank):
+            runs = []
+            for c0 in range(0, S, BANK):
+                bank = banks[(first_bank + c0 // BANK) % len(banks)]
+                n = min(BANK, S - c0)
+                for c in range(0, n, P):
+                    nc.tensor.transpose(bank[:, c:c + P], src[(c0 + c) // P], ident[:])
+                runs.append((bank, c0, n))
+            return runs
+
+        def gate_turned():
+            for bank, c0, n in turn(blocks(gate_sb), 0):
+                nc.scalar.copy(gate_col[:, c0 // P:(c0 + n) // P], bank[:, 0:n:P])
+            for bank, c0, n in turn(blocks(plain), 3):
+                for c in range(0, n, P):
+                    m = (c0 + c) // P
+                    nc.scalar.activation(turned[m], bank[:, c:c + P], COPY,
+                                         scale=gate_col[:, m:m + 1])
+            for bank, c0, n in turn(turned, 6):
+                nc.scalar.copy(staged[0][:, 0, c0:c0 + n], bank[:, 0:n])
+
         def gather(i, s0, n, to=None):
+            if i in COPIED:
+                nc.vector.tensor_copy(plain[:], x_rows[i][:].indirect(offs_sb[:]))
+                gate_turned()
+                return
             nc.vector.tensor_tensor(
                 staged[i // PAIR][:, i % PAIR, s0:s0 + n] if to is None else to,
                 x_rows[i][:].indirect(offs_sb[:, columns(s0, n)]),
@@ -128,7 +174,7 @@ def tile_moe_pre_lin_gelu_kernel(tc, xT, w_words, w_scales, b, gate, offs, pos1,
             j = (s0 // C) * PASSES + a
             w0 = word(a, s0)
             nc.tensor.matmul_mx(
-                out=acc[:],
+                out=acc,
                 lhsT=w_codes[:, j * N * PACK:(j + 1) * N * PACK].bitcast(FP8X4),
                 lhsT_scale=w_plane[:, j * N:(j + 1) * N],
                 rhs=codes[:, w0:w0 + n].bitcast(FP8X4), rhs_scale=plane[:, w0:w0 + n],
@@ -136,11 +182,11 @@ def tile_moe_pre_lin_gelu_kernel(tc, xT, w_words, w_scales, b, gate, offs, pos1,
 
         def activate(acc, s0, n):
             e = s0 // C
-            nc.scalar.activation(y[:, s0:s0 + n], acc[:], GELU, bias=bias_sb[:, e:e + 1])
+            nc.scalar.activation(y[:, s0:s0 + n], acc, GELU, bias=bias_sb[:, e:e + 1])
 
         whole = [(0, S)]
         last = (E - 1) * C
-        cuts = [GATE_PIECES, whole, whole, whole, whole, SECOND_PIECES, whole]
+        cuts = [whole, whole, whole, whole, whole, SECOND_PIECES, whole]
         for i in range(PASSES * PACK - 1):
             for s0, n in cuts[i]:
                 gather(i, s0, n)
@@ -148,7 +194,7 @@ def tile_moe_pre_lin_gelu_kernel(tc, xT, w_words, w_scales, b, gate, offs, pos1,
                     interleave(i // PAIR, s0, n)
 
         groups = [(e * C, C) for e in range(E - 1)] + [(last, HALF), (last + HALF, HALF)]
-        accs = [psum.tile([P, n], F32, name="acc%d" % s0) for s0, n in groups]
+        accs = [banks[1 + j][:, 0:n] for j, (s0, n) in enumerate(groups)]
 
         def step(w0, n):
             quantize(w0, n)

@@ -29,7 +29,7 @@ SECOND_PIECES = [(0, 512), (512, 768)]
 LAST_PIECES = [(0, 320), (320, 448), (768, 384), (1152, 128)]
 HALF = C // 2
 PAIR = 2
-GATE_PIECES = [(0, 512), (512, 512), (1024, 256)]
+GATE_PIECES = [(0, 1280)]
 FIRST_PIECES = [(0, 448), (448, 192)]
 OUT_PIECES = [(0, 448), (448, 192)]
 SPARE = 16
@@ -83,15 +83,13 @@ def tile_moe_pre_lin_gelu_kernel(tc, xT, w_words, w_scales, b, gate, offs, pos1,
 
         load_x(0)
         nc.sync.dma_start(offs_sb[:], offs)
-        load_x(1)
-        for i in range(len(GATE_PIECES)):
-            load_gate(i)
-        for i in range(2, PASSES * PACK):
+        load_gate(0)
+        for i in range(1, PASSES * PACK):
             load_x(i)
         w_to = w_codes[:].bitcast(I32).rearrange("p (g n) -> p g n", n=N)
         w_from = w_words.rearrange("e a p n r -> p (e a) (n r)").bitcast(I32)
-        for g0 in (0, E):
-            nc.sync.dma_start(w_to[:, g0:g0 + E, :], w_from[:, g0:g0 + E, :])
+        for g0 in range(0, E * PASSES, PASSES):
+            nc.sync.dma_start(w_to[:, g0:g0 + PASSES, :], w_from[:, g0:g0 + PASSES, :])
         scale_rows = w_scales.rearrange("e a q n -> q (e a) n").bitcast(I32)
         for q in range(4):
             nc.sync.dma_start(
@@ -223,7 +221,8 @@ def tile_moe_pre_lin_gelu_kernel(tc, xT, w_words, w_scales, b, gate, offs, pos1,
         step(word(1, 2 * C), C)
         step(word(1, 3 * C), C)
         step(word(0, last), C)
-        step(word(0, tail), C)
+        step(word(0, tail), HALF)
+        step(word(1, tail), HALF)
         for acc, (s0, m) in zip(accs, groups):
             activate(acc, s0, m)
 

@@ -25,7 +25,6 @@ GELU = mybir.ActivationFunctionType.Gelu_apprx_tanh
 FLOPS = 2 * K * N * S
 BYTES = 4 * K * T + E * K * N + E * K * N // 32 + 4 * N * E + 4 * S + 2 * P * (S + 2 * T) // 16 + 4 * N * T
 
-SECOND_PIECES = [(0, 512), (512, 768)]
 LAST_PIECES = [(0, 320), (320, 448), (768, 384), (1152, 128)]
 HALF = C // 2
 PAIR = 2
@@ -102,7 +101,7 @@ def tile_moe_pre_lin_gelu_kernel(tc, xT, w_words, w_scales, b, gate, offs, pos1,
         def columns(s0, n):
             return slice(s0 // PER_COLUMN, (s0 + n) // PER_COLUMN)
 
-        later = [(2, 0, 0), (2, 1, 0), (2, 1, SECOND_PIECES[1][0]), (3, 0, 0)]
+        later = [(2, 0, 0), (2, 1, 0), (3, 0, 0)]
         spots = [(1, 1, m * P) for m in range(BLOCKS - len(later))] + later
         turned = [staged[j][:, r, c:c + P] for j, r, c in spots]
 
@@ -184,7 +183,7 @@ def tile_moe_pre_lin_gelu_kernel(tc, xT, w_words, w_scales, b, gate, offs, pos1,
 
         whole = [(0, S)]
         last = (E - 1) * C
-        cuts = [whole, whole, whole, whole, whole, SECOND_PIECES, whole]
+        cuts = [whole] * (PASSES * PACK - 1)
         for i in range(PASSES * PACK - 1):
             for s0, n in cuts[i]:
                 gather(i, s0, n)

@@ -53,10 +53,15 @@ def tile_moe_pre_lin_gelu_kernel(tc, xT, w_words, w_scales, b, gate, offs, pos1,
         w_plane = keep.tile([P, E * PASSES * N], U8, name="w_plane", align_bytes=64)
         x_rows = [keep.tile([P, WIDE if i in COPIED else S + SPARE], F32, name="x_rows%d" % i)
                   for i in range(PASSES * PACK)]
-        staged = [keep.tile([P, PAIR, S], F32, name="staged%d" % i) for i in range(2)]
-        shared = keep.tile([P, (PAIR + 1) * S], F32, name="shared")
-        thirds = shared[:].rearrange("p (r n) -> p r n", n=S)
-        staged = [staged[0][:], thirds[:, 1:3, :], staged[1][:], thirds[:, 0:2, :]]
+        first_pair = keep.tile([P, PAIR, S], F32, name="first_pair")
+        tail = S - HALF
+        late = 3 * S + tail - HALF
+        shared = keep.tile([P, late + PAIR * S], F32, name="shared")
+
+        def rows(c0, step, count, n):
+            return shared[:, c0:c0 + count * step].rearrange("p (r n) -> p r n", n=step)[:, :, 0:n]
+
+        staged = [first_pair[:], rows(late, S, PAIR, S), rows(0, S, PAIR, S), rows(2 * S, late - 2 * S, PAIR, S)]
         grouped = keep.tile([P, PASSES * S, PACK], BF16, name="grouped", align_bytes=64)
         codes = keep.tile([P, PASSES * S], U32, name="codes", align_bytes=64)
         plane = keep.tile([P, PASSES * S], U8, name="plane", align_bytes=64)
@@ -163,13 +168,13 @@ def tile_moe_pre_lin_gelu_kernel(tc, xT, w_words, w_scales, b, gate, offs, pos1,
                                    staged[j][:, :, lo:end].rearrange("p r n -> p n r"))
                     lo = end
 
-        def quantize(w0, n):
-            nc.vector.quantize_mx(out=codes[:, w0:w0 + n].bitcast(FP8X4), scales=plane[:, w0:w0 + n],
+        def quantize(w0, n, c0):
+            nc.vector.quantize_mx(out=codes[:, c0:c0 + n].bitcast(FP8X4), scales=plane[:, c0:c0 + n],
                                   in_=grouped[:, w0:w0 + n, :].rearrange("p n r -> p (n r)"))
 
-        def multiply(acc, a, s0, n):
+        def multiply(acc, a, s0, n, shift):
             j = (s0 // C) * PASSES + a
-            w0 = word(a, s0)
+            w0 = word(a, s0) + shift
             nc.tensor.matmul_mx(
                 out=acc,
                 lhsT=w_codes[:, j * N * PACK:(j + 1) * N * PACK].bitcast(FP8X4),
@@ -188,17 +193,17 @@ def tile_moe_pre_lin_gelu_kernel(tc, xT, w_words, w_scales, b, gate, offs, pos1,
             for s0, n in cuts[i]:
                 gather(i, s0, n)
                 if i % PAIR == 1:
-                    interleave(i // PAIR, s0, n)
+                    interleave(i // PAIR, s0, n if i < PACK else tail)
 
         groups = [(e * C, C) for e in range(E - 1)] + [(last, HALF), (last + HALF, HALF)]
         accs = [banks[1 + j][:, 0:n] for j, (s0, n) in enumerate(groups)]
 
-        def step(w0, n):
-            quantize(w0, n)
+        def step(w0, n, shift=0):
+            quantize(w0, n, w0 + shift)
             for a in range(PASSES):
                 for acc, (s0, m) in zip(accs, groups):
                     if w0 <= word(a, s0) < w0 + n:
-                        multiply(acc, a, s0, m)
+                        multiply(acc, a, s0, m, shift)
 
         i = PASSES * PACK - 1
         gather(i, *LAST_PIECES[0])
@@ -211,16 +216,14 @@ def tile_moe_pre_lin_gelu_kernel(tc, xT, w_words, w_scales, b, gate, offs, pos1,
         interleave(3, last, HALF)
         step(word(0, 3 * C), C)
         step(word(0, 0), 2 * C)
-        tail = S - HALF
-        reach = S + C - HALF - tail
-        pair = shared[:, tail:tail + PAIR * reach].rearrange("p (r n) -> p r n", r=PAIR)[:, :, 0:HALF]
-        gather(i, tail, HALF, pair[:, 1, :])
-        nc.scalar.copy(grouped[:, word(1, tail):word(1, tail) + HALF, PAIR:PACK], pair.rearrange("p r n -> p n r"))
+        four = rows(tail, S, PACK, HALF)
+        gather(i, tail, HALF, four[:, PACK - 1, :])
+        nc.scalar.copy(grouped[:, word(1, tail):word(1, tail) + HALF, :], four.rearrange("p r n -> p n r"))
         step(word(1, C), C)
         step(word(1, 2 * C), C)
         step(word(1, 3 * C), C)
         step(word(0, last), C)
-        step(word(0, tail), HALF)
+        step(word(0, tail), HALF, word(1, C) - word(0, tail))
         step(word(1, tail), HALF)
         for acc, (s0, m) in zip(accs, groups):
             activate(acc, s0, m)

@@ -218,7 +218,9 @@ def tile_moe_pre_lin_gelu_kernel(tc, xT, w_words, w_scales, b, gate, offs, pos1,
         step(word(0, 0), 2 * C)
         four = rows(tail, S, PACK, HALF)
         gather(i, tail, HALF, four[:, PACK - 1, :])
-        nc.scalar.copy(grouped[:, word(1, tail):word(1, tail) + HALF, :], four.rearrange("p r n -> p n r"))
+        nc.scalar.copy(
+            grouped[:, word(1, tail):word(1, tail) + HALF, :].rearrange("p (c i) r -> p c r i", i=PACK),
+            four.rearrange("p r (c i) -> p c r i", i=PACK))
         step(word(1, C), C)
         step(word(1, 2 * C), C)
         step(word(1, 3 * C), C)

@@ -29,8 +29,8 @@ LAST_PIECES = [(0, 320), (320, 448), (768, 384), (1152, 128)]
 HALF = C // 2
 PAIR = 2
 GATE_PIECES = [(0, 1280)]
-FIRST_PIECES = [(0, 448), (448, 192)]
-OUT_PIECES = [(0, 448), (448, 192)]
+FIRST_PIECES = [(0, 384), (384, 256)]
+OUT_PIECES = [(0, 384), (384, 256)]
 SPARE = 16
 BANK = 512
 BLOCKS = S // P

@@ -1,7 +1,6 @@
 from contextlib import ExitStack
 
 import concourse.mybir as mybir
-from concourse.masks import make_identity
 
 K, T, E, C, N = 1024, 640, 5, 256, 128
 S = E * C
@@ -25,17 +24,13 @@ GELU = mybir.ActivationFunctionType.Gelu_apprx_tanh
 FLOPS = 2 * K * N * S
 BYTES = 4 * K * T + E * K * N + E * K * N // 32 + 4 * N * E + 4 * S + 2 * P * (S + 2 * T) // 16 + 4 * N * T
 
-LAST_PIECES = [(0, 320), (320, 448), (768, 384), (1152, 128)]
 HALF = C // 2
-PAIR = 2
-GATE_PIECES = [(0, 1280)]
-FIRST_PIECES = [(0, 384), (384, 256)]
-OUT_PIECES = [(0, 384), (384, 256)]
-SPARE = 16
 BANK = 512
-BLOCKS = S // P
-COPIED = (0,)
-WIDE = 1728
+WIDE = 1024
+OWN0 = 512
+OWN1 = 128
+HELP = 256
+RUN = 2
 
 
 def tile_moe_pre_lin_gelu_kernel(tc, xT, w_words, w_scales, b, gate, offs, pos1, pos2, out):
@@ -51,26 +46,11 @@ def tile_moe_pre_lin_gelu_kernel(tc, xT, w_words, w_scales, b, gate, offs, pos1,
         bias_sb = keep.tile([P, E], F32, name="bias_sb")
         w_codes = keep.tile([P, E * PASSES * N * PACK], U8, name="w_codes", align_bytes=64)
         w_plane = keep.tile([P, E * PASSES * N], U8, name="w_plane", align_bytes=64)
-        x_rows = [keep.tile([P, WIDE if i in COPIED else S + SPARE], F32, name="x_rows%d" % i)
-                  for i in range(PASSES * PACK)]
-        first_pair = keep.tile([P, PAIR, S], F32, name="first_pair")
-        tail = S - HALF
-        late = 3 * S + tail - HALF
-        shared = keep.tile([P, late + PAIR * S], F32, name="shared")
-
-        def rows(c0, step, count, n):
-            return shared[:, c0:c0 + count * step].rearrange("p (r n) -> p r n", n=step)[:, :, 0:n]
-
-        staged = [first_pair[:], rows(late, S, PAIR, S), rows(0, S, PAIR, S), rows(2 * S, late - 2 * S, PAIR, S)]
-        grouped = keep.tile([P, PASSES * S, PACK], BF16, name="grouped", align_bytes=64)
+        x_rows = [keep.tile([P, WIDE if i < PACK else T], F32, name="x_rows%d" % i) for i in range(PASSES * PACK)]
         codes = keep.tile([P, PASSES * S], U32, name="codes", align_bytes=64)
         plane = keep.tile([P, PASSES * S], U8, name="plane", align_bytes=64)
         y = keep.tile([P, S], F32, name="y")
-        ident = keep.tile([P, P], F32, name="ident")
-        plain = keep.tile([P, S], F32, name="plain")
-        gate_col = keep.tile([P, BLOCKS], F32, name="gate_col")
-        banks = [psum.tile([P, BANK], F32, name="bank%d" % i) for i in range(8)]
-        make_identity(nc, ident[:])
+        banks = [psum.tile([P, BANK], F32, name="bank%d" % i) for i in range(E + 1)]
 
         nc.vector.memset(w_plane[:].bitcast(I32), 0)
         warm = keep.tile([P, 1], F32, name="warm")
@@ -81,15 +61,16 @@ def tile_moe_pre_lin_gelu_kernel(tc, xT, w_words, w_scales, b, gate, offs, pos1,
         def load_x(i):
             nc.sync.dma_start(x_rows[i][:, 0:T], x_view[i // PACK, i % PACK])
 
-        def load_gate(i):
-            s0, n = GATE_PIECES[i]
-            nc.sync.dma_start(gate_sb[:, s0:s0 + n], gate[0:P, s0:s0 + n])
+        def load_gate(s0, s1):
+            nc.sync.dma_start(gate_sb[:, s0:s1], gate[0:P, s0:s1])
 
         load_x(0)
         nc.sync.dma_start(offs_sb[:], offs)
-        load_gate(0)
-        for i in range(1, PASSES * PACK):
+        load_gate(0, OWN0)
+        for i in range(1, PASSES * PACK - 1):
             load_x(i)
+        load_gate(OWN0, S)
+        load_x(PASSES * PACK - 1)
         w_to = w_codes[:].bitcast(I32).rearrange("p (g n) -> p g n", n=N)
         w_from = w_words.rearrange("e a p n r -> p (e a) (n r)").bitcast(I32)
         for g0 in range(0, E * PASSES, PASSES):
@@ -106,134 +87,110 @@ def tile_moe_pre_lin_gelu_kernel(tc, xT, w_words, w_scales, b, gate, offs, pos1,
         def columns(s0, n):
             return slice(s0 // PER_COLUMN, (s0 + n) // PER_COLUMN)
 
-        later = [(2, 0, 0), (2, 1, 0), (3, 0, 0)]
-        spots = [(1, 1, m * P) for m in range(BLOCKS - len(later))] + later
-        turned = [staged[j][:, r, c:c + P] for j, r, c in spots]
+        def picked(a, r, s0, n):
+            return x_rows[a * PACK + r][:].indirect(offs_sb[:, columns(s0, n)])
 
-        def blocks(tile):
-            return [tile[:, c:c + P] for c in range(0, S, P)]
+        def by_runs(staged):
+            return staged.rearrange("p r (c i) -> p c r i", i=RUN)
 
-        def turn(src, first_bank):
-            runs = []
-            for c0 in range(0, S, BANK):
-                bank = banks[(first_bank + c0 // BANK) % len(banks)]
-                n = min(BANK, S - c0)
-                for c in range(0, n, P):
-                    nc.tensor.transpose(bank[:, c:c + P], src[(c0 + c) // P], ident[:])
-                runs.append((bank, c0, n))
-            return runs
+        grouped = {}
 
-        def gate_turned():
-            for bank, c0, n in turn(blocks(gate_sb), 0):
-                nc.scalar.copy(gate_col[:, c0 // P:(c0 + n) // P], bank[:, 0:n:P])
-            for bank, c0, n in turn(blocks(plain), 3):
-                for c in range(0, n, P):
-                    m = (c0 + c) // P
-                    nc.scalar.activation(turned[m], bank[:, c:c + P], COPY,
-                                         scale=gate_col[:, m:m + 1])
-            for bank, c0, n in turn(turned, 6):
-                nc.scalar.copy(staged[0][:, 0, c0:c0 + n], bank[:, 0:n])
+        def words(a, s0, n):
+            tile = keep.tile([P, n, PACK], BF16, name="grouped%d_%d" % (a, s0), align_bytes=64)
+            grouped[a, s0] = tile
+            return tile[:].rearrange("p (c i) r -> p c r i", i=RUN)
 
-        def gather(i, s0, n, to=None):
-            if i in COPIED:
-                nc.vector.tensor_copy(plain[:], x_rows[i][:].indirect(offs_sb[:]))
-                gate_turned()
-                return
-            nc.vector.tensor_tensor(
-                staged[i // PAIR][:, i % PAIR, s0:s0 + n] if to is None else to,
-                x_rows[i][:].indirect(offs_sb[:, columns(s0, n)]),
-                gate_sb[:, s0:s0 + n], MULT)
+        def gather_gated(staged, a, r, s0, n):
+            nc.vector.tensor_tensor(staged[:, r, :], picked(a, r, s0, n), gate_sb[:, s0:s0 + n], MULT)
 
-        def word(a, s0):
-            e = s0 // C
-            if e < E - 1:
-                return C + s0 if a == 1 else s0 if e == 0 else 4 * C + s0
-            return PASSES * (s0 - s0 % HALF) + a * HALF + s0 % HALF
+        def gather_plain(staged, a, s0, n):
+            for r in range(PACK):
+                nc.scalar.activation(staged[:, r, :], picked(a, r, s0, n), COPY)
 
-        def interleave(j, s0, n):
-            a, r0 = j // PAIR, PAIR * (j % PAIR)
-            for c0, c1, m in ([(0, C, C), (C, 4 * C, 3 * C)], [(0, 4 * C, 4 * C)])[a] + [(4 * C, S, HALF)]:
-                lo, hi = max(c0, s0), min(c1, s0 + n)
-                if lo >= hi:
-                    continue
-                if (lo, hi) == (c0, c1) and m < hi - lo:
-                    words = grouped[:, PASSES * lo:PASSES * hi, r0:r0 + PAIR]
-                    words = words.rearrange("p (e a c) r -> p e a c r", a=PASSES, c=m)[:, :, a, :, :]
-                    nc.scalar.copy(words, staged[j][:, :, lo:hi].rearrange("p r (e c) -> p e c r", c=m))
-                    continue
-                while lo < hi:
-                    end = min(hi, lo - (lo - c0) % m + m)
-                    w0 = word(a, lo)
-                    nc.scalar.copy(grouped[:, w0:w0 + end - lo, r0:r0 + PAIR],
-                                   staged[j][:, :, lo:end].rearrange("p r n -> p n r"))
-                    lo = end
+        def lay(staged, a, s0, n):
+            nc.vector.tensor_copy(words(a, s0, n), by_runs(staged))
 
-        def quantize(w0, n, c0):
-            nc.vector.quantize_mx(out=codes[:, c0:c0 + n].bitcast(FP8X4), scales=plane[:, c0:c0 + n],
-                                  in_=grouped[:, w0:w0 + n, :].rearrange("p n r -> p (n r)"))
+        def gate_and_lay(staged, a, s0, n):
+            weight = gate_sb[:, s0:s0 + n].rearrange("p (c i) -> p c i", i=RUN).unsqueeze(2)
+            nc.vector.tensor_tensor(words(a, s0, n), by_runs(staged), weight.to_broadcast([P, n // RUN, PACK, RUN]), MULT)
 
-        def multiply(acc, a, s0, n, shift):
-            j = (s0 // C) * PASSES + a
-            w0 = word(a, s0) + shift
-            nc.tensor.matmul_mx(
-                out=acc,
-                lhsT=w_codes[:, j * N * PACK:(j + 1) * N * PACK].bitcast(FP8X4),
-                lhsT_scale=w_plane[:, j * N:(j + 1) * N],
-                rhs=codes[:, w0:w0 + n].bitcast(FP8X4), rhs_scale=plane[:, w0:w0 + n],
-                start=(a == 0), stop=(a == PASSES - 1))
-
-        def activate(acc, s0, n):
-            e = s0 // C
-            nc.scalar.activation(y[:, s0:s0 + n], acc, GELU, bias=bias_sb[:, e:e + 1])
-
-        whole = [(0, S)]
         last = (E - 1) * C
-        cuts = [whole] * (PASSES * PACK - 1)
-        for i in range(PASSES * PACK - 1):
-            for s0, n in cuts[i]:
-                gather(i, s0, n)
-                if i % PAIR == 1:
-                    interleave(i // PAIR, s0, n if i < PACK else tail)
-
         groups = [(e * C, C) for e in range(E - 1)] + [(last, HALF), (last + HALF, HALF)]
-        accs = [banks[1 + j][:, 0:n] for j, (s0, n) in enumerate(groups)]
+        accs = [banks[j][:, 0:n] for j, (s0, n) in enumerate(groups)]
+        done = [set(), set()]
+        issued = set()
 
-        def step(w0, n, shift=0):
-            quantize(w0, n, w0 + shift)
-            for a in range(PASSES):
-                for acc, (s0, m) in zip(accs, groups):
-                    if w0 <= word(a, s0) < w0 + n:
-                        multiply(acc, a, s0, m, shift)
+        def quantize(a, s0, n):
+            c0 = a * S + s0
+            nc.vector.quantize_mx(out=codes[:, c0:c0 + n].bitcast(FP8X4), scales=plane[:, c0:c0 + n],
+                                  in_=grouped[a, s0][:].rearrange("p n r -> p (n r)"))
+            for h in range(s0, s0 + n, HALF):
+                done[a].add(h)
+            for acc, (g0, m) in zip(accs, groups):
+                for pa in range(PASSES):
+                    ready = all(h in done[q] for q in range(pa + 1) for h in range(g0, g0 + m, HALF))
+                    if ready and (pa, g0) not in issued:
+                        issued.add((pa, g0))
+                        j = (g0 // C) * PASSES + pa
+                        w0 = pa * S + g0
+                        nc.tensor.matmul_mx(
+                            out=acc,
+                            lhsT=w_codes[:, j * N * PACK:(j + 1) * N * PACK].bitcast(FP8X4),
+                            lhsT_scale=w_plane[:, j * N:(j + 1) * N],
+                            rhs=codes[:, w0:w0 + m].bitcast(FP8X4), rhs_scale=plane[:, w0:w0 + m],
+                            start=(pa == 0), stop=(pa == PASSES - 1))
 
-        i = PASSES * PACK - 1
-        gather(i, *LAST_PIECES[0])
-        interleave(3, *LAST_PIECES[0])
-        gather(i, *LAST_PIECES[1])
-        interleave(3, *LAST_PIECES[1])
-        step(word(0, C), 2 * C)
-        gather(i, *LAST_PIECES[2])
-        interleave(3, 3 * C, C)
-        interleave(3, last, HALF)
-        step(word(0, 3 * C), C)
-        step(word(0, 0), 2 * C)
-        four = rows(tail, S, PACK, HALF)
-        gather(i, tail, HALF, four[:, PACK - 1, :])
-        nc.scalar.copy(
-            grouped[:, word(1, tail):word(1, tail) + HALF, :].rearrange("p (c i) r -> p c r i", i=PACK),
-            four.rearrange("p r (c i) -> p c r i", i=PACK))
-        step(word(1, C), C)
-        step(word(1, 2 * C), C)
-        step(word(1, 3 * C), C)
-        step(word(0, last), C)
-        step(word(0, tail), HALF, word(1, C) - word(0, tail))
-        step(word(1, tail), HALF)
+        rest = S - OWN0
+        third = rest // 2
+        own0 = keep.tile([P, PACK, OWN0], F32, name="own0")
+        own1 = keep.tile([P, PACK, OWN1], F32, name="own1")
+        early = keep.tile([P, PACK, rest], F32, name="early")
+        middle = keep.tile([P, PACK, 512], F32, name="middle")
+
+        nc.vector.tensor_copy(early[:, 0, 0:HELP], picked(0, 0, OWN0, HELP))
+        nc.scalar.activation(early[:, 0, HELP:rest], picked(0, 0, OWN0 + HELP, rest - HELP), COPY)
+        for r in range(1, PACK):
+            nc.scalar.activation(early[:, r, :], picked(0, r, OWN0, rest), COPY)
+        for r in range(PACK):
+            gather_gated(own0, 0, r, 0, OWN0)
+        gather_gated(own1, 1, 0, 0, OWN1)
+        lay(own0[:], 0, 0, OWN0)
+        gather_gated(own1, 1, 1, 0, OWN1)
+        quantize(0, 0, OWN0)
+        gather_gated(own1, 1, 2, 0, OWN1)
+        gather_plain(middle, 1, OWN1, 512)
+        gate_and_lay(early[:, :, 0:third], 0, OWN0, third)
+        gather_gated(own1, 1, 3, 0, OWN1)
+        gate_and_lay(early[:, :, third:rest], 0, OWN0 + third, third)
+        late = [(OWN1 + 512, third, 0), (last, HALF, third), (last + HALF, HALF, third + HALF)]
+        for s0, n, c0 in late:
+            gather_plain(early[:, :, c0:c0 + n], 1, s0, n)
+        lay(own1[:], 1, 0, OWN1)
+        quantize(0, OWN0, third)
+        quantize(0, OWN0 + third, third)
+        gate_and_lay(middle[:], 1, OWN1, 512)
+        quantize(1, 0, OWN1)
+        quantize(1, OWN1, 512)
+        before = None
+        for s0, n, c0 in late:
+            gate_and_lay(early[:, :, c0:c0 + n], 1, s0, n)
+            if before:
+                quantize(1, *before)
+            before = (s0, n)
+        quantize(1, *before)
         for acc, (s0, m) in zip(accs, groups):
-            activate(acc, s0, m)
+            e = s0 // C
+            nc.scalar.activation(y[:, s0:s0 + m], acc, GELU, bias=bias_sb[:, e:e + 1])
 
         first = keep.tile([P, T], F32, name="first")
-        for t0, n in FIRST_PIECES:
-            nc.vector.tensor_copy(first[:, t0:t0 + n], y[:].indirect(pos1_sb[:, columns(t0, n)]))
-        for t0, n in OUT_PIECES:
-            total = keep.tile([P, n], F32, name="total%d" % t0)
-            nc.vector.tensor_tensor(total[:], y[:].indirect(pos2_sb[:, columns(t0, n)]), first[:, t0:t0 + n], ADD)
-            nc.sync.dma_start(out[:, t0:t0 + n], total[:])
+        nc.vector.tensor_copy(first[:, 128:256], y[:].indirect(pos1_sb[:, columns(128, 128)]))
+        for t0, n in [(0, 128), (256, 128), (384, 256)]:
+            nc.scalar.activation(first[:, t0:t0 + n], y[:].indirect(pos1_sb[:, columns(t0, n)]), COPY)
+        for pieces in ([(0, 128), (128, 256)], [(384, 256)]):
+            start = pieces[0][0]
+            width = sum(n for t0, n in pieces)
+            total = keep.tile([P, width], F32, name="total%d" % start)
+            for t0, n in pieces:
+                nc.vector.tensor_tensor(total[:, t0 - start:t0 - start + n],
+                                        y[:].indirect(pos2_sb[:, columns(t0, n)]), first[:, t0:t0 + n], ADD)
+            nc.sync.dma_start(out[:, start:start + width], total[:])

@@ -1,6 +1,7 @@
 from contextlib import ExitStack
 
 import concourse.mybir as mybir
+from concourse.masks import make_identity
 
 K, T, E, C, N = 1024, 640, 5, 256, 128
 S = E * C
@@ -26,10 +27,11 @@ BYTES = 4 * K * T + E * K * N + E * K * N // 32 + 4 * N * E + 4 * S + 2 * P * (S
 
 HALF = C // 2
 BANK = 512
-WIDE = 1024
-OWN0 = 512
-OWN1 = 128
-HELP = 256
+FUSED = 256
+POOLED = 512
+COPIED = S - FUSED - POOLED
+LEAD = 128
+BLOCKS = S // P
 RUN = 2
 
 
@@ -42,15 +44,20 @@ def tile_moe_pre_lin_gelu_kernel(tc, xT, w_words, w_scales, b, gate, offs, pos1,
         offs_sb = keep.tile([P, S // PER_COLUMN], U16, name="offs_sb")
         pos1_sb = keep.tile([P, T // PER_COLUMN], U16, name="pos1_sb")
         pos2_sb = keep.tile([P, T // PER_COLUMN], U16, name="pos2_sb")
-        gate_sb = keep.tile([P, S], F32, name="gate_sb")
         bias_sb = keep.tile([P, E], F32, name="bias_sb")
         w_codes = keep.tile([P, E * PASSES * N * PACK], U8, name="w_codes", align_bytes=64)
         w_plane = keep.tile([P, E * PASSES * N], U8, name="w_plane", align_bytes=64)
-        x_rows = [keep.tile([P, WIDE if i < PACK else T], F32, name="x_rows%d" % i) for i in range(PASSES * PACK)]
+        x_rows = [keep.tile([P, T], F32, name="x_rows%d" % i) for i in range(PASSES * PACK)]
         codes = keep.tile([P, PASSES * S], U32, name="codes", align_bytes=64)
-        plane = keep.tile([P, PASSES * S], U8, name="plane", align_bytes=64)
         y = keep.tile([P, S], F32, name="y")
-        banks = [psum.tile([P, BANK], F32, name="bank%d" % i) for i in range(E + 1)]
+        banks = [psum.tile([P, BANK], F32, name="bank%d" % i) for i in range(8)]
+        ident = keep.tile([P, P], F32, name="ident")
+        make_identity(nc, ident[:])
+        copied = keep.tile([P, PACK, COPIED], F32, name="copied")
+        gate_fused = copied[:].rearrange("p r n -> p (r n)")[:, 2 * COPIED - FUSED // 2:2 * COPIED + FUSED // 2]
+        gate_pooled = keep.tile([P, POOLED], F32, name="gate_pooled", tag="then_plane", align_bytes=64)
+        gate_rows = keep.tile([P, P], F32, name="gate_rows")
+        gate_col = keep.tile([P, BLOCKS], F32, name="gate_col")
 
         nc.vector.memset(w_plane[:].bitcast(I32), 0)
         warm = keep.tile([P, 1], F32, name="warm")
@@ -61,16 +68,14 @@ def tile_moe_pre_lin_gelu_kernel(tc, xT, w_words, w_scales, b, gate, offs, pos1,
         def load_x(i):
             nc.sync.dma_start(x_rows[i][:, 0:T], x_view[i // PACK, i % PACK])
 
-        def load_gate(s0, s1):
-            nc.sync.dma_start(gate_sb[:, s0:s1], gate[0:P, s0:s1])
-
         load_x(0)
         nc.sync.dma_start(offs_sb[:], offs)
-        load_gate(0, OWN0)
-        for i in range(1, PASSES * PACK - 1):
+        nc.sync.dma_start(gate_fused, gate[0:P, 0:FUSED])
+        load_x(1)
+        nc.sync.dma_start(gate_rows[:], gate.rearrange("k (m c) -> (k m) c", c=P)[0:P])
+        for i in range(2, PASSES * PACK):
             load_x(i)
-        load_gate(OWN0, S)
-        load_x(PASSES * PACK - 1)
+        nc.sync.dma_start(gate_pooled[:], gate[0:P, FUSED:FUSED + POOLED])
         w_to = w_codes[:].bitcast(I32).rearrange("p (g n) -> p g n", n=N)
         w_from = w_words.rearrange("e a p n r -> p (e a) (n r)").bitcast(I32)
         for g0 in range(0, E * PASSES, PASSES):
@@ -93,26 +98,27 @@ def tile_moe_pre_lin_gelu_kernel(tc, xT, w_words, w_scales, b, gate, offs, pos1,
         def by_runs(staged):
             return staged.rearrange("p r (c i) -> p c r i", i=RUN)
 
-        grouped = {}
+        def words(tile):
+            return tile.rearrange("p (c i) r -> p c r i", i=RUN)
 
-        def words(a, s0, n):
-            tile = keep.tile([P, n, PACK], BF16, name="grouped%d_%d" % (a, s0), align_bytes=64)
-            grouped[a, s0] = tile
-            return tile[:].rearrange("p (c i) r -> p c r i", i=RUN)
-
-        def gather_gated(staged, a, r, s0, n):
-            nc.vector.tensor_tensor(staged[:, r, :], picked(a, r, s0, n), gate_sb[:, s0:s0 + n], MULT)
+        def spread(weight, n):
+            return weight.rearrange("p (c i) -> p c i", i=RUN).unsqueeze(2).to_broadcast([P, n // RUN, PACK, RUN])
 
         def gather_plain(staged, a, s0, n):
             for r in range(PACK):
                 nc.scalar.activation(staged[:, r, :], picked(a, r, s0, n), COPY)
 
-        def lay(staged, a, s0, n):
-            nc.vector.tensor_copy(words(a, s0, n), by_runs(staged))
+        gate_banks = [(0, 384, banks[5]), (384, 384, banks[6]), (768, 512, banks[7])]
+        nc.tensor.transpose(banks[0][:, 0:P], gate_rows[:], ident[:])
+        nc.vector.tensor_copy(gate_col[:], banks[0][:, 0:BLOCKS])
+        for s0, n, bank in reversed(gate_banks):
+            for c in range(0, n, P):
+                m = (s0 + c) // P
+                nc.tensor.transpose(bank[:, c:c + P], gate_col[:, m:m + 1].to_broadcast([P, P]), ident[:])
 
-        def gate_and_lay(staged, a, s0, n):
-            weight = gate_sb[:, s0:s0 + n].rearrange("p (c i) -> p c i", i=RUN).unsqueeze(2)
-            nc.vector.tensor_tensor(words(a, s0, n), by_runs(staged), weight.to_broadcast([P, n // RUN, PACK, RUN]), MULT)
+        def gate_and_lay(tile, staged, s0, n):
+            b0, bank = [(b0, bank) for b0, width, bank in gate_banks if b0 <= s0 < b0 + width][0]
+            nc.vector.tensor_tensor(words(tile), by_runs(staged), spread(bank[:, s0 - b0:s0 - b0 + n], n), MULT)
 
         last = (E - 1) * C
         groups = [(e * C, C) for e in range(E - 1)] + [(last, HALF), (last + HALF, HALF)]
@@ -120,10 +126,10 @@ def tile_moe_pre_lin_gelu_kernel(tc, xT, w_words, w_scales, b, gate, offs, pos1,
         done = [set(), set()]
         issued = set()
 
-        def quantize(a, s0, n):
+        def quantize(tile, a, s0, n):
             c0 = a * S + s0
             nc.vector.quantize_mx(out=codes[:, c0:c0 + n].bitcast(FP8X4), scales=plane[:, c0:c0 + n],
-                                  in_=grouped[a, s0][:].rearrange("p n r -> p (n r)"))
+                                  in_=tile.rearrange("p n r -> p (n r)"))
             for h in range(s0, s0 + n, HALF):
                 done[a].add(h)
             for acc, (g0, m) in zip(accs, groups):
@@ -140,44 +146,52 @@ def tile_moe_pre_lin_gelu_kernel(tc, xT, w_words, w_scales, b, gate, offs, pos1,
                             rhs=codes[:, w0:w0 + m].bitcast(FP8X4), rhs_scale=plane[:, w0:w0 + m],
                             start=(pa == 0), stop=(pa == PASSES - 1))
 
-        rest = S - OWN0
-        third = rest // 2
-        own0 = keep.tile([P, PACK, OWN0], F32, name="own0")
-        own1 = keep.tile([P, PACK, OWN1], F32, name="own1")
-        early = keep.tile([P, PACK, rest], F32, name="early")
-        middle = keep.tile([P, PACK, 512], F32, name="middle")
+        def grouped(name, n, tag):
+            return keep.tile([P, n, PACK], BF16, name=name, tag=tag, align_bytes=64)
 
-        nc.vector.tensor_copy(early[:, 0, 0:HELP], picked(0, 0, OWN0, HELP))
-        nc.scalar.activation(early[:, 0, HELP:rest], picked(0, 0, OWN0 + HELP, rest - HELP), COPY)
-        for r in range(1, PACK):
-            nc.scalar.activation(early[:, r, :], picked(0, r, OWN0, rest), COPY)
+        fused = keep.tile([P, PACK, FUSED], F32, name="fused")
+        ring = keep.tile([P, PACK, 768], F32, name="ring")
+        second = keep.tile([P, PACK, 384], F32, name="second")
+        copied_from = FUSED + POOLED
+
+        nc.vector.tensor_copy(copied[:, 0, :], picked(0, 0, copied_from, COPIED))
         for r in range(PACK):
-            gather_gated(own0, 0, r, 0, OWN0)
-        gather_gated(own1, 1, 0, 0, OWN1)
-        lay(own0[:], 0, 0, OWN0)
-        gather_gated(own1, 1, 1, 0, OWN1)
-        quantize(0, 0, OWN0)
-        gather_gated(own1, 1, 2, 0, OWN1)
-        gather_plain(middle, 1, OWN1, 512)
-        gate_and_lay(early[:, :, 0:third], 0, OWN0, third)
-        gather_gated(own1, 1, 3, 0, OWN1)
-        gate_and_lay(early[:, :, third:rest], 0, OWN0 + third, third)
-        late = [(OWN1 + 512, third, 0), (last, HALF, third), (last + HALF, HALF, third + HALF)]
-        for s0, n, c0 in late:
-            gather_plain(early[:, :, c0:c0 + n], 1, s0, n)
-        lay(own1[:], 1, 0, OWN1)
-        quantize(0, OWN0, third)
-        quantize(0, OWN0 + third, third)
-        gate_and_lay(middle[:], 1, OWN1, 512)
-        quantize(1, 0, OWN1)
-        quantize(1, OWN1, 512)
-        before = None
-        for s0, n, c0 in late:
-            gate_and_lay(early[:, :, c0:c0 + n], 1, s0, n)
-            if before:
-                quantize(1, *before)
-            before = (s0, n)
-        quantize(1, *before)
+            nc.vector.tensor_tensor(fused[:, r, :], picked(0, r, 0, FUSED), gate_fused, MULT)
+        gather_plain(ring[:, :, 256:768], 0, FUSED, POOLED)
+        for r in range(1, PACK):
+            nc.vector.tensor_copy(copied[:, r, :], picked(0, r, copied_from, COPIED))
+        gather_plain(second, 1, 0, 384)
+        g_fused = grouped("g_fused", FUSED, "ga")
+        nc.gpsimd.tensor_scalar(g_fused[:], fused[:].rearrange("p r n -> p n r"), 1.0, 0.0, MULT, ADD)
+        g_pooled = grouped("g_pooled", POOLED, "gb")
+        for c0, n in [(0, LEAD), (LEAD, POOLED - LEAD)]:
+            nc.gpsimd.tensor_tensor(
+                g_pooled[:, c0:c0 + n, :], ring[:, :, 256 + c0:256 + c0 + n].rearrange("p r n -> p n r"),
+                gate_pooled[:, c0:c0 + n].unsqueeze(2).to_broadcast([P, n, PACK]), MULT)
+            if c0 == 0:
+                gather_plain(ring[:, :, 0:384], 1, 384, 384)
+        plane = keep.tile([P, PASSES * S], U8, name="plane", tag="then_plane", align_bytes=64)
+        g_copied = grouped("g_copied", COPIED, "gc")
+        gate_and_lay(g_copied[:], copied[:], copied_from, COPIED)
+        g_second = grouped("g_second", 384, "gd")
+        gate_and_lay(g_second[:], second[:], 0, 384)
+        gather_plain(ring[:, :, 384:640], 1, 768, 256)
+        gather_plain(ring[:, :, 640:768], 1, 1024, 128)
+        quantize(g_fused[:], 0, 0, FUSED)
+        quantize(g_pooled[:], 0, FUSED, POOLED)
+        quantize(g_copied[:], 0, copied_from, COPIED)
+        g_third = grouped("g_third", 384, "ga")
+        gate_and_lay(g_third[:], ring[:, :, 0:384], 384, 384)
+        gather_plain(ring[:, :, 0:128], 1, 1152, 128)
+        quantize(g_second[:], 1, 0, 384)
+        g_fourth = grouped("g_fourth", 384, "gb")
+        gate_and_lay(g_fourth[:, 0:256, :], ring[:, :, 384:640], 768, 256)
+        gate_and_lay(g_fourth[:, 256:384, :], ring[:, :, 640:768], 1024, 128)
+        quantize(g_third[:], 1, 384, 384)
+        g_last = grouped("g_last", 128, "ge")
+        gate_and_lay(g_last[:], ring[:, :, 0:128], 1152, 128)
+        quantize(g_fourth[:], 1, 768, 384)
+        quantize(g_last[:], 1, 1152, 128)
         for acc, (s0, m) in zip(accs, groups):
             e = s0 // C
             nc.scalar.activation(y[:, s0:s0 + m], acc, GELU, bias=bias_sb[:, e:e + 1])

@@ -29,16 +29,18 @@ HALF = C // 2
 BANK = 512
 FUSED = 256
 POOLED = 512
-COPIED = S - FUSED - POOLED
-LEAD = 128
+COPIED = 512
+HELP = 128
+LENT = 128
 BLOCKS = S // P
-RUN = 2
+RUN = 4
 
 
 def tile_moe_pre_lin_gelu_kernel(tc, xT, w_words, w_scales, b, gate, offs, pos1, pos2, out):
     nc = tc.nc
     with ExitStack() as ctx:
         keep = ctx.enter_context(tc.tile_pool(name="keep", bufs=1))
+        over = ctx.enter_context(tc.tile_pool(name="over", bufs=1))
         psum = ctx.enter_context(tc.psum_pool(name="psum", bufs=1))
 
         offs_sb = keep.tile([P, S // PER_COLUMN], U16, name="offs_sb")
@@ -53,9 +55,9 @@ def tile_moe_pre_lin_gelu_kernel(tc, xT, w_words, w_scales, b, gate, offs, pos1,
         banks = [psum.tile([P, BANK], F32, name="bank%d" % i) for i in range(8)]
         ident = keep.tile([P, P], F32, name="ident")
         make_identity(nc, ident[:])
-        copied = keep.tile([P, PACK, COPIED], F32, name="copied")
-        gate_fused = copied[:].rearrange("p r n -> p (r n)")[:, 2 * COPIED - FUSED // 2:2 * COPIED + FUSED // 2]
-        gate_pooled = keep.tile([P, POOLED], F32, name="gate_pooled", tag="then_plane", align_bytes=64)
+        gate_fused = keep.tile([P, FUSED], F32, name="gate_fused")
+        gate_lead = keep.tile([P, C], F32, name="gate_lead")
+        gate_end = keep.tile([P, C + LENT], F32, name="gate_end")
         gate_rows = keep.tile([P, P], F32, name="gate_rows")
         gate_col = keep.tile([P, BLOCKS], F32, name="gate_col")
 
@@ -70,12 +72,16 @@ def tile_moe_pre_lin_gelu_kernel(tc, xT, w_words, w_scales, b, gate, offs, pos1,
 
         load_x(0)
         nc.sync.dma_start(offs_sb[:], offs)
-        nc.sync.dma_start(gate_fused, gate[0:P, 0:FUSED])
+        nc.sync.dma_start(gate_fused[:], gate[0:P, 0:FUSED])
         load_x(1)
+        load_x(2)
         nc.sync.dma_start(gate_rows[:], gate.rearrange("k (m c) -> (k m) c", c=P)[0:P])
-        for i in range(2, PASSES * PACK):
+        load_x(3)
+        load_x(4)
+        nc.sync.dma_start(gate_lead[:], gate[0:P, C:2 * C])
+        for i in range(5, PASSES * PACK):
             load_x(i)
-        nc.sync.dma_start(gate_pooled[:], gate[0:P, FUSED:FUSED + POOLED])
+        nc.sync.dma_start(gate_end[:], gate[0:P, 2 * C:3 * C + LENT])
         w_to = w_codes[:].bitcast(I32).rearrange("p (g n) -> p g n", n=N)
         w_from = w_words.rearrange("e a p n r -> p (e a) (n r)").bitcast(I32)
         for g0 in range(0, E * PASSES, PASSES):
@@ -108,10 +114,10 @@ def tile_moe_pre_lin_gelu_kernel(tc, xT, w_words, w_scales, b, gate, offs, pos1,
             for r in range(PACK):
                 nc.scalar.activation(staged[:, r, :], picked(a, r, s0, n), COPY)
 
-        gate_banks = [(0, 384, banks[5]), (384, 384, banks[6]), (768, 512, banks[7])]
+        gate_banks = [(0, 512, banks[5]), (512, 256, banks[6]), (768, 512, banks[7])]
         nc.tensor.transpose(banks[0][:, 0:P], gate_rows[:], ident[:])
-        nc.vector.tensor_copy(gate_col[:], banks[0][:, 0:BLOCKS])
-        for s0, n, bank in reversed(gate_banks):
+        nc.scalar.copy(gate_col[:], banks[0][:, 0:BLOCKS])
+        for s0, n, bank in [gate_banks[0], gate_banks[2], gate_banks[1]]:
             for c in range(0, n, P):
                 m = (s0 + c) // P
                 nc.tensor.transpose(bank[:, c:c + P], gate_col[:, m:m + 1].to_broadcast([P, P]), ident[:])
@@ -149,49 +155,70 @@ def tile_moe_pre_lin_gelu_kernel(tc, xT, w_words, w_scales, b, gate, offs, pos1,
         def grouped(name, n, tag):
             return keep.tile([P, n, PACK], BF16, name=name, tag=tag, align_bytes=64)
 
-        fused = keep.tile([P, PACK, FUSED], F32, name="fused")
-        ring = keep.tile([P, PACK, 768], F32, name="ring")
-        second = keep.tile([P, PACK, 384], F32, name="second")
-        copied_from = FUSED + POOLED
+        second_from = FUSED + POOLED
+        kept_from = second_from + LENT
+        wide = S - second_from
+        kept = S - kept_from
 
-        nc.vector.tensor_copy(copied[:, 0, :], picked(0, 0, copied_from, COPIED))
+        def rows(tile, c0, pitch, n):
+            return tile[:, c0:c0 + PACK * pitch].rearrange("p (r n) -> p r n", r=PACK)[:, :, 0:n]
+
+        early = keep.tile([P, PACK * wide], F32, name="early", tag="then_plane", align_bytes=64)
+        fused = rows(early, wide // 2, FUSED, FUSED)
+        second = rows(early, 0, wide, wide)
+        pooled = keep.tile([P, PACK, POOLED], F32, name="pooled")
+        middle = kept * PACK * 2
+        copied_front = over.tile([P, PACK, HALF], F32, name="copied_front", offset=middle - PACK * HALF * 2)
+        copied_back = keep.tile([P, PACK, COPIED - HALF], F32, name="copied_back", tag="sb")
+
+        nc.vector.tensor_copy(pooled[:, 0, 0:HELP], picked(0, 0, FUSED, HELP))
         for r in range(PACK):
-            nc.vector.tensor_tensor(fused[:, r, :], picked(0, r, 0, FUSED), gate_fused, MULT)
-        gather_plain(ring[:, :, 256:768], 0, FUSED, POOLED)
+            nc.vector.tensor_tensor(fused[:, r, :], picked(0, r, 0, FUSED), gate_fused[:], MULT)
+        nc.scalar.activation(pooled[:, 0, HELP:POOLED], picked(0, 0, FUSED + HELP, POOLED - HELP), COPY)
         for r in range(1, PACK):
-            nc.vector.tensor_copy(copied[:, r, :], picked(0, r, copied_from, COPIED))
-        gather_plain(second, 1, 0, 384)
-        g_fused = grouped("g_fused", FUSED, "ga")
-        nc.gpsimd.tensor_scalar(g_fused[:], fused[:].rearrange("p r n -> p n r"), 1.0, 0.0, MULT, ADD)
-        g_pooled = grouped("g_pooled", POOLED, "gb")
-        for c0, n in [(0, LEAD), (LEAD, POOLED - LEAD)]:
+            nc.scalar.activation(pooled[:, r, :], picked(0, r, FUSED, POOLED), COPY)
+        for r in range(PACK):
+            nc.vector.tensor_copy(copied_front[:, r, :], picked(1, r, 0, HALF))
+            nc.vector.tensor_copy(copied_back[:, r, :], picked(1, r, HALF, COPIED - HALF))
+        laid0 = grouped("laid0", kept_from, "ga")
+        nc.gpsimd.tensor_scalar(laid0[:, 0:FUSED, :], fused.rearrange("p r n -> p n r"), 1.0, 0.0, MULT, ADD)
+
+        def pool_gate_and_lay(staged, weight, s0, n):
             nc.gpsimd.tensor_tensor(
-                g_pooled[:, c0:c0 + n, :], ring[:, :, 256 + c0:256 + c0 + n].rearrange("p r n -> p n r"),
-                gate_pooled[:, c0:c0 + n].unsqueeze(2).to_broadcast([P, n, PACK]), MULT)
-            if c0 == 0:
-                gather_plain(ring[:, :, 0:384], 1, 384, 384)
+                laid0[:, s0:s0 + n, :], staged.rearrange("p r n -> p n r"),
+                weight.unsqueeze(2).to_broadcast([P, n, PACK]), MULT)
+
+        gather_plain(second, 0, second_from, wide)
+        pool_gate_and_lay(pooled[:, :, 0:C], gate_lead[:], C, C)
+        pool_gate_and_lay(pooled[:, :, C:2 * C], gate_end[:, 0:C], 2 * C, C)
+        pool_gate_and_lay(second[:, :, 0:LENT], gate_end[:, C:C + LENT], second_from, LENT)
+        laid1 = grouped("laid1", 768, "gb")
+        gate_and_lay(laid1[:, 0:HALF, :], copied_front[:], 0, HALF)
+        third = over.tile([P, PACK, C], F32, name="third", offset=middle)
+        gather_plain(third, 1, 512, 256)
+        gate_and_lay(laid1[:, HALF:COPIED, :], copied_back[:], HALF, COPIED - HALF)
+        fourth = keep.tile([P, PACK, 320], F32, name="fourth", tag="sb")
+        gather_plain(fourth, 1, 768, 320)
+        laid_kept = over.tile([P, kept, PACK], BF16, name="laid_kept", offset=0, align_bytes=64)
+        gate_and_lay(laid_kept[:], second[:, :, LENT:wide], kept_from, kept)
+        gate_and_lay(laid1[:, 512:768, :], third[:], 512, 256)
+        fifth = over.tile([P, PACK, HALF], F32, name="fifth", offset=middle)
+        gather_plain(fifth, 1, 1088, 128)
         plane = keep.tile([P, PASSES * S], U8, name="plane", tag="then_plane", align_bytes=64)
-        g_copied = grouped("g_copied", COPIED, "gc")
-        gate_and_lay(g_copied[:], copied[:], copied_from, COPIED)
-        g_second = grouped("g_second", 384, "gd")
-        gate_and_lay(g_second[:], second[:], 0, 384)
-        gather_plain(ring[:, :, 384:640], 1, 768, 256)
-        gather_plain(ring[:, :, 640:768], 1, 1024, 128)
-        quantize(g_fused[:], 0, 0, FUSED)
-        quantize(g_pooled[:], 0, FUSED, POOLED)
-        quantize(g_copied[:], 0, copied_from, COPIED)
-        g_third = grouped("g_third", 384, "ga")
-        gate_and_lay(g_third[:], ring[:, :, 0:384], 384, 384)
-        gather_plain(ring[:, :, 0:128], 1, 1152, 128)
-        quantize(g_second[:], 1, 0, 384)
-        g_fourth = grouped("g_fourth", 384, "gb")
-        gate_and_lay(g_fourth[:, 0:256, :], ring[:, :, 384:640], 768, 256)
-        gate_and_lay(g_fourth[:, 256:384, :], ring[:, :, 640:768], 1024, 128)
-        quantize(g_third[:], 1, 384, 384)
-        g_last = grouped("g_last", 128, "ge")
-        gate_and_lay(g_last[:], ring[:, :, 0:128], 1152, 128)
-        quantize(g_fourth[:], 1, 768, 384)
-        quantize(g_last[:], 1, 1152, 128)
+        quantize(laid0[:, 0:512, :], 0, 0, 512)
+        quantize(laid0[:, 512:kept_from, :], 0, 512, kept_from - 512)
+        quantize(laid_kept[:], 0, kept_from, kept)
+        sixth = over.tile([P, PACK, 64], F32, name="sixth", offset=0)
+        gather_plain(sixth, 1, 1216, 64)
+        quantize(laid1[:, 0:512, :], 1, 0, 512)
+        laid2 = grouped("laid2", 512, "ga")
+        gate_and_lay(laid2[:, 0:320, :], fourth[:], 768, 320)
+        quantize(laid1[:, 512:768, :], 1, 512, 256)
+        gate_and_lay(laid2[:, 320:448, :], fifth[:], 1088, 128)
+        quantize(laid2[:, 0:256, :], 1, 768, 256)
+        gate_and_lay(laid2[:, 448:512, :], sixth[:], 1216, 64)
+        quantize(laid2[:, 256:384, :], 1, 1024, 128)
+        quantize(laid2[:, 384:512, :], 1, 1152, 128)
         for acc, (s0, m) in zip(accs, groups):
             e = s0 // C
             nc.scalar.activation(y[:, s0:s0 + m], acc, GELU, bias=bias_sb[:, e:e + 1])

@@ -33,7 +33,7 @@ COPIED = 512
 HELP = 128
 LENT = 128
 BLOCKS = S // P
-RUN = 4
+RUN = 2
 
 
 def tile_moe_pre_lin_gelu_kernel(tc, xT, w_words, w_scales, b, gate, offs, pos1, pos2, out):

@@ -27,13 +27,14 @@ BYTES = 4 * K * T + E * K * N + E * K * N // 32 + 4 * N * E + 4 * S + 2 * P * (S
 
 HALF = C // 2
 BANK = 512
-FUSED = 256
+FUSED = 320
 POOLED = 512
 COPIED = 512
 HELP = 128
 LENT = 128
 BLOCKS = S // P
 RUN = 2
+BOTH = 96
 
 
 def tile_moe_pre_lin_gelu_kernel(tc, xT, w_words, w_scales, b, gate, offs, pos1, pos2, out):
@@ -55,9 +56,10 @@ def tile_moe_pre_lin_gelu_kernel(tc, xT, w_words, w_scales, b, gate, offs, pos1,
         banks = [psum.tile([P, BANK], F32, name="bank%d" % i) for i in range(8)]
         ident = keep.tile([P, P], F32, name="ident")
         make_identity(nc, ident[:])
-        gate_fused = keep.tile([P, FUSED], F32, name="gate_fused")
+        gate_fused = keep.tile([P, FUSED], F32, name="gate_fused", tag="then_plane", align_bytes=64)
         gate_lead = keep.tile([P, C], F32, name="gate_lead")
         gate_end = keep.tile([P, C + LENT], F32, name="gate_end")
+        gate_late = keep.tile([P, S - 3 * C], F32, name="gate_late")
         gate_rows = keep.tile([P, P], F32, name="gate_rows")
         gate_col = keep.tile([P, BLOCKS], F32, name="gate_col")
 
@@ -78,10 +80,10 @@ def tile_moe_pre_lin_gelu_kernel(tc, xT, w_words, w_scales, b, gate, offs, pos1,
         nc.sync.dma_start(gate_rows[:], gate.rearrange("k (m c) -> (k m) c", c=P)[0:P])
         load_x(3)
         load_x(4)
-        nc.sync.dma_start(gate_lead[:], gate[0:P, C:2 * C])
+        nc.sync.dma_start(gate_lead[:], gate[0:P, FUSED:FUSED + C])
         for i in range(5, PASSES * PACK):
             load_x(i)
-        nc.sync.dma_start(gate_end[:], gate[0:P, 2 * C:3 * C + LENT])
+        nc.sync.dma_start(gate_end[:], gate[0:P, FUSED + C:FUSED + 2 * C + LENT])
         w_to = w_codes[:].bitcast(I32).rearrange("p (g n) -> p g n", n=N)
         w_from = w_words.rearrange("e a p n r -> p (e a) (n r)").bitcast(I32)
         for g0 in range(0, E * PASSES, PASSES):
@@ -91,6 +93,7 @@ def tile_moe_pre_lin_gelu_kernel(tc, xT, w_words, w_scales, b, gate, offs, pos1,
             nc.sync.dma_start(
                 w_plane[32 * q:32 * q + 4, :].bitcast(I32).rearrange("p (g n) -> p g n", g=E * PASSES),
                 scale_rows[4 * q:4 * q + 4])
+        nc.sync.dma_start(gate_late[:], gate[0:P, 3 * C:S])
         nc.sync.dma_start(bias_sb[:], b)
         nc.sync.dma_start(pos1_sb[:], pos1)
         nc.sync.dma_start(pos2_sb[:], pos2)
@@ -114,17 +117,27 @@ def tile_moe_pre_lin_gelu_kernel(tc, xT, w_words, w_scales, b, gate, offs, pos1,
             for r in range(PACK):
                 nc.scalar.activation(staged[:, r, :], picked(a, r, s0, n), COPY)
 
-        gate_banks = [(0, 512, banks[5]), (512, 256, banks[6]), (768, 512, banks[7])]
         nc.tensor.transpose(banks[0][:, 0:P], gate_rows[:], ident[:])
-        nc.scalar.copy(gate_col[:], banks[0][:, 0:BLOCKS])
-        for s0, n, bank in [gate_banks[0], gate_banks[2], gate_banks[1]]:
+        nc.vector.tensor_copy(gate_col[:], banks[0][:, 0:BLOCKS])
+        held = {}
+
+        def spread_gate(bank, s0, n):
+            held[bank] = (s0, n)
             for c in range(0, n, P):
                 m = (s0 + c) // P
-                nc.tensor.transpose(bank[:, c:c + P], gate_col[:, m:m + 1].to_broadcast([P, P]), ident[:])
+                nc.tensor.transpose(banks[bank][:, c:c + P], gate_col[:, m:m + 1].to_broadcast([P, P]), ident[:])
 
         def gate_and_lay(tile, staged, s0, n):
-            b0, bank = [(b0, bank) for b0, width, bank in gate_banks if b0 <= s0 < b0 + width][0]
-            nc.vector.tensor_tensor(words(tile), by_runs(staged), spread(bank[:, s0 - b0:s0 - b0 + n], n), MULT)
+            bank = [j for j, (b0, width) in held.items() if b0 <= s0 and s0 + n <= b0 + width][0]
+            c0 = s0 - held[bank][0]
+            nc.vector.tensor_tensor(words(tile), by_runs(staged), spread(banks[bank][:, c0:c0 + n], n), MULT)
+
+        spread_gate(7, 0, HALF)
+        spread_gate(5, HALF, COPIED - HALF)
+        spread_gate(6, COPIED, C)
+
+        def gate_and_lay_late(tile, staged, s0, n):
+            nc.vector.tensor_tensor(words(tile), by_runs(staged), spread(gate_late[:, s0 - 3 * C:s0 - 3 * C + n], n), MULT)
 
         last = (E - 1) * C
         groups = [(e * C, C) for e in range(E - 1)] + [(last, HALF), (last + HALF, HALF)]
@@ -156,20 +169,15 @@ def tile_moe_pre_lin_gelu_kernel(tc, xT, w_words, w_scales, b, gate, offs, pos1,
             return keep.tile([P, n, PACK], BF16, name=name, tag=tag, align_bytes=64)
 
         second_from = FUSED + POOLED
-        kept_from = second_from + LENT
+        kept_from = 896
+        lent_to = second_from + LENT
         wide = S - second_from
         kept = S - kept_from
 
-        def rows(tile, c0, pitch, n):
-            return tile[:, c0:c0 + PACK * pitch].rearrange("p (r n) -> p r n", r=PACK)[:, :, 0:n]
-
-        early = keep.tile([P, PACK * wide], F32, name="early", tag="then_plane", align_bytes=64)
-        fused = rows(early, wide // 2, FUSED, FUSED)
-        second = rows(early, 0, wide, wide)
+        fused = keep.tile([P, PACK, FUSED], F32, name="fused")
         pooled = keep.tile([P, PACK, POOLED], F32, name="pooled")
-        middle = kept * PACK * 2
-        copied_front = over.tile([P, PACK, HALF], F32, name="copied_front", offset=middle - PACK * HALF * 2)
-        copied_back = keep.tile([P, PACK, COPIED - HALF], F32, name="copied_back", tag="sb")
+        laid_kept = grouped("laid_kept", kept, "gc")
+        copied = keep.tile([P, PACK, COPIED], F32, name="copied", tag="sb")
 
         nc.vector.tensor_copy(pooled[:, 0, 0:HELP], picked(0, 0, FUSED, HELP))
         for r in range(PACK):
@@ -178,45 +186,45 @@ def tile_moe_pre_lin_gelu_kernel(tc, xT, w_words, w_scales, b, gate, offs, pos1,
         for r in range(1, PACK):
             nc.scalar.activation(pooled[:, r, :], picked(0, r, FUSED, POOLED), COPY)
         for r in range(PACK):
-            nc.vector.tensor_copy(copied_front[:, r, :], picked(1, r, 0, HALF))
-            nc.vector.tensor_copy(copied_back[:, r, :], picked(1, r, HALF, COPIED - HALF))
+            nc.vector.tensor_copy(copied[:, r, :], picked(1, r, 0, COPIED))
         laid0 = grouped("laid0", kept_from, "ga")
-        nc.gpsimd.tensor_scalar(laid0[:, 0:FUSED, :], fused.rearrange("p r n -> p n r"), 1.0, 0.0, MULT, ADD)
+        nc.gpsimd.tensor_scalar(laid0[:, 0:FUSED, :], fused[:].rearrange("p r n -> p n r"), 1.0, 0.0, MULT, ADD)
 
         def pool_gate_and_lay(staged, weight, s0, n):
             nc.gpsimd.tensor_tensor(
-                laid0[:, s0:s0 + n, :], staged.rearrange("p r n -> p n r"),
+                laid0[:, s0:s0 + n, :] if s0 < kept_from else laid_kept[:, s0 - kept_from:s0 - kept_from + n, :], staged.rearrange("p r n -> p n r"),
                 weight.unsqueeze(2).to_broadcast([P, n, PACK]), MULT)
 
+        second = keep.tile([P, PACK, wide], F32, name="second", tag="then_plane", align_bytes=64)
         gather_plain(second, 0, second_from, wide)
-        pool_gate_and_lay(pooled[:, :, 0:C], gate_lead[:], C, C)
-        pool_gate_and_lay(pooled[:, :, C:2 * C], gate_end[:, 0:C], 2 * C, C)
-        pool_gate_and_lay(second[:, :, 0:LENT], gate_end[:, C:C + LENT], second_from, LENT)
+        pool_gate_and_lay(pooled[:, :, 0:C], gate_lead[:], FUSED, C)
+        pool_gate_and_lay(pooled[:, :, C:2 * C], gate_end[:, 0:C], FUSED + C, C)
+        inside = kept_from - second_from
+        pool_gate_and_lay(second[:, :, 0:inside], gate_end[:, C:C + inside], second_from, inside)
+        pool_gate_and_lay(second[:, :, inside:LENT], gate_end[:, C + inside:C + LENT], kept_from, LENT - inside)
         laid1 = grouped("laid1", 768, "gb")
-        gate_and_lay(laid1[:, 0:HALF, :], copied_front[:], 0, HALF)
-        third = over.tile([P, PACK, C], F32, name="third", offset=middle)
+        gate_and_lay(laid1[:, 0:HALF, :], copied[:, :, 0:HALF], 0, HALF)
+        spread_gate(7, kept_from, kept)
+        third = over.tile([P, PACK, C], F32, name="third", offset=0)
         gather_plain(third, 1, 512, 256)
-        gate_and_lay(laid1[:, HALF:COPIED, :], copied_back[:], HALF, COPIED - HALF)
-        fourth = keep.tile([P, PACK, 320], F32, name="fourth", tag="sb")
-        gather_plain(fourth, 1, 768, 320)
-        laid_kept = over.tile([P, kept, PACK], BF16, name="laid_kept", offset=0, align_bytes=64)
-        gate_and_lay(laid_kept[:], second[:, :, LENT:wide], kept_from, kept)
+        gate_and_lay(laid1[:, HALF:COPIED, :], copied[:, :, HALF:COPIED], HALF, COPIED - HALF)
+        gate_and_lay(laid_kept[:, lent_to - kept_from:, :], second[:, :, LENT:wide], lent_to, S - lent_to)
+        fourth = keep.tile([P, PACK, 384], F32, name="fourth", tag="sb")
+        gather_plain(fourth, 1, 768, 384)
         gate_and_lay(laid1[:, 512:768, :], third[:], 512, 256)
-        fifth = over.tile([P, PACK, HALF], F32, name="fifth", offset=middle)
-        gather_plain(fifth, 1, 1088, 128)
+        fifth = over.tile([P, PACK, HALF], F32, name="fifth", offset=0)
+        gather_plain(fifth, 1, 1152, 128)
         plane = keep.tile([P, PASSES * S], U8, name="plane", tag="then_plane", align_bytes=64)
         quantize(laid0[:, 0:512, :], 0, 0, 512)
         quantize(laid0[:, 512:kept_from, :], 0, 512, kept_from - 512)
         quantize(laid_kept[:], 0, kept_from, kept)
-        sixth = over.tile([P, PACK, 64], F32, name="sixth", offset=0)
-        gather_plain(sixth, 1, 1216, 64)
         quantize(laid1[:, 0:512, :], 1, 0, 512)
         laid2 = grouped("laid2", 512, "ga")
-        gate_and_lay(laid2[:, 0:320, :], fourth[:], 768, 320)
         quantize(laid1[:, 512:768, :], 1, 512, 256)
-        gate_and_lay(laid2[:, 320:448, :], fifth[:], 1088, 128)
+        gate_and_lay_late(laid2[:, 0:256, :], fourth[:, :, 0:256], 768, 256)
+        gate_and_lay_late(laid2[:, 256:384, :], fourth[:, :, 256:384], 1024, 128)
         quantize(laid2[:, 0:256, :], 1, 768, 256)
-        gate_and_lay(laid2[:, 448:512, :], sixth[:], 1216, 64)
+        gate_and_lay_late(laid2[:, 384:512, :], fifth[:], 1152, 128)
         quantize(laid2[:, 256:384, :], 1, 1024, 128)
         quantize(laid2[:, 384:512, :], 1, 1152, 128)
         for acc, (s0, m) in zip(accs, groups):
@@ -224,14 +232,21 @@ def tile_moe_pre_lin_gelu_kernel(tc, xT, w_words, w_scales, b, gate, offs, pos1,
             nc.scalar.activation(y[:, s0:s0 + m], acc, GELU, bias=bias_sb[:, e:e + 1])
 
         first = keep.tile([P, T], F32, name="first")
-        nc.vector.tensor_copy(first[:, 128:256], y[:].indirect(pos1_sb[:, columns(128, 128)]))
-        for t0, n in [(0, 128), (256, 128), (384, 256)]:
-            nc.scalar.activation(first[:, t0:t0 + n], y[:].indirect(pos1_sb[:, columns(t0, n)]), COPY)
-        for pieces in ([(0, 128), (128, 256)], [(384, 256)]):
-            start = pieces[0][0]
-            width = sum(n for t0, n in pieces)
-            total = keep.tile([P, width], F32, name="total%d" % start)
-            for t0, n in pieces:
-                nc.vector.tensor_tensor(total[:, t0 - start:t0 - start + n],
-                                        y[:].indirect(pos2_sb[:, columns(t0, n)]), first[:, t0:t0 + n], ADD)
-            nc.sync.dma_start(out[:, start:start + width], total[:])
+        both_from = T - BOTH
+        other = keep.tile([P, BOTH], F32, name="other")
+
+        def results(pos_sb, t0, t1):
+            return y[:].indirect(pos_sb[:, columns(t0, t1 - t0)])
+
+        nc.vector.tensor_copy(first[:, 96:224], results(pos1_sb, 96, 224))
+        for t0, t1 in [(0, 96), (224, 352), (352, both_from), (both_from, T)]:
+            nc.scalar.activation(first[:, t0:t1], results(pos1_sb, t0, t1), COPY)
+        nc.scalar.activation(other[:], results(pos2_sb, both_from, T), COPY)
+        front = keep.tile([P, 352], F32, name="front")
+        back = keep.tile([P, T - 352], F32, name="back")
+        for t0, t1 in [(0, 96), (96, 352)]:
+            nc.vector.tensor_tensor(front[:, t0:t1], results(pos2_sb, t0, t1), first[:, t0:t1], ADD)
+        nc.sync.dma_start(out[:, 0:352], front[:])
+        nc.vector.tensor_tensor(back[:, 0:both_from - 352], results(pos2_sb, 352, both_from), first[:, 352:both_from], ADD)
+        nc.vector.tensor_tensor(back[:, both_from - 352:], other[:], first[:, both_from:T], ADD)
+        nc.sync.dma_start(out[:, 352:T], back[:])

@@ -59,7 +59,7 @@ def tile_moe_pre_lin_gelu_kernel(tc, xT, w_words, w_scales, b, gate, offs, pos1,
         gate_fused = keep.tile([P, FUSED], F32, name="gate_fused", tag="then_plane", align_bytes=64)
         gate_lead = keep.tile([P, C], F32, name="gate_lead")
         gate_end = keep.tile([P, C + LENT], F32, name="gate_end")
-        gate_late = keep.tile([P, S - 3 * C], F32, name="gate_late")
+        gate_late = keep.tile([P, HALF], F32, name="gate_late")
         gate_rows = keep.tile([P, P], F32, name="gate_rows")
         gate_col = keep.tile([P, BLOCKS], F32, name="gate_col")
 
@@ -93,7 +93,7 @@ def tile_moe_pre_lin_gelu_kernel(tc, xT, w_words, w_scales, b, gate, offs, pos1,
             nc.sync.dma_start(
                 w_plane[32 * q:32 * q + 4, :].bitcast(I32).rearrange("p (g n) -> p g n", g=E * PASSES),
                 scale_rows[4 * q:4 * q + 4])
-        nc.sync.dma_start(gate_late[:], gate[0:P, 3 * C:S])
+        nc.sync.dma_start(gate_late[:], gate[0:P, 4 * C:4 * C + HALF])
         nc.sync.dma_start(bias_sb[:], b)
         nc.sync.dma_start(pos1_sb[:], pos1)
         nc.sync.dma_start(pos2_sb[:], pos2)
@@ -134,13 +134,10 @@ def tile_moe_pre_lin_gelu_kernel(tc, xT, w_words, w_scales, b, gate, offs, pos1,
 
         spread_gate(7, 0, HALF)
         spread_gate(5, HALF, COPIED - HALF)
-        spread_gate(6, COPIED, C)
-
-        def gate_and_lay_late(tile, staged, s0, n):
-            nc.vector.tensor_tensor(words(tile), by_runs(staged), spread(gate_late[:, s0 - 3 * C:s0 - 3 * C + n], n), MULT)
+        spread_gate(6, COPIED, 2 * C)
 
         last = (E - 1) * C
-        groups = [(e * C, C) for e in range(E - 1)] + [(last, HALF), (last + HALF, HALF)]
+        groups = [(e * C, C) for e in range(E - 1)] + [(last + HALF, HALF), (last, HALF)]
         accs = [banks[j][:, 0:n] for j, (s0, n) in enumerate(groups)]
         done = [set(), set()]
         issued = set()
@@ -190,18 +187,18 @@ def tile_moe_pre_lin_gelu_kernel(tc, xT, w_words, w_scales, b, gate, offs, pos1,
         laid0 = grouped("laid0", kept_from, "ga")
         nc.gpsimd.tensor_scalar(laid0[:, 0:FUSED, :], fused[:].rearrange("p r n -> p n r"), 1.0, 0.0, MULT, ADD)
 
-        def pool_gate_and_lay(staged, weight, s0, n):
+        def pool_gate_and_lay(tile, staged, weight, n):
             nc.gpsimd.tensor_tensor(
-                laid0[:, s0:s0 + n, :] if s0 < kept_from else laid_kept[:, s0 - kept_from:s0 - kept_from + n, :], staged.rearrange("p r n -> p n r"),
+                tile, staged.rearrange("p r n -> p n r"),
                 weight.unsqueeze(2).to_broadcast([P, n, PACK]), MULT)
 
         second = keep.tile([P, PACK, wide], F32, name="second", tag="then_plane", align_bytes=64)
         gather_plain(second, 0, second_from, wide)
-        pool_gate_and_lay(pooled[:, :, 0:C], gate_lead[:], FUSED, C)
-        pool_gate_and_lay(pooled[:, :, C:2 * C], gate_end[:, 0:C], FUSED + C, C)
+        pool_gate_and_lay(laid0[:, FUSED:FUSED + C, :], pooled[:, :, 0:C], gate_lead[:], C)
+        pool_gate_and_lay(laid0[:, FUSED + C:second_from, :], pooled[:, :, C:2 * C], gate_end[:, 0:C], C)
         inside = kept_from - second_from
-        pool_gate_and_lay(second[:, :, 0:inside], gate_end[:, C:C + inside], second_from, inside)
-        pool_gate_and_lay(second[:, :, inside:LENT], gate_end[:, C + inside:C + LENT], kept_from, LENT - inside)
+        pool_gate_and_lay(laid0[:, second_from:kept_from, :], second[:, :, 0:inside], gate_end[:, C:C + inside], inside)
+        pool_gate_and_lay(laid_kept[:, 0:LENT - inside, :], second[:, :, inside:LENT], gate_end[:, C + inside:C + LENT], LENT - inside)
         laid1 = grouped("laid1", 768, "gb")
         gate_and_lay(laid1[:, 0:HALF, :], copied[:, :, 0:HALF], 0, HALF)
         spread_gate(7, kept_from, kept)
@@ -219,14 +216,15 @@ def tile_moe_pre_lin_gelu_kernel(tc, xT, w_words, w_scales, b, gate, offs, pos1,
         quantize(laid0[:, 512:kept_from, :], 0, 512, kept_from - 512)
         quantize(laid_kept[:], 0, kept_from, kept)
         quantize(laid1[:, 0:512, :], 1, 0, 512)
-        laid2 = grouped("laid2", 512, "ga")
         quantize(laid1[:, 512:768, :], 1, 512, 256)
-        gate_and_lay_late(laid2[:, 0:256, :], fourth[:, :, 0:256], 768, 256)
-        gate_and_lay_late(laid2[:, 256:384, :], fourth[:, :, 256:384], 1024, 128)
-        quantize(laid2[:, 0:256, :], 1, 768, 256)
-        gate_and_lay_late(laid2[:, 384:512, :], fifth[:], 1152, 128)
-        quantize(laid2[:, 256:384, :], 1, 1024, 128)
-        quantize(laid2[:, 384:512, :], 1, 1152, 128)
+        laid2 = grouped("laid2", C + HALF, "ga")
+        laid3 = grouped("laid3", HALF, "gb")
+        gate_and_lay(laid2[:, 0:C, :], fourth[:, :, 0:C], 768, C)
+        pool_gate_and_lay(laid3[:], fourth[:, :, C:C + HALF], gate_late[:], HALF)
+        gate_and_lay(laid2[:, C:C + HALF, :], fifth[:], 1152, HALF)
+        quantize(laid2[:, 0:C, :], 1, 768, C)
+        quantize(laid2[:, C:C + HALF, :], 1, 1152, HALF)
+        quantize(laid3[:], 1, 1024, HALF)
         for acc, (s0, m) in zip(accs, groups):
             e = s0 // C
             nc.scalar.activation(y[:, s0:s0 + m], acc, GELU, bias=bias_sb[:, e:e + 1])

@@ -32,6 +32,7 @@ POOLED = 512
 COPIED = 512
 HELP = 128
 LENT = 128
+LATE = 96
 BLOCKS = S // P
 RUN = 2
 BOTH = 96
@@ -59,7 +60,7 @@ def tile_moe_pre_lin_gelu_kernel(tc, xT, w_words, w_scales, b, gate, offs, pos1,
         gate_fused = keep.tile([P, FUSED], F32, name="gate_fused", tag="then_plane", align_bytes=64)
         gate_lead = keep.tile([P, C], F32, name="gate_lead")
         gate_end = keep.tile([P, C + LENT], F32, name="gate_end")
-        gate_late = keep.tile([P, HALF], F32, name="gate_late")
+        gate_late = keep.tile([P, LATE], F32, name="gate_late")
         gate_rows = keep.tile([P, P], F32, name="gate_rows")
         gate_col = keep.tile([P, BLOCKS], F32, name="gate_col")
 
@@ -93,7 +94,7 @@ def tile_moe_pre_lin_gelu_kernel(tc, xT, w_words, w_scales, b, gate, offs, pos1,
             nc.sync.dma_start(
                 w_plane[32 * q:32 * q + 4, :].bitcast(I32).rearrange("p (g n) -> p g n", g=E * PASSES),
                 scale_rows[4 * q:4 * q + 4])
-        nc.sync.dma_start(gate_late[:], gate[0:P, 4 * C:4 * C + HALF])
+        nc.sync.dma_start(gate_late[:], gate[0:P, S - HALF - LATE:S - HALF])
         nc.sync.dma_start(bias_sb[:], b)
         nc.sync.dma_start(pos1_sb[:], pos1)
         nc.sync.dma_start(pos2_sb[:], pos2)
@@ -134,10 +135,9 @@ def tile_moe_pre_lin_gelu_kernel(tc, xT, w_words, w_scales, b, gate, offs, pos1,
 
         spread_gate(7, 0, HALF)
         spread_gate(5, HALF, COPIED - HALF)
-        spread_gate(6, COPIED, 2 * C)
+        spread_gate(6, COPIED, C)
 
-        last = (E - 1) * C
-        groups = [(e * C, C) for e in range(E - 1)] + [(last + HALF, HALF), (last, HALF)]
+        groups = [(e * C, C) for e in range(3)] + [(s0, HALF) for s0 in range(3 * C, S, HALF)]
         accs = [banks[j][:, 0:n] for j, (s0, n) in enumerate(groups)]
         done = [set(), set()]
         issued = set()
@@ -201,7 +201,7 @@ def tile_moe_pre_lin_gelu_kernel(tc, xT, w_words, w_scales, b, gate, offs, pos1,
         pool_gate_and_lay(laid_kept[:, 0:LENT - inside, :], second[:, :, inside:LENT], gate_end[:, C + inside:C + LENT], LENT - inside)
         laid1 = grouped("laid1", 768, "gb")
         gate_and_lay(laid1[:, 0:HALF, :], copied[:, :, 0:HALF], 0, HALF)
-        spread_gate(7, kept_from, kept)
+        spread_gate(7, 3 * C, 2 * C)
         third = over.tile([P, PACK, C], F32, name="third", offset=0)
         gather_plain(third, 1, 512, 256)
         gate_and_lay(laid1[:, HALF:COPIED, :], copied[:, :, HALF:COPIED], HALF, COPIED - HALF)
@@ -217,14 +217,15 @@ def tile_moe_pre_lin_gelu_kernel(tc, xT, w_words, w_scales, b, gate, offs, pos1,
         quantize(laid_kept[:], 0, kept_from, kept)
         quantize(laid1[:, 0:512, :], 1, 0, 512)
         quantize(laid1[:, 512:768, :], 1, 512, 256)
-        laid2 = grouped("laid2", C + HALF, "ga")
-        laid3 = grouped("laid3", HALF, "gb")
-        gate_and_lay(laid2[:, 0:C, :], fourth[:, :, 0:C], 768, C)
-        pool_gate_and_lay(laid3[:], fourth[:, :, C:C + HALF], gate_late[:], HALF)
-        gate_and_lay(laid2[:, C:C + HALF, :], fifth[:], 1152, HALF)
-        quantize(laid2[:, 0:C, :], 1, 768, C)
-        quantize(laid2[:, C:C + HALF, :], 1, 1152, HALF)
-        quantize(laid3[:], 1, 1024, HALF)
+        own = 384 - LATE
+        laid2 = laid1[:, 512 - own:512 + LATE, :]
+        laid3 = grouped("laid3", HALF, "ga")
+        gate_and_lay(laid2[:, 0:own, :], fourth[:, :, 0:own], 768, own)
+        pool_gate_and_lay(laid2[:, own:384, :], fourth[:, :, own:384], gate_late[:], LATE)
+        gate_and_lay(laid3[:], fifth[:], 1152, HALF)
+        for c0 in range(0, 384, HALF):
+            quantize(laid2[:, c0:c0 + HALF, :], 1, 768 + c0, HALF)
+        quantize(laid3[:], 1, 1152, HALF)
         for acc, (s0, m) in zip(accs, groups):
             e = s0 // C
             nc.scalar.activation(y[:, s0:s0 + m], acc, GELU, bias=bias_sb[:, e:e + 1])

@@ -32,7 +32,7 @@ POOLED = 512
 COPIED = 512
 HELP = 128
 LENT = 128
-LATE = 96
+LATE = 128
 BLOCKS = S // P
 RUN = 2
 BOTH = 96
@@ -210,13 +210,15 @@ def tile_moe_pre_lin_gelu_kernel(tc, xT, w_words, w_scales, b, gate, offs, pos1,
         gather_plain(fourth, 1, 768, 384)
         gate_and_lay(laid1[:, 512:768, :], third[:], 512, 256)
         fifth = over.tile([P, PACK, HALF], F32, name="fifth", offset=0)
-        gather_plain(fifth, 1, 1152, 128)
+        for r in range(1, PACK):
+            nc.scalar.activation(fifth[:, r, :], picked(1, r, S - HALF, HALF), COPY)
         plane = keep.tile([P, PASSES * S], U8, name="plane", tag="then_plane", align_bytes=64)
         quantize(laid0[:, 0:512, :], 0, 0, 512)
         quantize(laid0[:, 512:kept_from, :], 0, 512, kept_from - 512)
         quantize(laid_kept[:], 0, kept_from, kept)
         quantize(laid1[:, 0:512, :], 1, 0, 512)
         quantize(laid1[:, 512:768, :], 1, 512, 256)
+        nc.vector.tensor_copy(fifth[:, 0, :], picked(1, 0, S - HALF, HALF))
         own = 384 - LATE
         laid2 = laid1[:, 512 - own:512 + LATE, :]
         laid3 = grouped("laid3", HALF, "ga")

@@ -33,9 +33,10 @@ COPIED = 512
 HELP = 128
 LENT = 128
 LATE = 128
+LAST = 128
 BLOCKS = S // P
 RUN = 2
-BOTH = 96
+BOTH = 64
 
 
 def tile_moe_pre_lin_gelu_kernel(tc, xT, w_words, w_scales, b, gate, offs, pos1, pos2, out):
@@ -94,7 +95,7 @@ def tile_moe_pre_lin_gelu_kernel(tc, xT, w_words, w_scales, b, gate, offs, pos1,
             nc.sync.dma_start(
                 w_plane[32 * q:32 * q + 4, :].bitcast(I32).rearrange("p (g n) -> p g n", g=E * PASSES),
                 scale_rows[4 * q:4 * q + 4])
-        nc.sync.dma_start(gate_late[:], gate[0:P, S - HALF - LATE:S - HALF])
+        nc.sync.dma_start(gate_late[:], gate[0:P, S - LAST - LATE:S - LAST])
         nc.sync.dma_start(bias_sb[:], b)
         nc.sync.dma_start(pos1_sb[:], pos1)
         nc.sync.dma_start(pos2_sb[:], pos2)
@@ -162,18 +163,15 @@ def tile_moe_pre_lin_gelu_kernel(tc, xT, w_words, w_scales, b, gate, offs, pos1,
                             rhs=codes[:, w0:w0 + m].bitcast(FP8X4), rhs_scale=plane[:, w0:w0 + m],
                             start=(pa == 0), stop=(pa == PASSES - 1))
 
-        def grouped(name, n, tag):
-            return keep.tile([P, n, PACK], BF16, name=name, tag=tag, align_bytes=64)
+        def grouped(name, n):
+            return keep.tile([P, n, PACK], BF16, name=name, align_bytes=64)
 
         second_from = FUSED + POOLED
-        kept_from = 896
         lent_to = second_from + LENT
         wide = S - second_from
-        kept = S - kept_from
 
         fused = keep.tile([P, PACK, FUSED], F32, name="fused")
         pooled = keep.tile([P, PACK, POOLED], F32, name="pooled")
-        laid_kept = grouped("laid_kept", kept, "gc")
         copied = keep.tile([P, PACK, COPIED], F32, name="copied", tag="sb")
 
         nc.vector.tensor_copy(pooled[:, 0, 0:HELP], picked(0, 0, FUSED, HELP))
@@ -184,7 +182,7 @@ def tile_moe_pre_lin_gelu_kernel(tc, xT, w_words, w_scales, b, gate, offs, pos1,
             nc.scalar.activation(pooled[:, r, :], picked(0, r, FUSED, POOLED), COPY)
         for r in range(PACK):
             nc.vector.tensor_copy(copied[:, r, :], picked(1, r, 0, COPIED))
-        laid0 = grouped("laid0", kept_from, "ga")
+        laid0 = grouped("laid0", S)
         nc.gpsimd.tensor_scalar(laid0[:, 0:FUSED, :], fused[:].rearrange("p r n -> p n r"), 1.0, 0.0, MULT, ADD)
 
         def pool_gate_and_lay(tile, staged, weight, n):
@@ -196,38 +194,33 @@ def tile_moe_pre_lin_gelu_kernel(tc, xT, w_words, w_scales, b, gate, offs, pos1,
         gather_plain(second, 0, second_from, wide)
         pool_gate_and_lay(laid0[:, FUSED:FUSED + C, :], pooled[:, :, 0:C], gate_lead[:], C)
         pool_gate_and_lay(laid0[:, FUSED + C:second_from, :], pooled[:, :, C:2 * C], gate_end[:, 0:C], C)
-        inside = kept_from - second_from
-        pool_gate_and_lay(laid0[:, second_from:kept_from, :], second[:, :, 0:inside], gate_end[:, C:C + inside], inside)
-        pool_gate_and_lay(laid_kept[:, 0:LENT - inside, :], second[:, :, inside:LENT], gate_end[:, C + inside:C + LENT], LENT - inside)
-        laid1 = grouped("laid1", 768, "gb")
+        pool_gate_and_lay(laid0[:, second_from:lent_to, :], second[:, :, 0:LENT], gate_end[:, C:C + LENT], LENT)
+        laid1 = grouped("laid1", 768)
         gate_and_lay(laid1[:, 0:HALF, :], copied[:, :, 0:HALF], 0, HALF)
         spread_gate(7, 3 * C, 2 * C)
         third = over.tile([P, PACK, C], F32, name="third", offset=0)
         gather_plain(third, 1, 512, 256)
         gate_and_lay(laid1[:, HALF:COPIED, :], copied[:, :, HALF:COPIED], HALF, COPIED - HALF)
-        gate_and_lay(laid_kept[:, lent_to - kept_from:, :], second[:, :, LENT:wide], lent_to, S - lent_to)
-        fourth = keep.tile([P, PACK, 384], F32, name="fourth", tag="sb")
-        gather_plain(fourth, 1, 768, 384)
+        gate_and_lay(laid0[:, lent_to:S, :], second[:, :, LENT:wide], lent_to, S - lent_to)
+        fourth = keep.tile([P, PACK, 2 * C - LAST], F32, name="fourth", tag="sb")
+        gather_plain(fourth, 1, 768, 2 * C - LAST)
         gate_and_lay(laid1[:, 512:768, :], third[:], 512, 256)
-        fifth = over.tile([P, PACK, HALF], F32, name="fifth", offset=0)
+        fifth = over.tile([P, PACK, LAST], F32, name="fifth", offset=0)
         for r in range(1, PACK):
-            nc.scalar.activation(fifth[:, r, :], picked(1, r, S - HALF, HALF), COPY)
+            nc.scalar.activation(fifth[:, r, :], picked(1, r, S - LAST, LAST), COPY)
         plane = keep.tile([P, PASSES * S], U8, name="plane", tag="then_plane", align_bytes=64)
-        quantize(laid0[:, 0:512, :], 0, 0, 512)
-        quantize(laid0[:, 512:kept_from, :], 0, 512, kept_from - 512)
-        quantize(laid_kept[:], 0, kept_from, kept)
+        quantize(laid0[:, 0:1024, :], 0, 0, 1024)
+        quantize(laid0[:, 1024:S, :], 0, 1024, C)
         quantize(laid1[:, 0:512, :], 1, 0, 512)
         quantize(laid1[:, 512:768, :], 1, 512, 256)
-        nc.vector.tensor_copy(fifth[:, 0, :], picked(1, 0, S - HALF, HALF))
-        own = 384 - LATE
-        laid2 = laid1[:, 512 - own:512 + LATE, :]
-        laid3 = grouped("laid3", HALF, "ga")
+        nc.vector.tensor_copy(fifth[:, 0, :], picked(1, 0, S - LAST, LAST))
+        own = 2 * C - LAST - LATE
+        laid2 = laid1[:, 512 - own:1024 - own, :]
         gate_and_lay(laid2[:, 0:own, :], fourth[:, :, 0:own], 768, own)
-        pool_gate_and_lay(laid2[:, own:384, :], fourth[:, :, own:384], gate_late[:], LATE)
-        gate_and_lay(laid3[:], fifth[:], 1152, HALF)
-        for c0 in range(0, 384, HALF):
+        pool_gate_and_lay(laid2[:, own:own + LATE, :], fourth[:, :, own:own + LATE], gate_late[:], LATE)
+        gate_and_lay(laid2[:, own + LATE:2 * C, :], fifth[:], S - LAST, LAST)
+        for c0 in range(0, 2 * C, HALF):
             quantize(laid2[:, c0:c0 + HALF, :], 1, 768 + c0, HALF)
-        quantize(laid3[:], 1, 1152, HALF)
         for acc, (s0, m) in zip(accs, groups):
             e = s0 // C
             nc.scalar.activation(y[:, s0:s0 + m], acc, GELU, bias=bias_sb[:, e:e + 1])

@@ -30,7 +30,7 @@ BANK = 512
 FUSED = 320
 POOLED = 512
 COPIED = 512
-HELP = 128
+HELP = 192
 LENT = 128
 LATE = 128
 LAST = 128
@@ -58,7 +58,12 @@ def tile_moe_pre_lin_gelu_kernel(tc, xT, w_words, w_scales, b, gate, offs, pos1,
         banks = [psum.tile([P, BANK], F32, name="bank%d" % i) for i in range(8)]
         ident = keep.tile([P, P], F32, name="ident")
         make_identity(nc, ident[:])
-        gate_fused = keep.tile([P, FUSED], F32, name="gate_fused", tag="then_plane", align_bytes=64)
+        wide = S - FUSED - POOLED
+        fused_at = 3 * wide - C
+        early = keep.tile([P, fused_at + PACK * FUSED], F32, name="early", tag="then_plane", align_bytes=64)
+        second = early[:, 0:PACK * wide].rearrange("p (r n) -> p r n", r=PACK)
+        fused = early[:, fused_at:].rearrange("p (r n) -> p r n", r=PACK)
+        gate_fused = early[:, wide - HALF:wide - HALF + FUSED]
         gate_lead = keep.tile([P, C], F32, name="gate_lead")
         gate_end = keep.tile([P, C + LENT], F32, name="gate_end")
         gate_late = keep.tile([P, LATE], F32, name="gate_late")
@@ -76,15 +81,16 @@ def tile_moe_pre_lin_gelu_kernel(tc, xT, w_words, w_scales, b, gate, offs, pos1,
 
         load_x(0)
         nc.sync.dma_start(offs_sb[:], offs)
-        nc.sync.dma_start(gate_fused[:], gate[0:P, 0:FUSED])
+        nc.sync.dma_start(gate_fused, gate[0:P, 0:FUSED])
         load_x(1)
         load_x(2)
-        nc.sync.dma_start(gate_rows[:], gate.rearrange("k (m c) -> (k m) c", c=P)[0:P])
         load_x(3)
         load_x(4)
         nc.sync.dma_start(gate_lead[:], gate[0:P, FUSED:FUSED + C])
-        for i in range(5, PASSES * PACK):
-            load_x(i)
+        load_x(5)
+        nc.sync.dma_start(gate_rows[:], gate.rearrange("k (m c) -> (k m) c", c=P)[0:P])
+        load_x(6)
+        load_x(7)
         nc.sync.dma_start(gate_end[:], gate[0:P, FUSED + C:FUSED + 2 * C + LENT])
         w_to = w_codes[:].bitcast(I32).rearrange("p (g n) -> p g n", n=N)
         w_from = w_words.rearrange("e a p n r -> p (e a) (n r)").bitcast(I32)
@@ -168,30 +174,27 @@ def tile_moe_pre_lin_gelu_kernel(tc, xT, w_words, w_scales, b, gate, offs, pos1,
 
         second_from = FUSED + POOLED
         lent_to = second_from + LENT
-        wide = S - second_from
 
-        fused = keep.tile([P, PACK, FUSED], F32, name="fused")
         pooled = keep.tile([P, PACK, POOLED], F32, name="pooled")
         copied = keep.tile([P, PACK, COPIED], F32, name="copied", tag="sb")
 
-        nc.vector.tensor_copy(pooled[:, 0, 0:HELP], picked(0, 0, FUSED, HELP))
+        nc.vector.tensor_copy(second[:, 0, 0:HELP], picked(0, 0, second_from, HELP))
         for r in range(PACK):
-            nc.vector.tensor_tensor(fused[:, r, :], picked(0, r, 0, FUSED), gate_fused[:], MULT)
-        nc.scalar.activation(pooled[:, 0, HELP:POOLED], picked(0, 0, FUSED + HELP, POOLED - HELP), COPY)
-        for r in range(1, PACK):
-            nc.scalar.activation(pooled[:, r, :], picked(0, r, FUSED, POOLED), COPY)
+            nc.vector.tensor_tensor(fused[:, r, :], picked(0, r, 0, FUSED), gate_fused, MULT)
+        gather_plain(pooled, 0, FUSED, POOLED)
         for r in range(PACK):
             nc.vector.tensor_copy(copied[:, r, :], picked(1, r, 0, COPIED))
         laid0 = grouped("laid0", S)
-        nc.gpsimd.tensor_scalar(laid0[:, 0:FUSED, :], fused[:].rearrange("p r n -> p n r"), 1.0, 0.0, MULT, ADD)
+        nc.gpsimd.tensor_scalar(laid0[:, 0:FUSED, :], fused.rearrange("p r n -> p n r"), 1.0, 0.0, MULT, ADD)
 
         def pool_gate_and_lay(tile, staged, weight, n):
             nc.gpsimd.tensor_tensor(
                 tile, staged.rearrange("p r n -> p n r"),
                 weight.unsqueeze(2).to_broadcast([P, n, PACK]), MULT)
 
-        second = keep.tile([P, PACK, wide], F32, name="second", tag="then_plane", align_bytes=64)
-        gather_plain(second, 0, second_from, wide)
+        for r in range(PACK):
+            c0 = HELP if r == 0 else 0
+            nc.scalar.activation(second[:, r, c0:wide], picked(0, r, second_from + c0, wide - c0), COPY)
         pool_gate_and_lay(laid0[:, FUSED:FUSED + C, :], pooled[:, :, 0:C], gate_lead[:], C)
         pool_gate_and_lay(laid0[:, FUSED + C:second_from, :], pooled[:, :, C:2 * C], gate_end[:, 0:C], C)
         pool_gate_and_lay(laid0[:, second_from:lent_to, :], second[:, :, 0:LENT], gate_end[:, C:C + LENT], LENT)
@@ -206,14 +209,12 @@ def tile_moe_pre_lin_gelu_kernel(tc, xT, w_words, w_scales, b, gate, offs, pos1,
         gather_plain(fourth, 1, 768, 2 * C - LAST)
         gate_and_lay(laid1[:, 512:768, :], third[:], 512, 256)
         fifth = over.tile([P, PACK, LAST], F32, name="fifth", offset=0)
-        for r in range(1, PACK):
-            nc.scalar.activation(fifth[:, r, :], picked(1, r, S - LAST, LAST), COPY)
+        gather_plain(fifth, 1, S - LAST, LAST)
         plane = keep.tile([P, PASSES * S], U8, name="plane", tag="then_plane", align_bytes=64)
         quantize(laid0[:, 0:1024, :], 0, 0, 1024)
         quantize(laid0[:, 1024:S, :], 0, 1024, C)
         quantize(laid1[:, 0:512, :], 1, 0, 512)
         quantize(laid1[:, 512:768, :], 1, 512, 256)
-        nc.vector.tensor_copy(fifth[:, 0, :], picked(1, 0, S - LAST, LAST))
         own = 2 * C - LAST - LATE
         laid2 = laid1[:, 512 - own:1024 - own, :]
         gate_and_lay(laid2[:, 0:own, :], fourth[:, :, 0:own], 768, own)

@@ -30,8 +30,8 @@ BANK = 512
 FUSED = 320
 POOLED = 512
 COPIED = 512
-HELP = 192
-LENT = 128
+HELP = 256
+LENT = 112
 LATE = 128
 LAST = 128
 BLOCKS = S // P
@@ -183,7 +183,8 @@ def tile_moe_pre_lin_gelu_kernel(tc, xT, w_words, w_scales, b, gate, offs, pos1,
             nc.vector.tensor_tensor(fused[:, r, :], picked(0, r, 0, FUSED), gate_fused, MULT)
         gather_plain(pooled, 0, FUSED, POOLED)
         for r in range(PACK):
-            nc.vector.tensor_copy(copied[:, r, :], picked(1, r, 0, COPIED))
+            for c0, c1 in [(0, COPIED)] if r < PACK - 1 else [(0, HALF), (HALF, COPIED)]:
+                nc.vector.tensor_copy(copied[:, r, c0:c1], picked(1, r, c0, c1 - c0))
         laid0 = grouped("laid0", S)
         nc.gpsimd.tensor_scalar(laid0[:, 0:FUSED, :], fused.rearrange("p r n -> p n r"), 1.0, 0.0, MULT, ADD)
 

@@ -9,6 +9,9 @@ P = 128
 PACK = 4
 PASSES = K // (P * PACK)
 PER_COLUMN = 16
+HALF = C // 2
+BANK = 512
+BLOCKS = S // P
 
 F32 = mybir.dt.float32
 BF16 = mybir.dt.bfloat16
@@ -25,16 +28,14 @@ GELU = mybir.ActivationFunctionType.Gelu_apprx_tanh
 FLOPS = 2 * K * N * S
 BYTES = 4 * K * T + E * K * N + E * K * N // 32 + 4 * N * E + 4 * S + 2 * P * (S + 2 * T) // 16 + 4 * N * T
 
-HALF = C // 2
-BANK = 512
-FUSED = 320
+HEAD = 320
 POOLED = 512
-COPIED = 512
+REST = S - HEAD - POOLED
 HELP = 256
-LENT = 112
-LATE = 128
+LENT = 240
+COPIED = 544
+LATE = 144
 LAST = 128
-BLOCKS = S // P
 RUN = 2
 BOTH = 64
 
@@ -52,23 +53,24 @@ def tile_moe_pre_lin_gelu_kernel(tc, xT, w_words, w_scales, b, gate, offs, pos1,
         bias_sb = keep.tile([P, E], F32, name="bias_sb")
         w_codes = keep.tile([P, E * PASSES * N * PACK], U8, name="w_codes", align_bytes=64)
         w_plane = keep.tile([P, E * PASSES * N], U8, name="w_plane", align_bytes=64)
-        x_rows = [keep.tile([P, T], F32, name="x_rows%d" % i) for i in range(PASSES * PACK)]
+        slabs = [keep.tile([P, T], F32, name="slab%d" % i) for i in range(PASSES * PACK)]
         codes = keep.tile([P, PASSES * S], U32, name="codes", align_bytes=64)
         y = keep.tile([P, S], F32, name="y")
         banks = [psum.tile([P, BANK], F32, name="bank%d" % i) for i in range(8)]
         ident = keep.tile([P, P], F32, name="ident")
         make_identity(nc, ident[:])
-        wide = S - FUSED - POOLED
-        fused_at = 3 * wide - C
-        early = keep.tile([P, fused_at + PACK * FUSED], F32, name="early", tag="then_plane", align_bytes=64)
-        second = early[:, 0:PACK * wide].rearrange("p (r n) -> p r n", r=PACK)
-        fused = early[:, fused_at:].rearrange("p (r n) -> p r n", r=PACK)
-        gate_fused = early[:, wide - HALF:wide - HALF + FUSED]
-        gate_lead = keep.tile([P, C], F32, name="gate_lead")
-        gate_end = keep.tile([P, C + LENT], F32, name="gate_end")
+
+        rest_from = HEAD + POOLED
+        lent_to = rest_from + LENT
+        late_from = S - LAST - LATE
+        gated_at = 3 * REST - C
+        early = keep.tile([P, gated_at + PACK * HEAD], F32, name="early", tag="then_plane", align_bytes=64)
+        gate_head = early[:, REST - HALF:REST - HALF + HEAD]
+        gate_pooled = keep.tile([P, POOLED], F32, name="gate_pooled")
+        gate_lent = keep.tile([P, LENT], F32, name="gate_lent")
         gate_late = keep.tile([P, LATE], F32, name="gate_late")
         gate_rows = keep.tile([P, P], F32, name="gate_rows")
-        gate_col = keep.tile([P, BLOCKS], F32, name="gate_col")
+        gate_col = keep.tile([P, BLOCKS], F32, name="gate_col", tag="then_fourth")
 
         nc.vector.memset(w_plane[:].bitcast(I32), 0)
         warm = keep.tile([P, 1], F32, name="warm")
@@ -76,22 +78,22 @@ def tile_moe_pre_lin_gelu_kernel(tc, xT, w_words, w_scales, b, gate, offs, pos1,
 
         x_view = xT.rearrange("(a p r) t -> a r p t", p=P, r=PACK)
 
-        def load_x(i):
-            nc.sync.dma_start(x_rows[i][:, 0:T], x_view[i // PACK, i % PACK])
+        def load_slab(i):
+            nc.sync.dma_start(slabs[i][:], x_view[i // PACK, i % PACK])
 
-        load_x(0)
+        def load_gate(tile, s0, n):
+            nc.sync.dma_start(tile[:], gate[0:P, s0:s0 + n])
+
+        load_slab(0)
         nc.sync.dma_start(offs_sb[:], offs)
-        nc.sync.dma_start(gate_fused, gate[0:P, 0:FUSED])
-        load_x(1)
-        load_x(2)
-        load_x(3)
-        load_x(4)
-        nc.sync.dma_start(gate_lead[:], gate[0:P, FUSED:FUSED + C])
-        load_x(5)
+        nc.sync.dma_start(gate_head, gate[0:P, 0:HEAD])
+        for i in range(1, 6):
+            load_slab(i)
+        load_gate(gate_pooled, HEAD, POOLED)
         nc.sync.dma_start(gate_rows[:], gate.rearrange("k (m c) -> (k m) c", c=P)[0:P])
-        load_x(6)
-        load_x(7)
-        nc.sync.dma_start(gate_end[:], gate[0:P, FUSED + C:FUSED + 2 * C + LENT])
+        load_slab(6)
+        load_slab(7)
+        load_gate(gate_lent, rest_from, LENT)
         w_to = w_codes[:].bitcast(I32).rearrange("p (g n) -> p g n", n=N)
         w_from = w_words.rearrange("e a p n r -> p (e a) (n r)").bitcast(I32)
         for g0 in range(0, E * PASSES, PASSES):
@@ -101,7 +103,7 @@ def tile_moe_pre_lin_gelu_kernel(tc, xT, w_words, w_scales, b, gate, offs, pos1,
             nc.sync.dma_start(
                 w_plane[32 * q:32 * q + 4, :].bitcast(I32).rearrange("p (g n) -> p g n", g=E * PASSES),
                 scale_rows[4 * q:4 * q + 4])
-        nc.sync.dma_start(gate_late[:], gate[0:P, S - LAST - LATE:S - LAST])
+        load_gate(gate_late, late_from, LATE)
         nc.sync.dma_start(bias_sb[:], b)
         nc.sync.dma_start(pos1_sb[:], pos1)
         nc.sync.dma_start(pos2_sb[:], pos2)
@@ -110,19 +112,10 @@ def tile_moe_pre_lin_gelu_kernel(tc, xT, w_words, w_scales, b, gate, offs, pos1,
             return slice(s0 // PER_COLUMN, (s0 + n) // PER_COLUMN)
 
         def picked(a, r, s0, n):
-            return x_rows[a * PACK + r][:].indirect(offs_sb[:, columns(s0, n)])
+            return slabs[a * PACK + r][:].indirect(offs_sb[:, columns(s0, n)])
 
-        def by_runs(staged):
-            return staged.rearrange("p r (c i) -> p c r i", i=RUN)
-
-        def words(tile):
-            return tile.rearrange("p (c i) r -> p c r i", i=RUN)
-
-        def spread(weight, n):
-            return weight.rearrange("p (c i) -> p c i", i=RUN).unsqueeze(2).to_broadcast([P, n // RUN, PACK, RUN])
-
-        def gather_plain(staged, a, s0, n):
-            for r in range(PACK):
+        def scalar_gather(staged, a, s0, n, rows=range(PACK)):
+            for r in rows:
                 nc.scalar.activation(staged[:, r, :], picked(a, r, s0, n), COPY)
 
         nc.tensor.transpose(banks[0][:, 0:P], gate_rows[:], ident[:])
@@ -135,14 +128,26 @@ def tile_moe_pre_lin_gelu_kernel(tc, xT, w_words, w_scales, b, gate, offs, pos1,
                 m = (s0 + c) // P
                 nc.tensor.transpose(banks[bank][:, c:c + P], gate_col[:, m:m + 1].to_broadcast([P, P]), ident[:])
 
-        def gate_and_lay(tile, staged, s0, n):
+        def words(tile, run=RUN):
+            return tile.rearrange("p (c i) r -> p c r i", i=run)
+
+        def by_runs(staged, run=RUN):
+            return staged.rearrange("p r (c i) -> p c r i", i=run)
+
+        def spread(weight, n, run=RUN):
+            return weight.rearrange("p (c i) -> p c i", i=run).unsqueeze(2).to_broadcast([P, n // run, PACK, run])
+
+        def vector_lay(tile, staged, s0, n):
             bank = [j for j, (b0, width) in held.items() if b0 <= s0 and s0 + n <= b0 + width][0]
             c0 = s0 - held[bank][0]
             nc.vector.tensor_tensor(words(tile), by_runs(staged), spread(banks[bank][:, c0:c0 + n], n), MULT)
 
+        def pool_lay(tile, staged, weight, n):
+            nc.gpsimd.tensor_tensor(words(tile), by_runs(staged), spread(weight, n), MULT)
+
         spread_gate(7, 0, HALF)
-        spread_gate(5, HALF, COPIED - HALF)
-        spread_gate(6, COPIED, C)
+        spread_gate(5, HALF, BANK if COPIED > 2 * C else 3 * HALF)
+        spread_gate(6, 2 * C, C)
 
         groups = [(e * C, C) for e in range(3)] + [(s0, HALF) for s0 in range(3 * C, S, HALF)]
         accs = [banks[j][:, 0:n] for j, (s0, n) in enumerate(groups)]
@@ -169,60 +174,49 @@ def tile_moe_pre_lin_gelu_kernel(tc, xT, w_words, w_scales, b, gate, offs, pos1,
                             rhs=codes[:, w0:w0 + m].bitcast(FP8X4), rhs_scale=plane[:, w0:w0 + m],
                             start=(pa == 0), stop=(pa == PASSES - 1))
 
-        def grouped(name, n):
-            return keep.tile([P, n, PACK], BF16, name=name, align_bytes=64)
-
-        second_from = FUSED + POOLED
-        lent_to = second_from + LENT
-
+        rest = early[:, 0:PACK * REST].rearrange("p (r n) -> p r n", r=PACK)
+        gated = early[:, gated_at:].rearrange("p (r n) -> p r n", r=PACK)
         pooled = keep.tile([P, PACK, POOLED], F32, name="pooled")
-        copied = keep.tile([P, PACK, COPIED], F32, name="copied", tag="sb")
+        copied = keep.tile([P, PACK, COPIED], F32, name="copied")
+        laid0 = keep.tile([P, S, PACK], BF16, name="laid0", align_bytes=64)
+        laid1 = keep.tile([P, 2 * C + LATE + LAST, PACK], BF16, name="laid1", align_bytes=64)
 
-        nc.vector.tensor_copy(second[:, 0, 0:HELP], picked(0, 0, second_from, HELP))
+        nc.vector.tensor_copy(rest[:, 0, 0:HELP], picked(0, 0, rest_from, HELP))
         for r in range(PACK):
-            nc.vector.tensor_tensor(fused[:, r, :], picked(0, r, 0, FUSED), gate_fused, MULT)
-        gather_plain(pooled, 0, FUSED, POOLED)
+            nc.vector.tensor_tensor(gated[:, r, :], picked(0, r, 0, HEAD), gate_head, MULT)
+        scalar_gather(pooled, 0, HEAD, POOLED)
+        nc.gpsimd.tensor_scalar(words(laid0[:, 0:HEAD, :]), by_runs(gated), 1.0, 0.0, MULT, ADD)
+        nc.scalar.activation(rest[:, 0, HELP:REST], picked(0, 0, rest_from + HELP, REST - HELP), COPY)
         for r in range(PACK):
             for c0, c1 in [(0, COPIED)] if r < PACK - 1 else [(0, HALF), (HALF, COPIED)]:
                 nc.vector.tensor_copy(copied[:, r, c0:c1], picked(1, r, c0, c1 - c0))
-        laid0 = grouped("laid0", S)
-        nc.gpsimd.tensor_scalar(laid0[:, 0:FUSED, :], fused.rearrange("p r n -> p n r"), 1.0, 0.0, MULT, ADD)
+        scalar_gather(rest, 0, rest_from, REST, range(1, PACK))
+        pool_lay(laid0[:, HEAD:rest_from, :], pooled[:], gate_pooled[:], POOLED)
+        pool_lay(laid0[:, rest_from:lent_to, :], rest[:, :, 0:LENT], gate_lent[:], LENT)
 
-        def pool_gate_and_lay(tile, staged, weight, n):
-            nc.gpsimd.tensor_tensor(
-                tile, staged.rearrange("p r n -> p n r"),
-                weight.unsqueeze(2).to_broadcast([P, n, PACK]), MULT)
-
-        for r in range(PACK):
-            c0 = HELP if r == 0 else 0
-            nc.scalar.activation(second[:, r, c0:wide], picked(0, r, second_from + c0, wide - c0), COPY)
-        pool_gate_and_lay(laid0[:, FUSED:FUSED + C, :], pooled[:, :, 0:C], gate_lead[:], C)
-        pool_gate_and_lay(laid0[:, FUSED + C:second_from, :], pooled[:, :, C:2 * C], gate_end[:, 0:C], C)
-        pool_gate_and_lay(laid0[:, second_from:lent_to, :], second[:, :, 0:LENT], gate_end[:, C:C + LENT], LENT)
-        laid1 = grouped("laid1", 768)
-        gate_and_lay(laid1[:, 0:HALF, :], copied[:, :, 0:HALF], 0, HALF)
+        vector_lay(laid1[:, 0:HALF, :], copied[:, :, 0:HALF], 0, HALF)
         spread_gate(7, 3 * C, 2 * C)
-        third = over.tile([P, PACK, C], F32, name="third", offset=0)
-        gather_plain(third, 1, 512, 256)
-        gate_and_lay(laid1[:, HALF:COPIED, :], copied[:, :, HALF:COPIED], HALF, COPIED - HALF)
-        gate_and_lay(laid0[:, lent_to:S, :], second[:, :, LENT:wide], lent_to, S - lent_to)
-        fourth = keep.tile([P, PACK, 2 * C - LAST], F32, name="fourth", tag="sb")
-        gather_plain(fourth, 1, 768, 2 * C - LAST)
-        gate_and_lay(laid1[:, 512:768, :], third[:], 512, 256)
+        third = over.tile([P, PACK, 3 * C - COPIED], F32, name="third", offset=0)
+        scalar_gather(third, 1, COPIED, 3 * C - COPIED)
+        vector_lay(laid1[:, HALF:COPIED, :], copied[:, :, HALF:COPIED], HALF, COPIED - HALF)
+        vector_lay(laid0[:, lent_to:S, :], rest[:, :, LENT:REST], lent_to, S - lent_to)
+        fourth = keep.tile([P, PACK, 2 * C - LAST], F32, name="fourth", tag="then_fourth")
+        scalar_gather(fourth, 1, 3 * C, 2 * C - LAST)
+        vector_lay(laid1[:, COPIED:3 * C, :], third[:], COPIED, 3 * C - COPIED)
         fifth = over.tile([P, PACK, LAST], F32, name="fifth", offset=0)
-        gather_plain(fifth, 1, S - LAST, LAST)
+        scalar_gather(fifth, 1, S - LAST, LAST)
         plane = keep.tile([P, PASSES * S], U8, name="plane", tag="then_plane", align_bytes=64)
-        quantize(laid0[:, 0:1024, :], 0, 0, 1024)
-        quantize(laid0[:, 1024:S, :], 0, 1024, C)
-        quantize(laid1[:, 0:512, :], 1, 0, 512)
-        quantize(laid1[:, 512:768, :], 1, 512, 256)
-        own = 2 * C - LAST - LATE
-        laid2 = laid1[:, 512 - own:1024 - own, :]
-        gate_and_lay(laid2[:, 0:own, :], fourth[:, :, 0:own], 768, own)
-        pool_gate_and_lay(laid2[:, own:own + LATE, :], fourth[:, :, own:own + LATE], gate_late[:], LATE)
-        gate_and_lay(laid2[:, own + LATE:2 * C, :], fifth[:], S - LAST, LAST)
+        quantize(laid0[:, 0:4 * C, :], 0, 0, 4 * C)
+        quantize(laid0[:, 4 * C:S, :], 0, 4 * C, C)
+        quantize(laid1[:, 0:2 * C, :], 1, 0, 2 * C)
+        quantize(laid1[:, 2 * C:3 * C, :], 1, 2 * C, C)
+        own = late_from - 3 * C
+        laid2 = laid1[:, 2 * C - own:4 * C - own, :]
+        vector_lay(laid2[:, 0:own, :], fourth[:, :, 0:own], 3 * C, own)
+        pool_lay(laid2[:, own:own + LATE, :], fourth[:, :, own:own + LATE], gate_late[:], LATE)
+        vector_lay(laid2[:, own + LATE:2 * C, :], fifth[:], S - LAST, LAST)
         for c0 in range(0, 2 * C, HALF):
-            quantize(laid2[:, c0:c0 + HALF, :], 1, 768 + c0, HALF)
+            quantize(laid2[:, c0:c0 + HALF, :], 1, 3 * C + c0, HALF)
         for acc, (s0, m) in zip(accs, groups):
             e = s0 // C
             nc.scalar.activation(y[:, s0:s0 + m], acc, GELU, bias=bias_sb[:, e:e + 1])

@@ -44,7 +44,6 @@ def tile_moe_pre_lin_gelu_kernel(tc, xT, w_words, w_scales, b, gate, offs, pos1,
     nc = tc.nc
     with ExitStack() as ctx:
         keep = ctx.enter_context(tc.tile_pool(name="keep", bufs=1))
-        over = ctx.enter_context(tc.tile_pool(name="over", bufs=1))
         psum = ctx.enter_context(tc.psum_pool(name="psum", bufs=1))
 
         offs_sb = keep.tile([P, S // PER_COLUMN], U16, name="offs_sb")
@@ -63,11 +62,13 @@ def tile_moe_pre_lin_gelu_kernel(tc, xT, w_words, w_scales, b, gate, offs, pos1,
         rest_from = HEAD + POOLED
         lent_to = rest_from + LENT
         late_from = S - LAST - LATE
-        gated_at = 3 * REST - C
-        early = keep.tile([P, gated_at + PACK * HEAD], F32, name="early", tag="then_plane", align_bytes=64)
-        gate_head = early[:, REST - HALF:REST - HALF + HEAD]
+        third_from = COPIED
+        third_n = 3 * C - COPIED
+        gated_at = 3 * REST - 32
+        staging = keep.tile([P, PACK * (REST + third_n)], F32, name="staging")
+        gate_head = staging[:, REST - HALF:REST - HALF + HEAD]
         gate_pooled = keep.tile([P, POOLED], F32, name="gate_pooled")
-        gate_lent = keep.tile([P, LENT], F32, name="gate_lent")
+        gate_lent = keep.tile([P, LENT], F32, name="gate_lent", tag="then_plane", align_bytes=64)
         gate_late = keep.tile([P, LATE], F32, name="gate_late")
         gate_rows = keep.tile([P, P], F32, name="gate_rows")
         gate_col = keep.tile([P, BLOCKS], F32, name="gate_col", tag="then_fourth")
@@ -151,18 +152,17 @@ def tile_moe_pre_lin_gelu_kernel(tc, xT, w_words, w_scales, b, gate, offs, pos1,
 
         groups = [(e * C, C) for e in range(3)] + [(s0, HALF) for s0 in range(3 * C, S, HALF)]
         accs = [banks[j][:, 0:n] for j, (s0, n) in enumerate(groups)]
-        done = [set(), set()]
+        done = set()
         issued = set()
 
-        def quantize(tile, a, s0, n):
-            c0 = a * S + s0
+        def quantize(tile, c0, n):
             nc.vector.quantize_mx(out=codes[:, c0:c0 + n].bitcast(FP8X4), scales=plane[:, c0:c0 + n],
                                   in_=tile.rearrange("p n r -> p (n r)"))
-            for h in range(s0, s0 + n, HALF):
-                done[a].add(h)
+            for h in range(c0, c0 + n, HALF):
+                done.add(h)
             for acc, (g0, m) in zip(accs, groups):
                 for pa in range(PASSES):
-                    ready = all(h in done[q] for q in range(pa + 1) for h in range(g0, g0 + m, HALF))
+                    ready = all(q * S + h in done for q in range(pa + 1) for h in range(g0, g0 + m, HALF))
                     if ready and (pa, g0) not in issued:
                         issued.add((pa, g0))
                         j = (g0 // C) * PASSES + pa
@@ -174,12 +174,13 @@ def tile_moe_pre_lin_gelu_kernel(tc, xT, w_words, w_scales, b, gate, offs, pos1,
                             rhs=codes[:, w0:w0 + m].bitcast(FP8X4), rhs_scale=plane[:, w0:w0 + m],
                             start=(pa == 0), stop=(pa == PASSES - 1))
 
-        rest = early[:, 0:PACK * REST].rearrange("p (r n) -> p r n", r=PACK)
-        gated = early[:, gated_at:].rearrange("p (r n) -> p r n", r=PACK)
+        rest = staging[:, 0:PACK * REST].rearrange("p (r n) -> p r n", r=PACK)
+        gated = staging[:, gated_at:gated_at + PACK * HEAD].rearrange("p (r n) -> p r n", r=PACK)
         pooled = keep.tile([P, PACK, POOLED], F32, name="pooled")
         copied = keep.tile([P, PACK, COPIED], F32, name="copied")
-        laid0 = keep.tile([P, S, PACK], BF16, name="laid0", align_bytes=64)
-        laid1 = keep.tile([P, 2 * C + LATE + LAST, PACK], BF16, name="laid1", align_bytes=64)
+        laid = keep.tile([P, S + 2 * C + LATE + LAST, PACK], BF16, name="laid", align_bytes=64)
+        laid0 = laid[:, 0:S, :]
+        laid1 = laid[:, S:, :]
 
         nc.vector.tensor_copy(rest[:, 0, 0:HELP], picked(0, 0, rest_from, HELP))
         for r in range(PACK):
@@ -196,27 +197,25 @@ def tile_moe_pre_lin_gelu_kernel(tc, xT, w_words, w_scales, b, gate, offs, pos1,
 
         vector_lay(laid1[:, 0:HALF, :], copied[:, :, 0:HALF], 0, HALF)
         spread_gate(7, 3 * C, 2 * C)
-        third = over.tile([P, PACK, 3 * C - COPIED], F32, name="third", offset=0)
-        scalar_gather(third, 1, COPIED, 3 * C - COPIED)
+        third = staging[:, PACK * REST:].rearrange("p (r n) -> p r n", r=PACK)
+        scalar_gather(third, 1, third_from, third_n)
         vector_lay(laid1[:, HALF:COPIED, :], copied[:, :, HALF:COPIED], HALF, COPIED - HALF)
         vector_lay(laid0[:, lent_to:S, :], rest[:, :, LENT:REST], lent_to, S - lent_to)
         fourth = keep.tile([P, PACK, 2 * C - LAST], F32, name="fourth", tag="then_fourth")
         scalar_gather(fourth, 1, 3 * C, 2 * C - LAST)
-        vector_lay(laid1[:, COPIED:3 * C, :], third[:], COPIED, 3 * C - COPIED)
-        fifth = over.tile([P, PACK, LAST], F32, name="fifth", offset=0)
+        vector_lay(laid1[:, COPIED:3 * C, :], third, third_from, third_n)
+        fifth = staging[:, PACK * REST:PACK * (REST + LAST)].rearrange("p (r n) -> p r n", r=PACK)
         scalar_gather(fifth, 1, S - LAST, LAST)
         plane = keep.tile([P, PASSES * S], U8, name="plane", tag="then_plane", align_bytes=64)
-        quantize(laid0[:, 0:4 * C, :], 0, 0, 4 * C)
-        quantize(laid0[:, 4 * C:S, :], 0, 4 * C, C)
-        quantize(laid1[:, 0:2 * C, :], 1, 0, 2 * C)
-        quantize(laid1[:, 2 * C:3 * C, :], 1, 2 * C, C)
+        for c0, n in [(0, 4 * C), (4 * C, C), (5 * C, 2 * C), (7 * C, C)]:
+            quantize(laid[:, c0:c0 + n, :], c0, n)
         own = late_from - 3 * C
         laid2 = laid1[:, 2 * C - own:4 * C - own, :]
         vector_lay(laid2[:, 0:own, :], fourth[:, :, 0:own], 3 * C, own)
         pool_lay(laid2[:, own:own + LATE, :], fourth[:, :, own:own + LATE], gate_late[:], LATE)
-        vector_lay(laid2[:, own + LATE:2 * C, :], fifth[:], S - LAST, LAST)
+        vector_lay(laid2[:, own + LATE:2 * C, :], fifth, S - LAST, LAST)
         for c0 in range(0, 2 * C, HALF):
-            quantize(laid2[:, c0:c0 + HALF, :], 1, 3 * C + c0, HALF)
+            quantize(laid2[:, c0:c0 + HALF, :], S + 3 * C + c0, HALF)
         for acc, (s0, m) in zip(accs, groups):
             e = s0 // C
             nc.scalar.activation(y[:, s0:s0 + m], acc, GELU, bias=bias_sb[:, e:e + 1])

@@ -37,6 +37,7 @@ COPIED = 544
 LATE = 144
 LAST = 128
 RUN = 2
+POOL_RUN = 4
 BOTH = 64
 
 
@@ -144,7 +145,7 @@ def tile_moe_pre_lin_gelu_kernel(tc, xT, w_words, w_scales, b, gate, offs, pos1,
             nc.vector.tensor_tensor(words(tile), by_runs(staged), spread(banks[bank][:, c0:c0 + n], n), MULT)
 
         def pool_lay(tile, staged, weight, n):
-            nc.gpsimd.tensor_tensor(words(tile), by_runs(staged), spread(weight, n), MULT)
+            nc.gpsimd.tensor_tensor(words(tile, POOL_RUN), by_runs(staged, POOL_RUN), spread(weight, n, POOL_RUN), MULT)
 
         spread_gate(7, 0, HALF)
         spread_gate(5, HALF, BANK if COPIED > 2 * C else 3 * HALF)
@@ -186,7 +187,7 @@ def tile_moe_pre_lin_gelu_kernel(tc, xT, w_words, w_scales, b, gate, offs, pos1,
         for r in range(PACK):
             nc.vector.tensor_tensor(gated[:, r, :], picked(0, r, 0, HEAD), gate_head, MULT)
         scalar_gather(pooled, 0, HEAD, POOLED)
-        nc.gpsimd.tensor_scalar(words(laid0[:, 0:HEAD, :]), by_runs(gated), 1.0, 0.0, MULT, ADD)
+        nc.gpsimd.tensor_scalar(words(laid0[:, 0:HEAD, :], POOL_RUN), by_runs(gated, POOL_RUN), 1.0, 0.0, MULT, ADD)
         nc.scalar.activation(rest[:, 0, HELP:REST], picked(0, 0, rest_from + HELP, REST - HELP), COPY)
         for r in range(PACK):
             for c0, c1 in [(0, COPIED)] if r < PACK - 1 else [(0, HALF), (HALF, COPIED)]:
@@ -207,7 +208,7 @@ def tile_moe_pre_lin_gelu_kernel(tc, xT, w_words, w_scales, b, gate, offs, pos1,
         fifth = staging[:, PACK * REST:PACK * (REST + LAST)].rearrange("p (r n) -> p r n", r=PACK)
         scalar_gather(fifth, 1, S - LAST, LAST)
         plane = keep.tile([P, PASSES * S], U8, name="plane", tag="then_plane", align_bytes=64)
-        for c0, n in [(0, 4 * C), (4 * C, C), (5 * C, 2 * C), (7 * C, C)]:
+        for c0, n in [(0, 4 * C), (4 * C, 4 * C)]:
             quantize(laid[:, c0:c0 + n, :], c0, n)
         own = late_from - 3 * C
         laid2 = laid1[:, 2 * C - own:4 * C - own, :]

@@ -32,8 +32,8 @@ HEAD = 320
 POOLED = 512
 REST = S - HEAD - POOLED
 HELP = 256
-LENT = 240
-COPIED = 544
+LENT = 232
+COPIED = 512
 LATE = 144
 LAST = 128
 RUN = 2
@@ -65,7 +65,7 @@ def tile_moe_pre_lin_gelu_kernel(tc, xT, w_words, w_scales, b, gate, offs, pos1,
         late_from = S - LAST - LATE
         third_from = COPIED
         third_n = 3 * C - COPIED
-        gated_at = 3 * REST - 32
+        gated_at = PACK * (REST + third_n - HEAD) - 224
         staging = keep.tile([P, PACK * (REST + third_n)], F32, name="staging")
         gate_head = staging[:, REST - HALF:REST - HALF + HEAD]
         gate_pooled = keep.tile([P, POOLED], F32, name="gate_pooled")

@@ -32,7 +32,7 @@ HEAD = 320
 POOLED = 512
 REST = S - HEAD - POOLED
 HELP = 256
-LENT = 232
+LENT = 208
 COPIED = 512
 LATE = 144
 LAST = 128

@@ -32,13 +32,16 @@ HEAD = 320
 POOLED = 512
 REST = S - HEAD - POOLED
 HELP = 256
-LENT = 208
+LENT = 256
 COPIED = 512
 LATE = 144
 LAST = 128
 RUN = 2
-POOL_RUN = 4
-BOTH = 64
+POOL_RUN = 8
+BOTH = 96
+OWN = 160
+LEAD = 64
+FRONT = 448
 
 
 def tile_moe_pre_lin_gelu_kernel(tc, xT, w_words, w_scales, b, gate, offs, pos1, pos2, out):
@@ -228,15 +231,16 @@ def tile_moe_pre_lin_gelu_kernel(tc, xT, w_words, w_scales, b, gate, offs, pos1,
         def results(pos_sb, t0, t1):
             return y[:].indirect(pos_sb[:, columns(t0, t1 - t0)])
 
-        nc.vector.tensor_copy(first[:, 96:224], results(pos1_sb, 96, 224))
-        for t0, t1 in [(0, 96), (224, 352), (352, both_from), (both_from, T)]:
+        led = OWN + LEAD
+        nc.vector.tensor_copy(first[:, 0:OWN], results(pos1_sb, 0, OWN))
+        for t0, t1 in [(OWN, led), (led, FRONT), (FRONT, T)]:
             nc.scalar.activation(first[:, t0:t1], results(pos1_sb, t0, t1), COPY)
         nc.scalar.activation(other[:], results(pos2_sb, both_from, T), COPY)
-        front = keep.tile([P, 352], F32, name="front")
-        back = keep.tile([P, T - 352], F32, name="back")
-        for t0, t1 in [(0, 96), (96, 352)]:
+        front = keep.tile([P, FRONT], F32, name="front")
+        back = keep.tile([P, T - FRONT], F32, name="back")
+        for t0, t1 in [(OWN, led), (0, OWN), (led, FRONT)]:
             nc.vector.tensor_tensor(front[:, t0:t1], results(pos2_sb, t0, t1), first[:, t0:t1], ADD)
-        nc.sync.dma_start(out[:, 0:352], front[:])
-        nc.vector.tensor_tensor(back[:, 0:both_from - 352], results(pos2_sb, 352, both_from), first[:, 352:both_from], ADD)
-        nc.vector.tensor_tensor(back[:, both_from - 352:], other[:], first[:, both_from:T], ADD)
-        nc.sync.dma_start(out[:, 352:T], back[:])
+        nc.sync.dma_start(out[:, 0:FRONT], front[:])
+        nc.vector.tensor_tensor(back[:, 0:both_from - FRONT], results(pos2_sb, FRONT, both_from), first[:, FRONT:both_from], ADD)
+        nc.vector.tensor_tensor(back[:, both_from - FRONT:], other[:], first[:, both_from:T], ADD)
+        nc.sync.dma_start(out[:, FRONT:T], back[:])

@@ -32,7 +32,7 @@ HEAD = 320
 POOLED = 512
 REST = S - HEAD - POOLED
 HELP = 256
-LENT = 256
+LENT = 232
 COPIED = 512
 LATE = 144
 LAST = 128

from contextlib import ExitStack

import concourse.mybir as mybir
from concourse.masks import make_identity

K, T, E, C, N = 1024, 640, 5, 256, 128
S = E * C
P = 128
PACK = 4
PASSES = K // (P * PACK)
PER_COLUMN = 16
HALF = C // 2
BANK = 512
BLOCKS = S // P

F32 = mybir.dt.float32
BF16 = mybir.dt.bfloat16
I32 = mybir.dt.int32
U32 = mybir.dt.uint32
U16 = mybir.dt.uint16
U8 = mybir.dt.uint8
FP8X4 = mybir.dt.float8_e4m3fn_x4
MULT = mybir.AluOpType.mult
ADD = mybir.AluOpType.add
COPY = mybir.ActivationFunctionType.Copy
GELU = mybir.ActivationFunctionType.Gelu_apprx_tanh

FLOPS = 2 * K * N * S
BYTES = 4 * K * T + E * K * N + E * K * N // 32 + 4 * N * E + 4 * S + 2 * P * (S + 2 * T) // 16 + 4 * N * T

HEAD = 320
POOLED = 512
REST = S - HEAD - POOLED
HELP = 256
LENT = 232
COPIED = 512
LATE = 144
LAST = 128
RUN = 2
POOL_RUN = 8
BOTH = 96
OWN = 160
LEAD = 64
FRONT = 448


def tile_moe_pre_lin_gelu_kernel(tc, xT, w_words, w_scales, b, gate, offs, pos1, pos2, out):
    nc = tc.nc
    with ExitStack() as ctx:
        keep = ctx.enter_context(tc.tile_pool(name="keep", bufs=1))
        psum = ctx.enter_context(tc.psum_pool(name="psum", bufs=1))

        offs_sb = keep.tile([P, S // PER_COLUMN], U16, name="offs_sb")
        pos1_sb = keep.tile([P, T // PER_COLUMN], U16, name="pos1_sb")
        pos2_sb = keep.tile([P, T // PER_COLUMN], U16, name="pos2_sb")
        bias_sb = keep.tile([P, E], F32, name="bias_sb")
        w_codes = keep.tile([P, E * PASSES * N * PACK], U8, name="w_codes", align_bytes=64)
        w_plane = keep.tile([P, E * PASSES * N], U8, name="w_plane", align_bytes=64)
        slabs = [keep.tile([P, T], F32, name="slab%d" % i) for i in range(PASSES * PACK)]
        codes = keep.tile([P, PASSES * S], U32, name="codes", align_bytes=64)
        y = keep.tile([P, S], F32, name="y")
        banks = [psum.tile([P, BANK], F32, name="bank%d" % i) for i in range(8)]
        ident = keep.tile([P, P], F32, name="ident")
        make_identity(nc, ident[:])

        rest_from = HEAD + POOLED
        lent_to = rest_from + LENT
        late_from = S - LAST - LATE
        third_from = COPIED
        third_n = 3 * C - COPIED
        gated_at = PACK * (REST + third_n - HEAD) - 224
        staging = keep.tile([P, PACK * (REST + third_n)], F32, name="staging")
        gate_head = staging[:, REST - HALF:REST - HALF + HEAD]
        gate_pooled = keep.tile([P, POOLED], F32, name="gate_pooled")
        gate_lent = keep.tile([P, LENT], F32, name="gate_lent", tag="then_plane", align_bytes=64)
        gate_late = keep.tile([P, LATE], F32, name="gate_late")
        gate_rows = keep.tile([P, P], F32, name="gate_rows")
        gate_col = keep.tile([P, BLOCKS], F32, name="gate_col", tag="then_fourth")

        nc.vector.memset(w_plane[:].bitcast(I32), 0)
        warm = keep.tile([P, 1], F32, name="warm")
        nc.scalar.activation(warm[:], w_plane[:, 0:4].bitcast(U32), GELU)

        x_view = xT.rearrange("(a p r) t -> a r p t", p=P, r=PACK)

        def load_slab(i):
            nc.sync.dma_start(slabs[i][:], x_view[i // PACK, i % PACK])

        def load_gate(tile, s0, n):
            nc.sync.dma_start(tile[:], gate[0:P, s0:s0 + n])

        load_slab(0)
        nc.sync.dma_start(offs_sb[:], offs)
        nc.sync.dma_start(gate_head, gate[0:P, 0:HEAD])
        for i in range(1, 6):
            load_slab(i)
        load_gate(gate_pooled, HEAD, POOLED)
        nc.sync.dma_start(gate_rows[:], gate.rearrange("k (m c) -> (k m) c", c=P)[0:P])
        load_slab(6)
        load_slab(7)
        load_gate(gate_lent, rest_from, LENT)
        w_to = w_codes[:].bitcast(I32).rearrange("p (g n) -> p g n", n=N)
        w_from = w_words.rearrange("e a p n r -> p (e a) (n r)").bitcast(I32)
        for g0 in range(0, E * PASSES, PASSES):
            nc.sync.dma_start(w_to[:, g0:g0 + PASSES, :], w_from[:, g0:g0 + PASSES, :])
        scale_rows = w_scales.rearrange("e a q n -> q (e a) n").bitcast(I32)
        for q in range(4):
            nc.sync.dma_start(
                w_plane[32 * q:32 * q + 4, :].bitcast(I32).rearrange("p (g n) -> p g n", g=E * PASSES),
                scale_rows[4 * q:4 * q + 4])
        load_gate(gate_late, late_from, LATE)
        nc.sync.dma_start(bias_sb[:], b)
        nc.sync.dma_start(pos1_sb[:], pos1)
        nc.sync.dma_start(pos2_sb[:], pos2)

        def columns(s0, n):
            return slice(s0 // PER_COLUMN, (s0 + n) // PER_COLUMN)

        def picked(a, r, s0, n):
            return slabs[a * PACK + r][:].indirect(offs_sb[:, columns(s0, n)])

        def scalar_gather(staged, a, s0, n, rows=range(PACK)):
            for r in rows:
                nc.scalar.activation(staged[:, r, :], picked(a, r, s0, n), COPY)

        nc.tensor.transpose(banks[0][:, 0:P], gate_rows[:], ident[:])
        nc.vector.tensor_copy(gate_col[:], banks[0][:, 0:BLOCKS])
        held = {}

        def spread_gate(bank, s0, n):
            held[bank] = (s0, n)
            for c in range(0, n, P):
                m = (s0 + c) // P
                nc.tensor.transpose(banks[bank][:, c:c + P], gate_col[:, m:m + 1].to_broadcast([P, P]), ident[:])

        def words(tile, run=RUN):
            return tile.rearrange("p (c i) r -> p c r i", i=run)

        def by_runs(staged, run=RUN):
            return staged.rearrange("p r (c i) -> p c r i", i=run)

        def spread(weight, n, run=RUN):
            return weight.rearrange("p (c i) -> p c i", i=run).unsqueeze(2).to_broadcast([P, n // run, PACK, run])

        def vector_lay(tile, staged, s0, n):
            bank = [j for j, (b0, width) in held.items() if b0 <= s0 and s0 + n <= b0 + width][0]
            c0 = s0 - held[bank][0]
            nc.vector.tensor_tensor(words(tile), by_runs(staged), spread(banks[bank][:, c0:c0 + n], n), MULT)

        def pool_lay(tile, staged, weight, n):
            nc.gpsimd.tensor_tensor(words(tile, POOL_RUN), by_runs(staged, POOL_RUN), spread(weight, n, POOL_RUN), MULT)

        spread_gate(7, 0, HALF)
        spread_gate(5, HALF, BANK if COPIED > 2 * C else 3 * HALF)
        spread_gate(6, 2 * C, C)

        groups = [(e * C, C) for e in range(3)] + [(s0, HALF) for s0 in range(3 * C, S, HALF)]
        accs = [banks[j][:, 0:n] for j, (s0, n) in enumerate(groups)]
        done = set()
        issued = set()

        def quantize(tile, c0, n):
            nc.vector.quantize_mx(out=codes[:, c0:c0 + n].bitcast(FP8X4), scales=plane[:, c0:c0 + n],
                                  in_=tile.rearrange("p n r -> p (n r)"))
            for h in range(c0, c0 + n, HALF):
                done.add(h)
            for acc, (g0, m) in zip(accs, groups):
                for pa in range(PASSES):
                    ready = all(q * S + h in done for q in range(pa + 1) for h in range(g0, g0 + m, HALF))
                    if ready and (pa, g0) not in issued:
                        issued.add((pa, g0))
                        j = (g0 // C) * PASSES + pa
                        w0 = pa * S + g0
                        nc.tensor.matmul_mx(
                            out=acc,
                            lhsT=w_codes[:, j * N * PACK:(j + 1) * N * PACK].bitcast(FP8X4),
                            lhsT_scale=w_plane[:, j * N:(j + 1) * N],
                            rhs=codes[:, w0:w0 + m].bitcast(FP8X4), rhs_scale=plane[:, w0:w0 + m],
                            start=(pa == 0), stop=(pa == PASSES - 1))

        rest = staging[:, 0:PACK * REST].rearrange("p (r n) -> p r n", r=PACK)
        gated = staging[:, gated_at:gated_at + PACK * HEAD].rearrange("p (r n) -> p r n", r=PACK)
        pooled = keep.tile([P, PACK, POOLED], F32, name="pooled")
        copied = keep.tile([P, PACK, COPIED], F32, name="copied")
        laid = keep.tile([P, S + 2 * C + LATE + LAST, PACK], BF16, name="laid", align_bytes=64)
        laid0 = laid[:, 0:S, :]
        laid1 = laid[:, S:, :]

        nc.vector.tensor_copy(rest[:, 0, 0:HELP], picked(0, 0, rest_from, HELP))
        for r in range(PACK):
            nc.vector.tensor_tensor(gated[:, r, :], picked(0, r, 0, HEAD), gate_head, MULT)
        scalar_gather(pooled, 0, HEAD, POOLED)
        nc.gpsimd.tensor_scalar(words(laid0[:, 0:HEAD, :], POOL_RUN), by_runs(gated, POOL_RUN), 1.0, 0.0, MULT, ADD)
        nc.scalar.activation(rest[:, 0, HELP:REST], picked(0, 0, rest_from + HELP, REST - HELP), COPY)
        for r in range(PACK):
            for c0, c1 in [(0, COPIED)] if r < PACK - 1 else [(0, HALF), (HALF, COPIED)]:
                nc.vector.tensor_copy(copied[:, r, c0:c1], picked(1, r, c0, c1 - c0))
        scalar_gather(rest, 0, rest_from, REST, range(1, PACK))
        pool_lay(laid0[:, HEAD:rest_from, :], pooled[:], gate_pooled[:], POOLED)
        pool_lay(laid0[:, rest_from:lent_to, :], rest[:, :, 0:LENT], gate_lent[:], LENT)

        vector_lay(laid1[:, 0:HALF, :], copied[:, :, 0:HALF], 0, HALF)
        spread_gate(7, 3 * C, 2 * C)
        third = staging[:, PACK * REST:].rearrange("p (r n) -> p r n", r=PACK)
        scalar_gather(third, 1, third_from, third_n)
        vector_lay(laid1[:, HALF:COPIED, :], copied[:, :, HALF:COPIED], HALF, COPIED - HALF)
        vector_lay(laid0[:, lent_to:S, :], rest[:, :, LENT:REST], lent_to, S - lent_to)
        fourth = keep.tile([P, PACK, 2 * C - LAST], F32, name="fourth", tag="then_fourth")
        scalar_gather(fourth, 1, 3 * C, 2 * C - LAST)
        vector_lay(laid1[:, COPIED:3 * C, :], third, third_from, third_n)
        fifth = staging[:, PACK * REST:PACK * (REST + LAST)].rearrange("p (r n) -> p r n", r=PACK)
        scalar_gather(fifth, 1, S - LAST, LAST)
        plane = keep.tile([P, PASSES * S], U8, name="plane", tag="then_plane", align_bytes=64)
        for c0, n in [(0, 4 * C), (4 * C, 4 * C)]:
            quantize(laid[:, c0:c0 + n, :], c0, n)
        own = late_from - 3 * C
        laid2 = laid1[:, 2 * C - own:4 * C - own, :]
        vector_lay(laid2[:, 0:own, :], fourth[:, :, 0:own], 3 * C, own)
        pool_lay(laid2[:, own:own + LATE, :], fourth[:, :, own:own + LATE], gate_late[:], LATE)
        vector_lay(laid2[:, own + LATE:2 * C, :], fifth, S - LAST, LAST)
        for c0 in range(0, 2 * C, HALF):
            quantize(laid2[:, c0:c0 + HALF, :], S + 3 * C + c0, HALF)
        for acc, (s0, m) in zip(accs, groups):
            e = s0 // C
            nc.scalar.activation(y[:, s0:s0 + m], acc, GELU, bias=bias_sb[:, e:e + 1])

        first = keep.tile([P, T], F32, name="first")
        both_from = T - BOTH
        other = keep.tile([P, BOTH], F32, name="other")

        def results(pos_sb, t0, t1):
            return y[:].indirect(pos_sb[:, columns(t0, t1 - t0)])

        led = OWN + LEAD
        nc.vector.tensor_copy(first[:, 0:OWN], results(pos1_sb, 0, OWN))
        for t0, t1 in [(OWN, led), (led, FRONT), (FRONT, T)]:
            nc.scalar.activation(first[:, t0:t1], results(pos1_sb, t0, t1), COPY)
        nc.scalar.activation(other[:], results(pos2_sb, both_from, T), COPY)
        front = keep.tile([P, FRONT], F32, name="front")
        back = keep.tile([P, T - FRONT], F32, name="back")
        for t0, t1 in [(OWN, led), (0, OWN), (led, FRONT)]:
            nc.vector.tensor_tensor(front[:, t0:t1], results(pos2_sb, t0, t1), first[:, t0:t1], ADD)
        nc.sync.dma_start(out[:, 0:FRONT], front[:])
        nc.vector.tensor_tensor(back[:, 0:both_from - FRONT], results(pos2_sb, FRONT, both_from), first[:, FRONT:both_from], ADD)
        nc.vector.tensor_tensor(back[:, both_from - FRONT:], other[:], first[:, both_from:T], ADD)
        nc.sync.dma_start(out[:, FRONT:T], back[:])
